import numpy as np, ml_dtypes
CORES = [23,119,17,113]
N = 4
BF = ml_dtypes.bfloat16
V, C, S, IT, Q, RO, D = 2048, 256, 256, 4, 9, 2, 2048
P = V + 2 * C * RO
def mesh(rng, m, isb, chain):
    o = rng.permutation(V); x = np.zeros(3 * V, np.int64); sn = np.zeros(2 * S, np.int64); rest = V - 2 * m
    x[2 * V + o[0:2 * m:2]] = o[1:2 * m:2]; x[2 * V + o[1:2 * m:2]] = o[0:2 * m:2]
    up = 2 * V + o[2 * m:]; leg = rng.integers(0, 2, rest) * V + o[:rest] if chain else rng.permutation(2 * V)[:rest]
    left = np.ones(2 * V, bool); left[leg] = False
    jb, jl = np.flatnonzero(isb), np.flatnonzero(~isb); c = rng.permutation(rest); cut, keep = c[:len(jb)], c[len(jb):]
    x[up[keep]] = leg[keep] % V; x[leg[keep]] = up[keep] - 2 * V
    x[up[cut]] = P + jb; sn[jb] = up[cut] - 2 * V
    pool = np.concatenate([rng.permutation(leg[cut]), rng.permutation(np.flatnonzero(left))]); h = rng.permutation(pool[:len(jl)])
    x[h] = P + jl; sn[jl] = h % V
    k = rng.permutation(pool[len(jl):]).reshape(2, -1); x[k[0]] = k[1] % V; x[k[1]] = k[0] % V
    return x.reshape(3, V), sn, o
def meshes(rng, m, chain=False):
    x = rng.choice(4, (N, 8, S), p=[0.35, 0.35, 0.2, 0.1])
    isb = np.concatenate([np.roll((x == 1) | (x == 3), 1, axis=0), (x == 0) | (x == 3)], axis=2)
    z = [[mesh(rng, int(m[a, g]), isb[a, g], chain) for g in range(8)] for a in range(N)]
    return tuple(np.stack([np.stack([u[i] for u in row]) for row in z]) for i in range(3))
def levels(rng):
    return rng.permuted(np.tile(np.array([60, 90, 110, 130, 150, 165, 180, 200]), (N, 1)), axis=1)[:, :, None, None] + rng.integers(-20, 21, (N, 8, 16, 1))
def errors(rng):
    return (256 * (0.25 + 0.75 * rng.random((N, 8, 1, V))) * rng.random((N, 8, 16, V))).astype(np.int64)
def under(rng, th):
    return np.minimum((th * rng.random((N, 8, 16, V))).astype(np.int64), th - 1)
def plant(rng, e, t, x, y, cnt):
    on = np.argsort(rng.random((16, len(x))), axis=0) < cnt[None, :]; one = rng.random(on.shape) < 0.5
    v = np.where(rng.random(on.shape) < 0.5, t, np.minimum(t + (rng.random(on.shape) * (256 - t)).astype(np.int64), 255))
    e[:, x] = np.where(on & one, v, e[:, x]); e[:, y] = np.where(on & ~one, v, e[:, y])
def more(rng):
    return rng.integers(0, 256, (N, 8, 16, D)), rng.integers(0, 256, (N, 8, 16, 1))
def pack(err, p, sn, det, wt, th):
    b = lambda a: np.ascontiguousarray(a.reshape(N, 128, -1)).astype(np.float32).astype(BF)
    i = lambda a: np.ascontiguousarray(a).astype(np.int32)
    return {"err": b(err), "lt": i(p[:, :, 0]), "rt": i(p[:, :, 1]), "bs": i(p[:, :, 2]), "snd": i(sn), "det": b(det), "wt": i(wt.reshape(N, 128, 1)), "th": i(th.reshape(N, 128, 1))}
def setup_inputs(rng):
    p, sn, o = meshes(rng, rng.integers(V // 8, V // 3 + 1, (N, 8))); det, wt = more(rng)
    return pack(errors(rng), p, sn, det, wt, levels(rng))
def setup_inputs_room(rng):
    M = V // 3; p, sn, o = meshes(rng, np.full((N, 8), M)); det, wt = more(rng)
    th = np.repeat(rng.integers(64, 192, (1, 8, 16, 1)), N, axis=0); err = under(rng, th)
    for a in range(N):
        for g in range(8):
            n = (C, C + 1, 0, 1, C - 1, M, C, C + 1)[(a + g) % 8]
            plant(rng, err[a, g], th[a, g], o[a, g, 0:2 * M:2], o[a, g, 1:2 * M:2], np.where(rng.permutation(M) < n, Q, Q - 1))
    return pack(err, p, sn, det, wt, th)
def setup_inputs_chain(rng):
    M = V // (2 * (IT + 3)); p, sn, o = meshes(rng, np.full((N, 8), M), True); det, wt = more(rng)
    th = np.repeat(rng.integers(64, 192, (1, 8, 16, 1)), N, axis=0); err = under(rng, th); far = np.array([0, 1, IT - 1, IT, IT, IT + 1, IT + 1])
    for a in range(N):
        for g in range(8):
            i = 2 * np.arange(M) + 2 * M * rng.permuted(np.resize(far, M))
            plant(rng, err[a, g], th[a, g], o[a, g, i], o[a, g, i + 1], np.where(rng.random(M) < 0.8, Q, Q - 1))
    return pack(err, p, sn, det, wt, th)
def setup_inputs_ties(rng):
    p, sn, o = meshes(rng, rng.integers(V // 8, V // 3 + 1, (N, 8))); det, wt = more(rng)
    th = np.clip(np.array([1, 2, 100, 128, 254, 255, 255, 30])[None, :, None, None] + rng.integers(-1, 2, (N, 8, 16, 1)), 1, 255); th[:, 6] = 255
    err = np.clip(th - 1 + (rng.random((N, 8, 16, V)) < 0.5 * rng.random((N, 8, 1, V))) * rng.integers(1, 3, (N, 8, 16, V)), 0, 255)
    err[:, 6] = np.minimum(err[:, 6], 254); err[:, 7] = 255
    det[:, 1] = 255; det[:, 2] = 0; wt[:, 0] = 0; wt[:, 1] = 255
    return pack(err, p, sn, det, wt, th)
def pools(rng):
    return [[int(z) for z in rng.permutation(V)] for a in range(N)], rng.permutation(S)[:8 * N].reshape(N, 2, 4)
def watch(x, leg, u, v, slot):
    x[leg, u] = P + slot; x[1 - leg, u] = v; x[2, u] = v; x[:, v] = u
def renamed(rng, x, sn, e):
    pool, kk = pools(rng)
    for a in range(N):
        for s in range(2):
            k, k2, kb, kb2 = [int(z) for z in kk[a, s]]; q, z = (a + 2 * s - 1) % N, (a - 2 * s + 1) % N
            t, b = pool[a].pop(), pool[a].pop()
            x[a, 2, t] = b; x[a, 2, b] = t; x[a, 0, t] = P + (1 - s) * S + k2; x[a, 1, t] = P + s * S + k; e[a, :, t] = 255
            sn[a, s * S + k] = t; sn[a, (1 - s) * S + k] = t
            u, v = pool[q].pop(), pool[q].pop(); sn[q, (1 - s) * S + k] = u; watch(x[q], s, u, v, (1 - s) * S + k)
            u, v = pool[z].pop(), pool[z].pop(); sn[z, s * S + k2] = u; watch(x[z], 1 - s, u, v, s * S + k)
            t, b = pool[a].pop(), pool[a].pop()
            x[a, 2, t] = b; x[a, 2, b] = t; x[a, 0, t] = P + s * S + kb2; e[a, :, t] = 255
            x[a, 1, t] = (P + s * S + kb) % (2 * S) + 2 * S * int(rng.integers(0, V // (2 * S))); sn[a, s * S + kb] = t
            u, v = pool[q].pop(), pool[q].pop(); sn[q, (1 - s) * S + kb2] = u; watch(x[q], s, u, v, (1 - s) * S + kb)
def allpairs(rng, x, e):
    for a in range(N):
        pr = np.sort(rng.permutation(V).reshape(-1, 2), axis=1); pr = pr[np.argsort(pr[:, 0])]
        x[a, 0, pr[0::2]] = pr[1::2]; x[a, 0, pr[1::2]] = pr[0::2]
        for i in (1, 2):
            x[a, i, pr[:, 0]] = pr[:, 1]; x[a, i, pr[:, 1]] = pr[:, 0]
        e[a][:, pr[len(pr) - C // 2:].reshape(-1)] = 255
def crowded(rng, x, sn, e):
    pool, kk = pools(rng)
    for a in range(N):
        for s in range(2):
            q = (a + 2 * s - 1) % N
            for i in range(2):
                k, kn = int(kk[a, s, 2 * i]), int(kk[a, s, 2 * i + 1]); many = [pool[a].pop() for z in range(V // 16)]
                x[a, 2, np.array(many)] = P + s * S + kn
                t = max(many) if i == 0 else min(many); e[a, :, t] = 255; sn[a, s * S + k] = t
                u, v = pool[q].pop(), pool[q].pop(); sn[q, (1 - s) * S + kn] = u; watch(x[q], 1 - i, u, v, (1 - s) * S + k)
def newbases(rng, x, sn, e, th):
    pool, kk = pools(rng)
    for a in range(N):
        pr = np.sort(np.array(pool[a][:2 * S]).reshape(S, 2), axis=1); pr = pr[np.argsort(pr[:, 0])]
        x[a, 2, pr[:, 0]] = pr[:, 1]; x[a, 2, pr[:, 1]] = pr[:, 0]
        plant(rng, e[a], th[a], pr[:, 0], pr[:, 1], rng.integers(Q, 17, S))
        for s in range(2):
            q = (a + 2 * s - 1) % N
            for i in range(2):
                k, kn = int(kk[a, s, 2 * i]), int(kk[a, s, 2 * i + 1]); j = (s * S + kn + P - V) % (2 * S)
                y = int(pr[j // 2, j % 2]); w = pool[a].pop()
                x[a, :, w] = y; x[a, 1, y] = w; e[a, :, w] = 255; sn[a, s * S + k] = w
                u, v = pool[q].pop(), pool[q].pop(); sn[q, (1 - s) * S + kn] = u; watch(x[q], i, u, v, (1 - s) * S + k)
def setup_inputs_free(rng):
    p = rng.choice(np.concatenate([np.arange(V), P + np.arange(2 * S)]), (N, 8, 3, V)); sn = rng.integers(0, V, (N, 8, 2 * S)); m = V // 4
    det, wt = more(rng); err = errors(rng); th = levels(rng)
    for a in range(N):
        for g in range(0, 8, 2):
            o = rng.permutation(V); x = p[a, g]; x[2, o[0:2 * m:2]] = o[1:2 * m:2]; x[2, o[1:2 * m:2]] = o[0:2 * m:2]
            v = o[2 * m:]; v = v[x[2, v] < V]; x[rng.integers(0, 2, len(v)), x[2, v]] = v
            x[0, o[:40]] = o[:40]; x[1, o[20:60]] = o[20:60]; x[0, o[100:140]] = x[1, o[100:140]]; x[1, o[200:240:2]] = o[201:240:2]
            j = rng.permutation(2 * S)[:S // 2]; x[1, sn[a, g, j]] = P + j
    for a in range(N):
        for g in range(0, 8, 2):
            for s in range(2):
                q = (a + 2 * s - 1) % N; k = rng.integers(0, S, 32); k2 = rng.integers(0, S, 32)
                p[q, g, 2, sn[q, g, (1 - s) * S + k]] = P + (1 - s) * S + k2
                p[a, g, rng.integers(0, 2, 32), sn[a, g, s * S + k2]] = P + s * S + k
    p[:, 0, 2, 0] = V - 1; p[:, 0, 2, V - 1] = 0; err[:, 0, :, 0] = 255; err[:, 0, :, V - 1] = 255
    n = 16; me = np.arange(V); two, lone = {}, {}
    for a in range(N):
        for g in range(0, 8, 2):
            x = p[a, g]
            b = np.minimum(x[2], V - 1); pair = (x[2] < V) & (x[2, b] == me) & (b != me)
            t = rng.permutation(np.flatnonzero(pair & (me < b) & (me > 0)))
            two[a, g] = rng.permuted(np.stack([t[:2 * n], b[t[:2 * n]]]), axis=0)
            lone[a, g] = rng.permutation(np.flatnonzero(~pair & (me > 0) & (me < V - 1)))[:2 * n]
            cut = t[C - 4 * n:]; x[2, cut] = P + rng.integers(0, 2 * S, len(cut))
    for g in range(0, 8, 2):
        k, k2 = rng.permutation(S)[:2 * n].reshape(2, n)
        for a in range(N):
            for s in range(2):
                q = (a + 2 * s - 1) % N; u, v = two[a, g][:, s * n:(s + 1) * n]; w = lone[q, g][(1 - s) * n:(2 - s) * n]
                sn[a, g, s * S + k2] = u; sn[q, g, (1 - s) * S + k] = w
                x = p[a, g]; x[0, u] = P + s * S + k; x[1, u] = v; x[0, v] = u; x[1, v] = u
                p[q, g, 2, w] = np.where(np.arange(n) < n // 2, P + s * S + k2, (P + k2) % S + S * rng.integers(0, V // S, n))
                e = err[a, g]; c = np.concatenate([u, v]); e[:, c] = np.minimum(e[:, c], th[a, g] - 1)
                plant(rng, err[q, g], th[a, g], w, w, rng.integers(Q, 17, n))
    th[:, 1::2] = rng.integers(20, 121, (N, 4, 16, 1)); err[:, 1::2] = under(rng, th)[:, 1::2]
    p[:, 1::2, 2] = P + rng.integers(0, 2 * S, (N, 4, V)); p[:, 5] = P + rng.integers(0, 2 * S, (N, 3, V))
    sn[:, 5] = rng.choice(np.array([0, V - 1, V // 2, 5]), (N, 2 * S))
    renamed(rng, p[:, 1], sn[:, 1], err[:, 1]); allpairs(rng, p[:, 3], err[:, 3])
    crowded(rng, p[:, 5], sn[:, 5], err[:, 5]); newbases(rng, p[:, 7], sn[:, 7], err[:, 7], th[:, 7])
    return pack(err, p, sn, det, wt, th)
def setup_inputs_spread(rng):
    p, sn, o = meshes(rng, rng.integers(V // 8, V // 3 + 1, (N, 8)))
    err = (np.exp2(8 * rng.random((N, 8, 1, V))) * rng.random((N, 8, 16, V))).astype(np.int64)
    det = (np.exp2(8 * rng.random((N, 8, 1, D))) * rng.random((N, 8, 16, D))).astype(np.int64)
    wt = np.minimum(np.exp2(8 * rng.random((N, 8, 16, 1))).astype(np.int64), 255)
    th = np.clip(np.exp2(3 + 5 * rng.random((N, 8, 1, 1)) + rng.random((N, 8, 16, 1)) - 0.5).astype(np.int64), 1, 255)
    return pack(np.minimum(err, 255), p, sn, np.minimum(det, 255), wt, th)
def check_inputs(d):
    bad = []
    for k in ("err", "det"):
        x = np.asarray(d[k]).astype(np.float32)
        if not np.all((x >= 0) & (x <= 255) & (x == np.floor(x))): bad.append("range of " + k)
    for k in ("lt", "rt", "bs"):
        x = d[k]
        if not np.all(((x >= 0) & (x < V)) | ((x >= P) & (x < P + 2 * S))): bad.append("range of " + k)
    for k, lo, hi in (("snd", 0, V - 1), ("wt", 0, 255), ("th", 1, 255)):
        if np.min(d[k]) < lo or np.max(d[k]) > hi: bad.append("range of " + k)
    return bad
def ghosts(x):
    return np.concatenate([np.roll(x[..., S:], 1, axis=0), np.roll(x[..., :S], -1, axis=0)], axis=-1)
def reference(err, lt, rt, bs, snd, det, wt, th):
    take = np.take_along_axis; me = np.arange(P)
    e = np.zeros((N, 8, 16, P), np.int32); e[..., :V] = err.astype(np.float32).astype(np.int32).reshape(N, 8, 16, V)
    dt = det.astype(np.float32).astype(np.int32).reshape(N, 8, 16, D); wq = wt.astype(np.int32).reshape(N, 8, 16, 1); tq = th.astype(np.int32).reshape(N, 8, 16, 1)
    p = np.zeros((N, 8, 3, P), np.int64) + me
    p[:, :, 0, :V] = lt; p[:, :, 1, :V] = rt; p[:, :, 2, :V] = bs
    sn = snd.astype(np.int64)
    lo = np.repeat(np.array([0, S]), S); off = np.repeat(np.array([-S, S]), S)
    for t in range(RO):
        L, R, B = p[:, :, 0], p[:, :, 1], p[:, :, 2]
        j = ghosts(take(B, sn, 2)) - P + off
        gb = np.where((j >= lo) & (j < lo + S), take(sn, np.clip(j, 0, 2 * S - 1), 2), -1)
        base = np.concatenate([B, gb], axis=2); gl = (take(base, L, 2) == me)[:, :, None]; gr = (take(base, R, 2) == me)[:, :, None]
        W = e
        for it in range(IT):
            A = np.concatenate([W, ghosts(take(W, sn[:, :, None], 3))], axis=3)
            W = np.maximum(W, np.maximum(np.where(gl, take(A, L[:, :, None], 3), 0), np.where(gr, take(A, R[:, :, None], 3), 0)))
        bo = np.minimum(B, P - 1); pair = (B < P) & (take(B, bo, 2) == me) & (me < B)
        rows = np.add.reduce((np.maximum(W, take(W, bo[:, :, None], 3)) >= tq).astype(np.int32), axis=2)
        go = (pair & (rows >= Q)).astype(np.int64); k = np.add.accumulate(go, axis=2) - go
        a, g, x = np.nonzero((go == 1) & (k < C)); y = B[a, g, x]
        new = np.zeros((N, 8, P), np.int64)
        new[a, g, x] = V + 2 * C * t + 2 * k[a, g, x]; new[a, g, y] = new[a, g, x] + 1
        nx = np.concatenate([new, np.zeros((N, 8, 2 * S), np.int64)], axis=2); rx = np.concatenate([R, np.full((N, 8, 2 * S), -1)], axis=2)
        pn = np.stack([np.where((take(nx, T, 2) > 0) & (take(rx, T, 2) == me), take(nx, T, 2), T) for T in (L, R, B)], axis=2)
        sn = np.where((take(new, sn, 2) > 0) & (take(R, sn, 2) == P + np.arange(2 * S)), take(new, sn, 2), sn)
        a = np.concatenate([a, a]); g = np.concatenate([g, g]); s = np.concatenate([x, y]); o = np.concatenate([y, x])
        n, m = new[a, g, s], new[a, g, o]; bl, br = pn[a, g, 0, s], pn[a, g, 1, s]
        pn[a, g, 0, s] = n; pn[a, g, 1, s] = m; pn[a, g, 2, s] = bl
        pn[a, g, 0, n] = o; pn[a, g, 1, n] = s; pn[a, g, 2, n] = br
        p = pn
        es = e[a, g, :, s]; h = np.add.reduce(wq * e, axis=2)[a, g, s]
        for place in (s, n):
            e[a, g, :, place] = (es >> 1) + (dt[a, g, :, (h + place) & (D - 1)] >> 1)
    return {"ye": e.reshape(N, 128, P).astype(np.float32).astype(BF), "yl": p[:, :, 0].astype(np.float32), "yr": p[:, :, 1].astype(np.float32), "yb": p[:, :, 2].astype(np.float32)}

@@ -1,0 +1,684 @@
+from concourse.bass import DstId, RemoteDMATransfer
+from concourse.mybir import AluOpType as O, ActivationFunctionType as F
+
+V, P, G, Q = 2048, 3072, 3584, 9
+WW = G + 16
+ZW = 143
+bf, f4, i4, u2 = "bfloat16", "float32", "int32", "uint16"
+NCH = {0: (1, 2, 2, 1), 1: (1, 2, 2, 1)}
+
+
+def _s(n, d):
+    return ("sbuf", [128, n], d)
+
+
+SCRATCH = {}
+PACK = {}
+WIDTH = {}
+
+
+def _tiles():
+    tiles = {
+        i4: "IP 1 IG 1 II 1 IJ 1 IM 128 IM2 32 ISi 32 SNI 32 THI 1 WTI 1 MEN 128 MEN2 32 hx 64 hy 64",
+        f4: "IXX 143 IL 160 IK 128 ILs 32 IS 32 pc 1 gc 1 jc 4 jj 1 ZF 143 MEL 160 MELm 160 D256 160 MEW 160 OWN 64 OWL 64 mA 128 mB 128 mE 128 mD 128 thc 1 wtc 1 "
+            "PE 64 SN1 32 SNLf 32 gt 32 BLm 160 LM 160 RM 160 SLM 32 SRM 32 RSq 32 RSn 32 ea 160 eb 160 pa 160 pb 160 pr 160 pt 160 TH9 160 ones 160 sc 160 kk 160 c8 160 "
+            "TF 32 em 32 hz 64 TN 32 ON 32 e1 32 e2 32 e3 32 nz 160 zz 160 nq 160 pz 160 sq 32",
+        bf: "ZA 143 ZB 143 ZR 143 ZL 143 ZM 143 ZH 143 BLK 128 NLE 128 IDN 128 N4K 128 MHI 128 MLO 128 OHI 64 OLO 64 PEH 64 PEL 64 SH 32 SL_ 32 SH1 32 SL1 32 go 160",
+        u2: "SNL 32 BL 160 LL 160 RL 160 GL 160 GR 160 SL 32 SR 32 PB 160 TG 160 TD 32 HX 64",
+    }
+    for d, names in tiles.items():
+        w = names.split()
+        o = 0
+        for k, n in zip(w[0::2], w[1::2]):
+            PACK[k] = ("pk" + d, o)
+            WIDTH[k] = int(n)
+            o += (int(n) + 15) // 16 * 16
+        SCRATCH["pk" + d] = _s(o, d)
+    big = {
+        i4: "PI 384",
+        f4: "PF0 384 PF1 480 PF2 576 F3 480 q3 480",
+        bf: "HI 384 LO 384 HI1 480 LO1 480 TAB0 3584 TAB1 3584 SNDT0 576 SNDT1 576 E 3600 W1 3600 W2 3600 W3 3600 W4 2576 ED 2560 WD 1536 M 2560 FL 2560 AB 2560 AC 2560 X 2560 "
+            "OUTL 2560 OUTR 3072 OUTB 2560 NL 2560 NR 3072 NB 2560 OBS 512 OSL 512 OSR 512 ONS 512 NEW0 3584 NEW1 3584 MC0 512 MC1 512 CMP0 2816 CMP1 2816 "
+            "DR 2048 DX 2048 DT 2064 ET 512 E2 512 CL 512 OT 512 ORT 512 ONT 512 CZ 1024 " + " ".join("BB%d%d 512" % (t, k) for t in range(2) for k in range(4)),
+        u2: "GO0 32 GO1 32 GI0 32 GI1 32",
+    }
+    for d, names in big.items():
+        w = names.split()
+        for k, n in zip(w[0::2], w[1::2]):
+            WIDTH[k] = int(n)
+            SCRATCH[k] = _s(int(n), d)
+    for k in range(8):
+        WIDTH["ps%d" % k] = 512
+        SCRATCH["ps%d" % k] = ("psum", [128, 512], f4)
+
+
+_tiles()
+SEMAPHORES = ["sV", "sS", "sP", "sG", "sX", "gi0", "gi1"] + ["ga%d%d" % (t, k) for t in range(2) for k in range(4)] + ["d%d" % k for k in range(40)]
+
+
+def rank_program(g, core, T, topo):
+    rank = T.rank_of(core)
+    if rank is None:
+        return
+    eng = {"V": g.vector, "S": g.scalar, "P": g.tensor, "G": g, "Y": g.sync}
+    count = {"V": 0, "S": 0, "P": 0, "G": 0}
+    seen = {q: {} for q in eng}
+    hist = {}
+    dcount = {}
+    closed = set()
+
+    def wait(q, tok):
+        sem, val, clock = tok
+        if sem in dcount:
+            val = dcount[sem]
+            closed.add(sem)
+        if seen[q].get(sem, 0) < val:
+            eng[q].wait_ge(T.sem[sem], val)
+            seen[q][sem] = val
+        for s, v in clock.items():
+            if seen[q].get(s, 0) < v:
+                seen[q][s] = v
+
+    def deps(q, reads, writes):
+        toks = []
+        for kind, regs in (("r", reads), ("w", writes)):
+            for b, lo, hi, row in regs:
+                ps = b.startswith("ps")
+                for rlo, rhi, rrow, rk, rq, tok in hist.get(b, []):
+                    if rlo >= hi or lo >= rhi or (row is not None and rrow is not None and row != rrow):
+                        continue
+                    if rk == "r" and kind == "r" and not (ps and rq != q):
+                        continue
+                    if rq == q and q == "P" and kind == "w":
+                        continue
+                    toks.append(tok)
+        toks.sort(key=lambda t: -t[1])
+        for t in toks:
+            wait(q, t)
+
+    def note(q, reads, writes, tok):
+        for kind, regs in (("w", writes), ("r", reads)):
+            for b, lo, hi, row in regs:
+                h = hist.setdefault(b, [])
+                if kind == "w" and row is None:
+                    h[:] = [r for r in h if not (lo <= r[0] and r[1] <= hi)]
+                h.append((lo, hi, row, kind, q, tok))
+
+    def loc(b):
+        return PACK.get(b, (b, 0))
+
+    def A(b, lo=None, hi=None, st=1):
+        if lo is None:
+            lo, hi = 0, WIDTH[b]
+        return ("a", b, lo, hi, st)
+
+    def IN(b, lo, hi, ob, c0, c1):
+        return ("i", b, lo, hi, ob, c0, c1)
+
+    def mk(x):
+        if not isinstance(x, tuple):
+            return x
+        b, o = loc(x[1])
+        if x[0] == "a":
+            if x[4] == 1:
+                return T[b][:, o + x[2]:o + x[3]]
+            return T[b][:, o + x[2]:o + x[3]:x[4]]
+        ob, oo = loc(x[4])
+        return T[b][:, o + x[2]:o + x[3]].indirect(T[ob][:, oo + x[5]:oo + x[6]])
+
+    def regs(x):
+        if not isinstance(x, tuple):
+            return []
+        b, o = loc(x[1])
+        return [(b, 0, 512, None) if b.startswith("ps") else (b, o + x[2], o + x[3], None)]
+
+    def offs(x):
+        if isinstance(x, tuple) and x[0] == "i":
+            ob, oo = loc(x[4])
+            return [(ob, oo + x[5], oo + x[6], None)]
+        return []
+
+    def call(q, fn, outs, ins):
+        reads = [r for x in ins for r in regs(x) + offs(x)] + [r for x in outs for r in offs(x)]
+        writes = [r for x in outs for r in regs(x)]
+        deps(q, reads, writes)
+        sem = "s" + q
+        count[q] += 1
+        fn(eng[q]).then_inc(T.sem[sem], 1)
+        ck = dict(seen[q])
+        ck[sem] = count[q]
+        note(q, reads, writes, (sem, count[q], ck))
+
+    def copy(out, in_):
+        call("V", lambda e: e.tensor_copy(mk(out), mk(in_)), [out], [in_])
+
+    def scopy(out, in_):
+        call("S", lambda e: e.activation(mk(out), mk(in_), F.Copy), [out], [in_])
+
+    def slin(out, in_, scale, bias):
+        call("S", lambda e: e.activation(mk(out), mk(in_), F.Identity, bias=bias, scale=scale), [out], [in_])
+
+    def fill(out, c):
+        call("V", lambda e: e.memset(mk(out), c), [out], [])
+
+    def tt(out, a, b, op):
+        call("V", lambda e: e.tensor_tensor(mk(out), mk(a), mk(b), op), [out], [a, b])
+
+    def ts(out, a, s1, op0, s2=None, op1=None):
+        if op1 is None:
+            call("V", lambda e: e.tensor_scalar(mk(out), mk(a), mk(s1), None, op0), [out], [a, s1])
+        else:
+            call("V", lambda e: e.tensor_scalar(mk(out), mk(a), mk(s1), mk(s2), op0, op1), [out], [a, s1, s2])
+
+    def iota(out, pat, cm, base=0, flag=False):
+        if flag:
+            call("G", lambda e: e.iota(mk(out), pat, base, cm, allow_small_or_imprecise_dtypes=True), [out], [])
+        else:
+            call("G", lambda e: e.iota(mk(out), pat, base, cm), [out], [])
+
+    def dma(q, bat, out, in_, rd, wr):
+        assert bat not in closed
+        rd = [(loc(b)[0], loc(b)[1] + lo, loc(b)[1] + hi, row) for b, lo, hi, row in rd]
+        wr = [(loc(b)[0], loc(b)[1] + lo, loc(b)[1] + hi, row) for b, lo, hi, row in wr]
+        deps(q, rd, wr)
+        eng[q].dma_start(out, in_).then_inc(T.sem[bat], 16)
+        dcount[bat] = dcount.get(bat, 0) + 16
+        note(q, rd, wr, (bat, dcount[bat], dict(seen[q])))
+
+    def rows(q, bat, dst, lo, hi, row, tile, c0, c1):
+        b, o = loc(tile)
+        dma(q, bat, T[dst][row::16, lo:hi], T[b][:, o + c0:o + c1], [(tile, c0, c1, None)], [(dst, lo, hi, row)])
+
+    def load(q, bat, b, lo, hi, src):
+        bb, o = loc(b)
+        dma(q, bat, T[bb][:, o + lo:o + hi], src, [], [(b, lo, hi, None)])
+
+    def spread(q, bat, b, lo, hi, src):
+        while lo < hi:
+            m = min(hi, lo + 1024)
+            dma(q, bat, T[b][:, lo:m], T[src][:, 0:m - lo], [(src, 0, m - lo, None)], [(b, lo, m, None)])
+            lo = m
+
+    psn = [0]
+
+    def bank():
+        psn[0] = (psn[0] + 1) % 6
+        return "ps%d" % psn[0]
+
+    def wrap(bk, o, n, z, src, sl, w=None, r0=0, r1=16):
+        zs = [z, w or z]
+        lo = min(sl(r)[0] for r in range(r0, r1))
+        hi = max(sl(r)[1] for r in range(r0, r1))
+
+        def f(e):
+            for r in range(r0, r1):
+                zb, zo = loc(zs[r % 2])
+                a, b, st = sl(r)
+                rhs = T[src][:, a:b] if st == 1 else T[src][:, a:b:st]
+                i = e.matmul(T[bk][:, o:o + n], T[zb][:, zo + 15 - r:zo + 143 - r], rhs, r == 0, r == 15)
+            return i
+        call("P", f, [A(bk)], [A(src, lo, hi)] + [A(x) for x in sorted(set(zs))])
+
+    def wlist(bk, o, z, src, n, lo=0):
+        wrap(bk, o, n // 16, z, src, lambda r: (lo + r, lo + n, 16))
+
+    def wnat(bk, o, z, src, w):
+        wrap(bk, o, 128, z, src, lambda r: (128 * r, 128 * r + 128, 1), None, 0, 8)
+        wrap(bk, o, 128, z, src, lambda r: (128 * r, 128 * r + 128, 1), None, 8, 16)
+        if w == 160:
+            wrap(bk, o + 128, 32, z, src, lambda r: (V + 32 * r, V + 32 * r + 32, 1))
+
+    def mm(bk, o, n, z, src, start=True, stop=True, s0=0):
+        zb, zo = loc(z)
+        sb, so = loc(src)
+        call("P", lambda e: e.matmul(T[bk][:, o:o + n], T[zb][:, zo:zo + 128], T[sb][:, so + s0:so + s0 + n], start, stop), [A(bk)], [A(z, 0, 128), A(src, s0, s0 + n)])
+
+    def scal(ab, lo, hi):
+        b = bank()
+        mm(b, 0, hi - lo, "IDN", ab, s0=lo)
+        return A(b, 0, hi - lo)
+
+    nb = [T.cores[(rank - 1) % 4], T.cores[(rank + 1) % 4]]
+    lsum = [0]
+
+    def send(src, s0, w, dst, d0, sem):
+        tr = []
+        for s in range(2):
+            e = topo.engines(core, nb[s])
+            h = len(e) // 2
+            m = sum(1 << x for x in (e[:h], e[h:])[s])
+            rid, pid, _ = topo.addr(nb[s])
+            lsum[0] += h
+            tr.append(RemoteDMATransfer(dst_ids=[DstId(rid=rid, pnc=pid)], dma_engine_mask=m, remote_sem=T.sem[sem],
+                                        src=T[src][:, s0 + w * s:s0 + w * s + w], dst=T[dst][:, d0 + w * (1 - s):d0 + w * (1 - s) + w]))
+        deps("G", [(src, s0, s0 + 2 * w, None)], [])
+        g.remote_dma_fused(tr, local_sem=T.sem.sX)
+        note("X", [], [(dst, d0, d0 + 2 * w, None)], (sem, 2 * h, dict(seen["G"])))
+
+    load("Y", "d0", "PI", 256, 384, T.bs[:])
+    load("S", "d1", "SNI", 0, 16, T.snd[:, 0:256])
+    load("S", "d1", "SNI", 16, 32, T.snd[:, 256:512])
+    load("Y", "d2", "PI", 128, 256, T.rt[:])
+    load("Y", "d2", "PI", 0, 128, T.lt[:])
+    load("S", "d3", "E", 0, V, T["err"][:])
+    load("S", "d6", "ED", 0, V, T["err"][:])
+    iota(A("IP"), [[0, 1]], 1)
+    iota(A("IM"), [[1, 128]], 128)
+    iota(A("IXX"), [[1, ZW]], 0, -15, True)
+    iota(A("IM2"), [[1, 32]], 32)
+    iota(A("ISi"), [[0, 2], [1, 16]], 16)
+    iota(A("IL"), [[16, 160]], 1, 0, True)
+    iota(A("ILs"), [[256, 2], [16, 16]], 1, P, True)
+    iota(A("IK"), [[1, 128]], 0, 0, True)
+    fill(A("TAB0", 0, V), -1.0)
+    ts(A("MEN"), A("IM"), 2047, O.bitwise_and)
+    copy(A("MHI"), A("MEN"))
+    tt(A("MLO"), A("MEN"), A("MHI"), O.subtract)
+    rows("Y", "d4", "TAB0", 0, V, 6, "MHI", 0, 128)
+    rows("Y", "d4", "TAB0", 0, V, 7, "MLO", 0, 128)
+    fill(A("SNDT0"), -1.0)
+    copy(A("HI", 256, 384), A("PI", 256, 384))
+    tt(A("LO", 256, 384), A("PI", 256, 384), A("HI", 256, 384), O.subtract)
+    rows("Y", "d4", "TAB0", 0, V, 0, "HI", 256, 384)
+    rows("Y", "d4", "TAB0", 0, V, 1, "LO", 256, 384)
+    copy(A("SH"), A("SNI"))
+    tt(A("SL_"), A("SNI"), A("SH"), O.subtract)
+    for s in range(2):
+        rows("S", "d5", "SNDT0", 16 + 288 * s, 272 + 288 * s, 0, "SH", 16 * s, 16 * s + 16)
+        rows("S", "d5", "SNDT0", 16 + 288 * s, 272 + 288 * s, 1, "SL_", 16 * s, 16 * s + 16)
+    copy(A("HI", 0, 256), A("PI", 0, 256))
+    tt(A("LO", 0, 256), A("PI", 0, 256), A("HI", 0, 256), O.subtract)
+    for a, i in ((1, 2), (0, 4)):
+        rows("Y", "d4", "TAB0", 0, V, i, "HI", 128 * a, 128 * a + 128)
+        rows("Y", "d4", "TAB0", 0, V, i + 1, "LO", 128 * a, 128 * a + 128)
+    copy(A("pc"), A("IP"))
+    ts(A("IG"), A("IP"), 112, O.bitwise_and)
+    copy(A("gc"), A("IG"))
+    ts(A("II"), A("IP"), 15, O.bitwise_and)
+    ts(A("IJ"), A("II"), 1, O.arith_shift_right)
+    copy(A("jj"), A("IJ"))
+    ts(A("ZF"), A("IXX"), A("gc"), O.is_equal)
+
+    def pick(j):
+        ts(A("jc", j, j + 1), A("jj"), float(j), O.is_equal)
+        ts(A(("ZB", "ZR", "ZL", "ZM")[j]), A("ZF"), A("jc", j, j + 1), O.mult)
+    pick(0)
+    pick(2)
+    pick(1)
+    load("Y", "d8", "DR", 0, 2048, T["det"][:])
+    load("Y", "d9", "THI", 0, 1, T["th"][:])
+    load("Y", "d9", "WTI", 0, 1, T["wt"][:])
+
+    def consts_a():
+        fill(A("TAB0", V, G), -1.0)
+        ts(A("MEN2"), A("IM2"), 511, O.bitwise_and)
+        for t in range(2):
+            ts(A("OWN", 32 * t, 32 * t + 32), A("MEN2"), float(V + 512 * t), O.add)
+        copy(A("OHI"), A("OWN"))
+        tt(A("OLO"), A("OWN"), A("OHI"), O.subtract)
+        rows("Y", "d7", "TAB0", V, V + 512, 2, "OHI", 0, 32)
+        rows("Y", "d7", "TAB0", V, V + 512, 3, "OLO", 0, 32)
+
+    def consts_a2():
+        ts(A("MEL"), A("IL"), A("gc"), O.subtract)
+        pick(3)
+        fill(A("CZ"), 0.0)
+        for b in ("E", "W1", "W2", "W3"):
+            spread("Y", "d12", b, V, P, "CZ")
+            spread("Y", "d12", b, G, WW, "CZ")
+        spread("Y", "d12", "W4", V, 2576, "CZ")
+        ts(A("IDN"), A("IK"), A("pc"), O.is_equal)
+        ts(A("MELm"), A("MEL"), -2560.0, O.add)
+
+    def consts_n():
+        ts(A("N4K"), A("IK"), A("pc"), O.is_equal, -4096.0, O.mult)
+        ts(A("mD"), A("IK"), A("gc"), O.subtract)
+        ts(A("mA"), A("mD"), 0.0, O.is_ge)
+        ts(A("mB"), A("mD"), 16.0, O.is_ge)
+        ts(A("mE"), A("IK"), A("pc"), O.is_gt)
+        tt(A("BLK"), A("mA"), A("mB"), O.subtract)
+        tt(A("NLE"), A("mE"), A("mA"), O.subtract)
+        ts(A("D256"), A("MEL"), 256.0, O.add)
+        fill(A("ones"), 1.0)
+
+    def consts_b():
+        copy(A("PF0"), A("PI"))
+        copy(A("thc"), A("THI"))
+        copy(A("wtc"), A("WTI"))
+        ts(A("ILs"), A("ILs"), A("gc"), O.subtract)
+        copy(A("MEW", 0, 128), A("MEN"))
+        copy(A("MEW", 128, 160), A("OWN", 0, 32))
+        copy(A("ZA"), A("ZF"))
+
+    def consts_c():
+        ts(A("ZH"), A("ZF"), A("wtc"), O.mult)
+        for t in range(2):
+            ts(A("OWL", 32 * t, 32 * t + 32), A("MEL", 0, 32), float(V + 512 * t), O.add)
+        ts(A("ISi"), A("ISi"), 255, O.bitwise_and)
+        for s in range(2):
+            ts(A("IS", 16 * s, 16 * s + 16), A("ISi", 16 * s, 16 * s + 16), float(P + 256 * s), O.add)
+        for t in range(2):
+            copy(A("PE", 16 * t, 16 * t + 16), A("OWN", 32 * t, 32 * t + 32, 2))
+            copy(A("PE", 32 + 16 * t, 48 + 16 * t), A("OWN", 32 * t + 1, 32 * t + 32, 2))
+        copy(A("PEH"), A("PE"))
+        tt(A("PEL"), A("PE"), A("PEH"), O.subtract)
+        fill(A("DT", 2048, 2064), -128.0)
+
+    def consts_d(t):
+        spread("Y", "d%d" % (13 + t), "NEW%d" % t, 0, G, "CZ")
+        spread("Y", "d%d" % (13 + t), "MC%d" % t, 0, 512, "CZ")
+        spread("Y", "d%d" % (13 + t), "CMP%d" % t, 0, 256, "CZ")
+        if t == 0:
+            spread("Y", "d15", "OUTR", V, P, "CZ")
+            spread("Y", "d15", "NR", V, P, "CZ")
+        else:
+            spread("Y", "d16", "TAB1", 0, G, "CZ")
+            spread("Y", "d16", "SNDT1", 0, 576, "SNDT0")
+        d = "d%d" % (10 + t)
+        rows("Y", d, "MC%d" % t, 0, 512, 0, "OHI", 32 * t, 32 * t + 32)
+        rows("Y", d, "MC%d" % t, 0, 512, 1, "OLO", 32 * t, 32 * t + 32)
+        for i, o in ((6, 0), (0, 32)):
+            rows("Y", d, "CMP%d" % t, 0, 256, i, "PEH", o + 16 * t, o + 16 * t + 16)
+            rows("Y", d, "CMP%d" % t, 0, 256, i + 1, "PEL", o + 16 * t, o + 16 * t + 16)
+        if t == 1:
+            rows("Y", d, "TAB1", 0, V, 6, "MHI", 0, 128)
+            rows("Y", d, "TAB1", 0, V, 7, "MLO", 0, 128)
+            rows("Y", d, "TAB1", V, V + 512, 6, "OHI", 0, 32)
+            rows("Y", d, "TAB1", V, V + 512, 7, "OLO", 0, 32)
+            for i in (0, 2):
+                rows("Y", d, "TAB1", V + 512, P, i, "OHI", 32, 64)
+                rows("Y", d, "TAB1", V + 512, P, i + 1, "OLO", 32, 64)
+
+    late = []
+
+    for t in range(2):
+        n = V + 512 * t
+        nc = n // 16
+        h = n // 2
+        w = 128 + 32 * t
+        hh = (1024, 1536)[t]
+        TAB, SNDT, NEW, MC, CMP, PF = ["%s%d" % (x, t) for x in ("TAB", "SNDT", "NEW", "MC", "CMP", "PF")]
+        BB = ["BB%d%d" % (t, k) for k in range(4)]
+        WB = ["E", "W1", "W2", "W3", "W4"]
+        if t == 0:
+            b = bank()
+            wrap(b, 0, 34, "ZB", SNDT, lambda r: (16 + r, 16 + r + 544, 16))
+            for s in range(2):
+                copy(A("SNL", 16 * s, 16 * s + 16), A(b, 18 * s, 18 * s + 16))
+            for s in range(2):
+                copy(A("SNLf", 16 * s, 16 * s + 16), A(b, 18 * s, 18 * s + 16))
+        else:
+            late[0]()
+        copy(A("OBS"), IN(TAB, 0, n, "SNL", 0, 32))
+        b = bank()
+        wlist(b, 0, "ZB", "OBS", 512)
+        if t == 0:
+            scopy(A(BB[0]), IN("E", 0, n, "SNL", 0, 32))
+            consts_a()
+        else:
+            late[4]()
+        for s in range(2):
+            ts(A("gt", 16 * s, 16 * s + 16), A(b, 16 * s, 16 * s + 16), float(-(P + 256 * s) + 16), O.add, 15.0, O.max)
+        for s in range(2):
+            ts(A("GO%d" % t, 16 * s, 16 * s + 16), A("gt", 16 * s, 16 * s + 16), 272.0, O.min, float(288 * (1 - s)), O.add)
+        send("GO%d" % t, 0, 16, "GI%d" % t, 0, "gi%d" % t)
+        bl = bank()
+        wlist(bl, 0, "ZL", TAB, n)
+        br = bank()
+        wlist(br, 0, "ZR", TAB, n)
+        bb = bank()
+        wlist(bb, 0, "ZB", TAB, n)
+        if t == 1:
+            late[1]()
+            late[2]()
+            late[3]()
+            scopy(A(BB[0]), IN("E", 0, n, "SNL", 0, 32))
+        send(BB[0], 0, 256, "E", P, "ga%d0" % t)
+        if t == 0:
+            consts_a2()
+        copy(A("LL", 0, nc), A(bl, 0, nc))
+        ts(A("LM", 0, nc), A(bl, 0, nc), float(-G), O.add)
+        if t == 0:
+            consts_n()
+        copy(A("RL", 0, nc), A(br, 0, nc))
+        ts(A("RM", 0, nc), A(br, 0, nc), float(-G), O.add)
+        if t == 0:
+            consts_b()
+            slin(A("DX"), A("DR"), 0.5, 127.8)
+        copy(A(TAB, P, G), IN(SNDT, 0, 576, "GI%d" % t, 0, 32))
+        b1 = bank()
+        b2 = bank()
+        for j in range(2):
+            copy(A("OUTL", h * j, h * j + h), IN(TAB, 0, G, "LL", nc // 2 * j, nc // 2 * j + nc // 2))
+            scopy(A("OUTR", h * j, h * j + h), IN(TAB, 0, G, "RL", nc // 2 * j, nc // 2 * j + nc // 2))
+            wlist(b1, nc // 2 * j, "ZB", "OUTL", h, h * j)
+            wlist(b2, nc // 2 * j, "ZB", "OUTR", h, h * j)
+        ts(A("BL", 0, nc), A(bb, 0, nc), float(P - 1), O.min)
+        ts(A("BLm", 0, nc), A(bb, 0, nc), -2560.0, O.add)
+        copy(A("OSL"), IN("OUTL", 0, n, "SNL", 0, 32))
+        scopy(A("OSR"), IN("OUTR", 0, n, "SNL", 0, 32))
+        bs = bank()
+        wlist(bs, 0, "ZL", "OBS", 512)
+        wlist(bs, 32, "ZR", "OBS", 512)
+        b3 = bank()
+        wlist(b3, 0, "ZB", "OSL", 512)
+        wlist(b3, 32, "ZB", "OSR", 512)
+        scopy(A("OUTB", 0, n), IN(TAB, 0, G, "BL", 0, nc))
+        if t == 0:
+            slin(A("DT", 0, 2048), A("DX"), 1.0, -256.0)
+
+        def valid(bk, o, me, lm, gl, k):
+            x, y = ("ea", "pa") if gl in ("GL", "SL") else ("eb", "pb")
+            tt(A(x, 0, k), A(bk, o, o + k), A(me, 0, k), O.is_equal)
+            tt(A(y, 0, k), A(x, 0, k), A(lm, 0, k), O.mult)
+            ts(A(gl, 0, k), A(y, 0, k), float(G), O.add)
+
+        if t == 0:
+            consts_c()
+        valid(b2, 0, "MEL", "RM", "GR", nc)
+        valid(b1, 0, "MEL", "LM", "GL", nc)
+        for k in range(4):
+            wi, wo = WB[k], WB[k + 1]
+            nchunk = n // 512
+            na = nchunk - NCH[t][k]
+            for x, c in [("R", c) for c in range(na)] + [(x, c) for c in range(na, nchunk) for x in "LR"]:
+                scopy(A("AB" if x == "R" else "AC", 512 * c, 512 * c + 512), IN(wi, 0, WW, "G" + x, 32 * c, 32 * c + 32))
+
+            def xs(c0, c1):
+                if c0 < c1:
+                    tt(A("X", 512 * c0, 512 * c1), IN(wi, 0, WW, "GL", 32 * c0, 32 * c1), A("ED", 512 * c0, 512 * c1), O.max)
+            c0 = 0
+            if k == 0:
+                c0 = 1
+                xs(0, 1)
+                ts(A("SLM"), A(bs, 0, 32), float(-G), O.add)
+                ts(A("SRM"), A(bs, 32, 64), float(-G), O.add)
+                if t == 0:
+                    tt(A("RSq"), A(bs, 32, 64), A("ILs"), O.is_equal)
+                valid(b3, 0, "SNLf", "SLM", "SL", 32)
+                valid(b3, 32, "SNLf", "SRM", "SR", 32)
+            if k < 3:
+                tt(A("M", 0, 512), IN(wi, 0, WW, "SL", 0, 32), A(BB[k]), O.max)
+                tt(A(BB[k + 1]), IN(wi, 0, WW, "SR", 0, 32), A("M", 0, 512), O.max)
+                send(BB[k + 1], 0, 256, WB[k + 1], P, "ga%d%d" % (t, k + 1))
+            xs(c0, na)
+            for c in range(nchunk):
+                lo, hi = 512 * c, 512 * c + 512
+                if c >= na:
+                    tt(A("X", lo, hi), A("ED", lo, hi), scal("AC", lo, hi), O.max)
+                tt(A(wo, lo, hi), A("X", lo, hi), scal("AB", lo, hi), O.max)
+                if k == 3 and hi <= hh:
+                    scopy(A("WD", lo, hi), A(wo, lo, hi))
+            if k == 1:
+                if t == 0:
+                    consts_d(0)
+                wlist("ps6", 0, "ZB", "OUTB", n)
+                if t == 0:
+                    for s in range(2):
+                        wrap("ps6", 160 + 16 * s, 16, "ZR", "OBS", lambda r: (256 * s + 16 * r, 256 * s + 16 * r + 16, 1))
+            if k == 2:
+                if t == 0:
+                    tt(A("RSn"), A("ps6", 160, 192), A("IS"), O.is_equal)
+                tt(A("pr", 0, nc), A("ps6", 0, nc), A("MEL", 0, nc), O.is_equal)
+                tt(A("pt", 0, nc), A("BLm", 0, nc), A("pr", 0, nc), O.mult)
+                ts(A("PB", 0, nc), A("pt", 0, nc), 2560.0, O.add)
+                tt(A("pa", 0, nc), A("MELm", 0, nc), A("BLm", 0, nc), O.is_lt)
+                tt(A("pa", 0, nc), A("pa", 0, nc), A("pr", 0, nc), O.mult)
+                ts(A("TH9", 0, nc), A("pa", 0, nc), -1000.0, O.mult, float(Q + 1000), O.add)
+            if k == 2 and t == 0:
+                consts_d(1)
+            if k < 3:
+                wnat("ps7", w * k, "ZR", ("OUTL", "OUTR", "OUTB")[k], w)
+            if k == 3:
+                for a in range(3):
+                    tt(A("F3", a * w, a * w + w), A("ps7", a * w, a * w + w), A("MEW", 0, w), O.is_equal)
+        scopy(A("AC", hh, n), IN("W4", 0, 2576, "PB", hh // 16, nc))
+        bm = bank()
+        tt(A("M", 0, hh), IN("W4", 0, 2576, "PB", 0, hh // 16), A("WD", 0, hh), O.max)
+        ts(A("FL", 0, hh), A("M", 0, hh), A("thc"), O.is_ge)
+        parts = [(lo, hi, scal("AC", lo, hi)) for lo, hi in ((hh, hh + 512), (hh + 512, n))]
+        wlist(bm, 0, "ZA", "FL", hh)
+        for lo, hi, ps in parts:
+            tt(A("M", lo, hi), A("W4", lo, hi), ps, O.max)
+            ts(A("FL", lo, hi), A("M", lo, hi), A("thc"), O.is_ge)
+        wlist(bm, hh // 16, "ZA", "FL", n - hh, hh)
+        tt(A("go", 0, nc), A(bm, 0, nc), A("TH9", 0, nc), O.is_ge)
+        b = bank()
+        b2 = bank()
+        mm(b, 0, nc, "BLK", "go")
+        mm(b2, 0, nc, "NLE", "go", True, False)
+        mm(b2, 0, nc, "N4K", "go", False, True)
+        call("V", lambda e: e.tensor_tensor_scan(mk(A("sc", 0, nc)), mk(A("ones", 0, nc)), mk(A(b, 0, nc)), 4096.0, O.mult, O.add), [A("sc", 0, nc)], [A("ones", 0, nc), A(b, 0, nc)])
+        tt(A("kk", 0, nc), A(b2, 0, nc), A("sc", 0, nc), O.add)
+        ts(A("c8", 0, nc), A("kk", 0, nc), 256.0, O.is_ge, 8192.0, O.mult)
+        tt(A("kk", 0, nc), A("kk", 0, nc), A("c8", 0, nc), O.add)
+        tt(A("c8", 0, nc), A("kk", 0, nc), A("D256", 0, nc), O.min)
+        copy(A("TG", 0, nc), A("c8", 0, nc))
+        copy(IN(CMP, 0, 256 + n, "TG", 0, nc), A(TAB, 0, n))
+        b = bank()
+        wrap(b, 0, 32, "ZM", CMP, lambda r: (r >> 1, 256, 8), "ZB")
+        copy(A("TD"), A(b, 0, 32))
+        copy(IN(NEW, 0, G, "TD", 0, 32), A(MC))
+        copy(A("TF"), A(b, 0, 32))
+        bh = "ps7"
+
+        def errs():
+            scopy(A("ET"), IN("E", 0, P, "TD", 0, 32))
+            wlist(bh, 0, "ZH", "ET", 512)
+
+        if t == 1:
+            errs()
+        scopy(A("OT"), IN(TAB, 0, G, "TD", 0, 32))
+        scopy(A("ORT"), IN("OUTR", 0, P, "TD", 0, 32))
+        (copy, scopy)[t](A("NR", 0, 1024), IN(NEW, 0, G, "RL", 0, 64))
+        scopy(A("NR", 1024, n), IN(NEW, 0, G, "RL", 64, nc))
+        for lo, hi in ((0, 1024), (1024, n)):
+            copy(A("NB", lo, hi), IN(NEW, 0, G, "BL", lo // 16, hi // 16))
+            scopy(A("NL", lo, hi), IN(NEW, 0, G, "LL", lo // 16, hi // 16))
+        bn = bank()
+        wrap(bn, 0, 16, "ZM", CMP, lambda r: (16 * r, 16 * r + 16, 1))
+        wrap(bn, 16, 16, "ZB", CMP, lambda r: (16 * r, 16 * r + 16, 1))
+        bo = bank()
+        wnat(bo, 0, "ZB", NEW, w)
+        bR, bB, bL = bank(), bank(), bank()
+        wnat(bR, 0, "ZB", "NR", w)
+        wnat(bB, 0, "ZB", "NB", w)
+        wnat(bL, 0, "ZB", "NL", w)
+        scopy(A("ONT"), IN("NR", 0, P, "TD", 0, 32))
+        if t == 0:
+            scopy(A("ONS"), IN(NEW, 0, G, "SNL", 0, 32))
+            errs()
+        for x in range(2):
+            copy(A("TN", x, 32, 2), A(bn, 16 * x, 16 * x + 16))
+            copy(A("ON", 1 - x, 32, 2), A(bn, 16 * x, 16 * x + 16))
+        ts(A("nz", 0, w), A(bo, 0, w), 0.0, O.is_equal)
+        ts(A("zz", 0, w), A(bo, 0, w), 0.0, O.is_gt)
+        copy(A("nq", 0, w), A(bo, 0, w))
+
+        def err0(t=t, n=n):
+            tt(A("hx", 0, 32), A(bh, 0, 32), A("TF"), O.add)
+            tt(A("hx", 32, 64), A(bh, 0, 32), A("OWL", 32 * t, 32 * t + 32), O.add)
+            ts(A("hy"), A("hx"), 2047, O.bitwise_and)
+            ts(A("em"), A("TF"), float(n), O.is_ge, 2048.0, O.mult)
+            for x in range(2):
+                tt(A("hz", 32 * x, 32 * x + 32), A("hy", 32 * x, 32 * x + 32), A("em"), O.max)
+            copy(A("HX"), A("hz"))
+            ts(A("E2"), A("ET"), 0.5, O.mult, 127.8, O.add)
+            tt(A("CL"), IN("DT", 0, 2064, "HX", 0, 32), A("E2"), O.add)
+
+        def err1(n=n):
+            tt(A("E", n, n + 512), IN("DT", 0, 2064, "HX", 32, 64), A("E2"), O.add)
+
+        def err2():
+            copy(IN("E", 0, P, "TD", 0, 32), A("CL"))
+
+        def err3():
+            dma("Y", "d25", T["ED"][:], T["E"][:, 0:2560], [("E", 0, 2560, None)], [("ED", 0, 2560, None)])
+
+        late = [err0, err2, err1, err3]
+        if t == 1:
+            err0()
+            err2()
+            err1()
+            dma("Y", "d30", T["ye"][:], T["E"][:, 0:P], [("E", 0, P, None)], [])
+        PN = "PF%d" % (t + 1)
+        wn = w + 32
+        q = [A("q3", a * w, a * w + w) for a in range(3)]
+        pn = [A(PN, a * wn, a * wn + w) for a in range(3)]
+        nw = [A(PN, a * wn + w, a * wn + wn) for a in range(3)]
+        own = A("OWN", 32 * t, 32 * t + 32)
+        tt(q[1], A(bR, 0, w), A("F3", w, 2 * w), O.mult)
+        tt(q[2], A(bB, 0, w), A("F3", 2 * w, 3 * w), O.mult)
+        tt(A("pz", 0, w), A(bB, 0, w), A("zz", 0, w), O.mult)
+        tt(q[0], A(bL, 0, w), A("F3", 0, w), O.mult)
+        tt(A("q3", 0, 3 * w), A("q3", 0, 3 * w), A(PF), O.max)
+        tt(A("zz", 0, w), A("zz", 0, w), q[0], O.mult)
+        for a in range(3):
+            tt(pn[a], q[a], A("nz", 0, w), O.mult)
+        for a, x in ((0, "nq"), (1, "pz"), (2, "zz")):
+            tt(pn[a], pn[a], A(x, 0, w), O.add)
+        bq = bank()
+        wrap(bq, 0, 32, "ZR", "OT", lambda r: (32 * r, 32 * r + 32, 1))
+        wrap(bq, 32, 32, "ZR", "ORT", lambda r: (32 * r, 32 * r + 32, 1))
+        wrap(bq, 64, 32, "ZB", "ONT", lambda r: (32 * r, 32 * r + 32, 1))
+        copy(nw[1], A("TN"))
+        ts(A("e2"), A("TN"), float(n), O.is_ge)
+        tt(A("e3"), own, A("ON"), O.subtract)
+        tt(A("e3"), A("e3"), A("e2"), O.mult)
+        tt(nw[0], A("ON"), A("e3"), O.add)
+        tt(A("e1"), A(bq, 32, 64), A("TN"), O.is_equal)
+        tt(A("e1"), A(bq, 64, 96), A("e1"), O.mult)
+        tt(nw[2], A(bq, 0, 32), A("e1"), O.max)
+        if t == 1:
+            for a, y in enumerate(("yl", "yr", "yb")):
+                for lo, hi, c0, c1 in ((0, V, 0, 128), (V, V + 512, 128, 160), (V + 512, P, 160, 192)):
+                    dma("YSY"[a], "d31", T[y][:, lo:hi], T[PN][:, a * wn + c0:a * wn + c1], [(PN, a * wn, a * wn + wn, None)], [])
+            break
+        copy(A("HI1"), A(PN))
+        tt(A("LO1"), A(PN), A("HI1"), O.subtract)
+        for a, i in ((2, 0), (1, 2), (0, 4)):
+            for hl, x in enumerate(("HI1", "LO1")):
+                rows("YS"[hl], "d20", "TAB1", 0, V, i + hl, x, a * wn, a * wn + w)
+                rows("YS"[hl], "d20", "TAB1", V, V + 512, i + hl, x, a * wn + w, a * wn + wn)
+        bs = bank()
+        wlist(bs, 0, "ZB", "ONS", 512)
+        tt(A("sq"), A(bs, 0, 32), A("RSq"), O.mult)
+        tt(A("SNLf"), A("SNLf"), A("sq"), O.max)
+        copy(A("SNL"), A("SNLf"))
+        for s in range(2):
+            wrap("ps6", 16 * s, 16, "ZB", "ONS", lambda r: (256 * s + 16 * r, 256 * s + 16 * r + 16, 1))
+
+        def snd_rows():
+            tt(A("sq"), A("ps6", 0, 32), A("RSn"), O.mult)
+            tt(A("SN1"), A("sq"), A("SNI"), O.max)
+            copy(A("SH1"), A("SN1"))
+            tt(A("SL1"), A("SN1"), A("SH1"), O.subtract)
+            for s in range(2):
+                rows("Y", "d24", "SNDT1", 16 + 288 * s, 272 + 288 * s, 0, "SH1", 16 * s, 16 * s + 16)
+                rows("Y", "d24", "SNDT1", 16 + 288 * s, 272 + 288 * s, 1, "SL1", 16 * s, 16 * s + 16)
+        late.append(snd_rows)
+    for d in sorted(dcount):
+        wait("Y", (d, dcount[d], {}))
+    for q in ("V", "S", "P", "G"):
+        wait("Y", ("s" + q, count[q], {}))
+    g.wait_ge(T.sem.sX, lsum[0])

@@ -4,8 +4,10 @@ from concourse.mybir import AluOpType as O, ActivationFunctionType as F
 V, P, G, Q = 2048, 3072, 3584, 9
 WW = G + 16
 ZW = 143
+DUMP = 3 * WW
+BIG = 16384.0
 bf, f4, i4, u2 = "bfloat16", "float32", "int32", "uint16"
-NCH = {0: (1, 2, 2, 1), 1: (1, 2, 2, 1)}
+VPART = (1280, 1536)
 
 
 def _s(n, d):
@@ -19,12 +21,13 @@ WIDTH = {}
 
 def _tiles():
     tiles = {
-        i4: "IP 1 IG 1 II 1 IJ 1 IM 128 IM2 32 ISi 32 SNI 32 THI 1 WTI 1 MEN 128 MEN2 32 hx 64 hy 64",
-        f4: "IXX 143 IL 160 IK 128 ILs 32 IS 32 pc 1 gc 1 jc 4 jj 1 ZF 143 MEL 160 MELm 160 D256 160 MEW 160 OWN 64 OWL 64 mA 128 mB 128 mE 128 mD 128 thc 1 wtc 1 "
-            "PE 64 SN1 32 SNLf 32 gt 32 BLm 160 LM 160 RM 160 SLM 32 SRM 32 RSq 32 RSn 32 ea 160 eb 160 pa 160 pb 160 pr 160 pt 160 TH9 160 ones 160 sc 160 kk 160 c8 160 "
-            "TF 32 em 32 hz 64 TN 32 ON 32 e1 32 e2 32 e3 32 nz 160 zz 160 nq 160 pz 160 sq 32",
-        bf: "ZA 143 ZB 143 ZR 143 ZL 143 ZM 143 ZH 143 BLK 128 NLE 128 IDN 128 N4K 128 MHI 128 MLO 128 OHI 64 OLO 64 PEH 64 PEL 64 SH 32 SL_ 32 SH1 32 SL1 32 go 160",
-        u2: "SNL 32 BL 160 LL 160 RL 160 GL 160 GR 160 SL 32 SR 32 PB 160 TG 160 TD 32 HX 64",
+        i4: "IP 1 IG 1 II 1 IJ 1 IO 1 IM 128 IM2 32 SNI 32 THI 1 WTI 1 MEN 128 hx 64 hy 64",
+        f4: "IXX 143 IL 160 IK 128 ILs 32 IS 32 IB 12 pc 1 gc 1 jc 6 jj 1 ev 1 odf 1 one 1 nth 1 bth 1 ZF 143 MEL 160 D1280 160 MEW 160 OWL 64 mA 128 mB 128 mE 128 mD 128 wtc 1 "
+            "SN1 32 SNLf 32 LM 160 RM 160 SM 64 RSq 32 RSn 32 pa 160 pb 160 ones 160 sc 160 c8 160 "
+            "TF 32 em 32 hz 64 DUM 32 e1 64 e2 32 e3 32 sq 32 GOf 32 GOd 32 alt 32 sp 32 sg 160 ql 160 da 160 db 160 dc 160 eq2 320 eqb 160 nw 96",
+        bf: "ZA 143 ZB 143 ZR 143 ZL 143 ZM 143 ZO 143 ZT 143 ZU 143 TH 160 TL 160 ZH 143 BLK 128 NLE 128 IDN 128 N4K 128 SH 32 SL_ 32 SH1 32 SL1 32 go 160 ne 160 ge 160 "
+            "thc 1 od 1 c1 1 HB 12 LOW 256",
+        u2: "SNL 32 BL 160 LL 160 RL 160 GL 160 GR 160 SRAW 64 SG 64 TG 160 TD 32 HX 64 TR 32",
     }
     for d, names in tiles.items():
         w = names.split()
@@ -35,11 +38,11 @@ def _tiles():
             o += (int(n) + 15) // 16 * 16
         SCRATCH["pk" + d] = _s(o, d)
     big = {
-        i4: "PI 384",
-        f4: "PF0 384 PF1 480 PF2 576 F3 480 q3 480",
-        bf: "HI 384 LO 384 HI1 480 LO1 480 TAB0 3584 TAB1 3584 SNDT0 576 SNDT1 576 E 3600 W1 3600 W2 3600 W3 3600 W4 2576 ED 2560 WD 1536 M 2560 FL 2560 AB 2560 AC 2560 X 2560 "
-            "OUTL 2560 OUTR 3072 OUTB 2560 NL 2560 NR 3072 NB 2560 OBS 512 OSL 512 OSR 512 ONS 512 NEW0 3584 NEW1 3584 MC0 512 MC1 512 CMP0 2816 CMP1 2816 "
-            "DR 2048 DX 2048 DT 2064 ET 512 E2 512 CL 512 OT 512 ORT 512 ONT 512 CZ 1024 " + " ".join("BB%d%d 512" % (t, k) for t in range(2) for k in range(4)),
+        i4: "PI 384 PX 480",
+        f4: "OV 480 PO 480 PN 480",
+        bf: "HI 384 LO 384 TAB 3584 SNDT 544 E 3600 WALL 13360 M 2560 FL 2560 AB 2560 AQ 512 "
+            "OUTL 3072 OUTR 2560 OUTB 2560 OBS 512 OSS 1024 ONS 512 CMP 3840 "
+            "DR 2048 DX 2048 DT 2064 DG 1024 ET 512 E2 512 CR 512 GT 512 ONT 512 " + " ".join("BB%d%d 512" % (t, k) for t in range(2) for k in range(4)),
         u2: "GO0 32 GO1 32 GI0 32 GI1 32",
     }
     for d, names in big.items():
@@ -47,6 +50,10 @@ def _tiles():
         for k, n in zip(w[0::2], w[1::2]):
             WIDTH[k] = int(n)
             SCRATCH[k] = _s(int(n), d)
+    for k, b, o, n in [("W%d" % k, "WALL", WW * (k - 1), WW if k < 4 else 2560) for k in (1, 2, 3, 4)] + [
+            ("RN", "WALL", 0, DUMP + 512), ("H", "OUTL", 0, P), ("OS", "OUTL", 0, P)]:
+        PACK[k] = (b, o)
+        WIDTH[k] = n
     for k in range(8):
         WIDTH["ps%d" % k] = 512
         SCRATCH["ps%d" % k] = ("psum", [128, 512], f4)
@@ -152,8 +159,8 @@ def rank_program(g, core, T, topo):
     def copy(out, in_):
         call("V", lambda e: e.tensor_copy(mk(out), mk(in_)), [out], [in_])
 
-    def scopy(out, in_):
-        call("S", lambda e: e.activation(mk(out), mk(in_), F.Copy), [out], [in_])
+    def scopy(out, in_, f=F.Copy):
+        call("S", lambda e: e.activation(mk(out), mk(in_), f), [out], [in_])
 
     def slin(out, in_, scale, bias):
         call("S", lambda e: e.activation(mk(out), mk(in_), F.Identity, bias=bias, scale=scale), [out], [in_])
@@ -169,6 +176,10 @@ def rank_program(g, core, T, topo):
             call("V", lambda e: e.tensor_scalar(mk(out), mk(a), mk(s1), None, op0), [out], [a, s1])
         else:
             call("V", lambda e: e.tensor_scalar(mk(out), mk(a), mk(s1), mk(s2), op0, op1), [out], [a, s1, s2])
+
+    def hilo(hi, lo, x):
+        copy(hi, x)
+        tt(lo, x, hi, O.subtract)
 
     def iota(out, pat, cm, base=0, flag=False):
         if flag:
@@ -187,62 +198,53 @@ def rank_program(g, core, T, topo):
 
     def rows(q, bat, dst, lo, hi, row, tile, c0, c1):
         b, o = loc(tile)
-        dma(q, bat, T[dst][row::16, lo:hi], T[b][:, o + c0:o + c1], [(tile, c0, c1, None)], [(dst, lo, hi, row)])
+        db, do = loc(dst)
+        dma(q, bat, T[db][row::16, do + lo:do + hi], T[b][:, o + c0:o + c1], [(tile, c0, c1, None)], [(dst, lo, hi, row)])
+
+    def rows2(q, bat, dst, lo, hi, row, th, tl, c0, c1):
+        rows(q[0], bat, dst, lo, hi, row, th, c0, c1)
+        rows(q[-1], bat, dst, lo, hi, row + 1, tl, c0, c1)
 
     def load(q, bat, b, lo, hi, src):
         bb, o = loc(b)
         dma(q, bat, T[bb][:, o + lo:o + hi], src, [], [(b, lo, hi, None)])
 
-    def spread(q, bat, b, lo, hi, src):
-        while lo < hi:
-            m = min(hi, lo + 1024)
-            dma(q, bat, T[b][:, lo:m], T[src][:, 0:m - lo], [(src, 0, m - lo, None)], [(b, lo, m, None)])
-            lo = m
+    def gfill(b, lo, hi):
+        iota(A(b, lo, hi), [[0, hi - lo]], 0, 0, True)
 
-    psn = [0]
-
-    def bank():
-        psn[0] = (psn[0] + 1) % 6
-        return "ps%d" % psn[0]
-
-    def wrap(bk, o, n, z, src, sl, w=None, r0=0, r1=16):
+    def wrap(bk, o, n, z, src, sl, w=None, first=True, last=True):
         zs = [z, w or z]
-        lo = min(sl(r)[0] for r in range(r0, r1))
-        hi = max(sl(r)[1] for r in range(r0, r1))
+        sb, so = loc(src)
+        lo = min(sl(r)[0] for r in range(16))
+        hi = max(sl(r)[1] for r in range(16))
 
         def f(e):
-            for r in range(r0, r1):
+            for r in range(16):
                 zb, zo = loc(zs[r % 2])
                 a, b, st = sl(r)
-                rhs = T[src][:, a:b] if st == 1 else T[src][:, a:b:st]
-                i = e.matmul(T[bk][:, o:o + n], T[zb][:, zo + 15 - r:zo + 143 - r], rhs, r == 0, r == 15)
+                rhs = T[sb][:, so + a:so + b] if st == 1 else T[sb][:, so + a:so + b:st]
+                i = e.matmul(T[bk][:, o:o + n], T[zb][:, zo + 15 - r:zo + 143 - r], rhs, first and r == 0, last and r == 15)
             return i
         call("P", f, [A(bk)], [A(src, lo, hi)] + [A(x) for x in sorted(set(zs))])
 
-    def wlist(bk, o, z, src, n, lo=0):
-        wrap(bk, o, n // 16, z, src, lambda r: (lo + r, lo + n, 16))
+    def wlist(bk, o, z, src, n, lo=0, first=True, last=True):
+        wrap(bk, o, n // 16, z, src, lambda r: (lo + r, lo + n, 16), first=first, last=last)
 
-    def wnat(bk, o, z, src, w):
-        wrap(bk, o, 128, z, src, lambda r: (128 * r, 128 * r + 128, 1), None, 0, 8)
-        wrap(bk, o, 128, z, src, lambda r: (128 * r, 128 * r + 128, 1), None, 8, 16)
-        if w == 160:
-            wrap(bk, o + 128, 32, z, src, lambda r: (V + 32 * r, V + 32 * r + 32, 1))
+    def wnat(bk, o, z, src, w, s0=0):
+        wrap(bk, o, w, z, src, lambda r: (s0 + w * r, s0 + w * r + w, 1))
 
     def mm(bk, o, n, z, src, start=True, stop=True, s0=0):
         zb, zo = loc(z)
         sb, so = loc(src)
         call("P", lambda e: e.matmul(T[bk][:, o:o + n], T[zb][:, zo:zo + 128], T[sb][:, so + s0:so + s0 + n], start, stop), [A(bk)], [A(z, 0, 128), A(src, s0, s0 + n)])
 
-    def scal(ab, lo, hi):
-        b = bank()
-        mm(b, 0, hi - lo, "IDN", ab, s0=lo)
-        return A(b, 0, hi - lo)
-
     nb = [T.cores[(rank - 1) % 4], T.cores[(rank + 1) % 4]]
     lsum = [0]
 
     def send(src, s0, w, dst, d0, sem):
         tr = []
+        dst, do = loc(dst)
+        d0 += do
         for s in range(2):
             e = topo.engines(core, nb[s])
             h = len(e) // 2
@@ -255,428 +257,504 @@ def rank_program(g, core, T, topo):
         g.remote_dma_fused(tr, local_sem=T.sem.sX)
         note("X", [], [(dst, d0, d0 + 2 * w, None)], (sem, 2 * h, dict(seen["G"])))
 
-    load("Y", "d0", "PI", 256, 384, T.bs[:])
-    load("S", "d1", "SNI", 0, 16, T.snd[:, 0:256])
-    load("S", "d1", "SNI", 16, 32, T.snd[:, 256:512])
-    load("Y", "d2", "PI", 128, 256, T.rt[:])
-    load("Y", "d2", "PI", 0, 128, T.lt[:])
-    load("S", "d3", "E", 0, V, T["err"][:])
-    load("S", "d6", "ED", 0, V, T["err"][:])
+    TAB, SNDT, CMP = "TAB", "SNDT", "CMP"
+
+    load("Y", "d1", "SNI", 0, 32, T.snd[:])
+    load("S", "d0", "PI", 256, 384, T.bs[:])
+    load("Y", "d2", "PI", 0, 128, T.rt[:])
+    load("S", "d3", "PI", 128, 256, T.lt[:])
+    load("Y", "d6", "E", 0, V, T["err"][:])
     iota(A("IP"), [[0, 1]], 1)
-    iota(A("IM"), [[1, 128]], 128)
+    iota(A("IB"), [[256, 12]], 0, 0, True)
+    iota(A("LOW"), [[1, 256]], 0, 0, True)
     iota(A("IXX"), [[1, ZW]], 0, -15, True)
-    iota(A("IM2"), [[1, 32]], 32)
-    iota(A("ISi"), [[0, 2], [1, 16]], 16)
     iota(A("IL"), [[16, 160]], 1, 0, True)
-    iota(A("ILs"), [[256, 2], [16, 16]], 1, P, True)
     iota(A("IK"), [[1, 128]], 0, 0, True)
-    fill(A("TAB0", 0, V), -1.0)
-    ts(A("MEN"), A("IM"), 2047, O.bitwise_and)
-    copy(A("MHI"), A("MEN"))
-    tt(A("MLO"), A("MEN"), A("MHI"), O.subtract)
-    rows("Y", "d4", "TAB0", 0, V, 6, "MHI", 0, 128)
-    rows("Y", "d4", "TAB0", 0, V, 7, "MLO", 0, 128)
-    fill(A("SNDT0"), -1.0)
-    copy(A("HI", 256, 384), A("PI", 256, 384))
-    tt(A("LO", 256, 384), A("PI", 256, 384), A("HI", 256, 384), O.subtract)
-    rows("Y", "d4", "TAB0", 0, V, 0, "HI", 256, 384)
-    rows("Y", "d4", "TAB0", 0, V, 1, "LO", 256, 384)
-    copy(A("SH"), A("SNI"))
-    tt(A("SL_"), A("SNI"), A("SH"), O.subtract)
-    for s in range(2):
-        rows("S", "d5", "SNDT0", 16 + 288 * s, 272 + 288 * s, 0, "SH", 16 * s, 16 * s + 16)
-        rows("S", "d5", "SNDT0", 16 + 288 * s, 272 + 288 * s, 1, "SL_", 16 * s, 16 * s + 16)
-    copy(A("HI", 0, 256), A("PI", 0, 256))
-    tt(A("LO", 0, 256), A("PI", 0, 256), A("HI", 0, 256), O.subtract)
-    for a, i in ((1, 2), (0, 4)):
-        rows("Y", "d4", "TAB0", 0, V, i, "HI", 128 * a, 128 * a + 128)
-        rows("Y", "d4", "TAB0", 0, V, i + 1, "LO", 128 * a, 128 * a + 128)
-    copy(A("pc"), A("IP"))
-    ts(A("IG"), A("IP"), 112, O.bitwise_and)
-    copy(A("gc"), A("IG"))
+    iota(A("IM"), [[1, 128]], 128)
+    iota(A("IM2"), [[1, 32]], 32)
+    iota(A("ILs"), [[256, 2], [16, 16]], 1, P - G, True)
+    iota(A("MEW"), [[1, 160]], 160, 0, True)
+    gfill("E", V, P)
+    fill(A(SNDT), -1.0)
+    ts(A("IO"), A("IP"), 1, O.bitwise_and)
     ts(A("II"), A("IP"), 15, O.bitwise_and)
+    ts(A("IG"), A("IP"), 112, O.bitwise_and)
+    copy(A("odf"), A("IO"))
+    ts(A("ev"), A("IO"), -1.0, O.mult, 1.0, O.add)
     ts(A("IJ"), A("II"), 1, O.arith_shift_right)
+    ts(A("HB"), A("IB"), A("ev"), O.mult)
+    copy(A("gc"), A("IG"))
     copy(A("jj"), A("IJ"))
+
+    def own(b0, b1):
+        for b in range(b0, b1):
+            x, y = A(TAB, 256 * b, 256 * b + 256), A("HB", b, b + 1)
+            call("S", lambda e: e.activation(mk(x), mk(A("LOW")), F.Identity, bias=mk(y), scale=mk(A("odf"))), [x], [y, A("LOW"), A("odf")])
+    own(0, 8)
     ts(A("ZF"), A("IXX"), A("gc"), O.is_equal)
 
     def pick(j):
         ts(A("jc", j, j + 1), A("jj"), float(j), O.is_equal)
-        ts(A(("ZB", "ZR", "ZL", "ZM")[j]), A("ZF"), A("jc", j, j + 1), O.mult)
-    pick(0)
-    pick(2)
-    pick(1)
-    load("Y", "d8", "DR", 0, 2048, T["det"][:])
+        ts(A(("ZB", "ZR", "ZL", "ZM", "ZT", "ZU")[j]), A("ZF"), A("jc", j, j + 1), O.mult)
+    hilo(A("SH"), A("SL_"), A("SNI"))
+    rows2("SY", "d5", SNDT, 16, 528, 0, "SH", "SL_", 0, 32)
+    for a in (2, 0, 1):
+        hilo(A("HI", 128 * a, 128 * a + 128), A("LO", 128 * a, 128 * a + 128), A("PI", 128 * a, 128 * a + 128))
+        rows2("SY", "d4", TAB, 0, V, (2, 4, 0)[a], "HI", "LO", 128 * a, 128 * a + 128)
     load("Y", "d9", "THI", 0, 1, T["th"][:])
     load("Y", "d9", "WTI", 0, 1, T["wt"][:])
+    pick(0)
+    pick(1)
+    pick(2)
+    own(8, 12)
+    ts(A("MEN"), A("IM"), 2047, O.bitwise_and)
+    copy(A("pc"), A("IP"))
+    ts(A("MEL"), A("IL"), A("gc"), O.subtract)
+    ts(A("IDN"), A("IK"), A("pc"), O.is_equal)
+    ts(A("ILs"), A("ILs"), A("gc"), O.subtract)
+    for b in ("E", "W1", "W2", "W3"):
+        fill(A(b, G, WW), 0.0)
+    fill(A("W1", V, P), 0.0)
+    fill(A("DT", 2048, 2064), -128.0)
 
     def consts_a():
-        fill(A("TAB0", V, G), -1.0)
-        ts(A("MEN2"), A("IM2"), 511, O.bitwise_and)
-        for t in range(2):
-            ts(A("OWN", 32 * t, 32 * t + 32), A("MEN2"), float(V + 512 * t), O.add)
-        copy(A("OHI"), A("OWN"))
-        tt(A("OLO"), A("OWN"), A("OHI"), O.subtract)
-        rows("Y", "d7", "TAB0", V, V + 512, 2, "OHI", 0, 32)
-        rows("Y", "d7", "TAB0", V, V + 512, 3, "OLO", 0, 32)
-
-    def consts_a2():
-        ts(A("MEL"), A("IL"), A("gc"), O.subtract)
-        pick(3)
-        fill(A("CZ"), 0.0)
-        for b in ("E", "W1", "W2", "W3"):
-            spread("Y", "d12", b, V, P, "CZ")
-            spread("Y", "d12", b, G, WW, "CZ")
-        spread("Y", "d12", "W4", V, 2576, "CZ")
-        ts(A("IDN"), A("IK"), A("pc"), O.is_equal)
-        ts(A("MELm"), A("MEL"), -2560.0, O.add)
+        for j in (3, 4, 5):
+            pick(j)
+        ts(A("ev"), A("jj"), 7.0, O.is_equal, 4096.0, O.mult)
+        ts(A("c1"), A("II"), 7.0, O.is_equal)
+        ts(A("od"), A("II"), 8.0, O.is_ge, BIG, O.mult)
+        tt(A("ev"), A("ev"), A("jc", 3, 4), O.add)
+        copy(A("ZA"), A("ZF"))
+        tt(A("c1"), A("c1"), A("od"), O.add)
+        ts(A("jj"), A("gc"), 160.0, O.mult)
+        ts(A("ZO"), A("ZF"), A("ev"), O.mult)
+        ts(A("MEW"), A("MEW"), A("jj"), O.subtract)
+        ts(A("N4K"), A("IK"), A("pc"), O.is_equal, -4096.0, O.mult)
 
     def consts_n():
-        ts(A("N4K"), A("IK"), A("pc"), O.is_equal, -4096.0, O.mult)
         ts(A("mD"), A("IK"), A("gc"), O.subtract)
+        ts(A("mE"), A("IK"), A("pc"), O.is_gt)
         ts(A("mA"), A("mD"), 0.0, O.is_ge)
         ts(A("mB"), A("mD"), 16.0, O.is_ge)
-        ts(A("mE"), A("IK"), A("pc"), O.is_gt)
+        ts(A("D1280"), A("MEL"), 1280.0, O.add)
         tt(A("BLK"), A("mA"), A("mB"), O.subtract)
         tt(A("NLE"), A("mE"), A("mA"), O.subtract)
-        ts(A("D256"), A("MEL"), 256.0, O.add)
         fill(A("ones"), 1.0)
-
-    def consts_b():
-        copy(A("PF0"), A("PI"))
-        copy(A("thc"), A("THI"))
-        copy(A("wtc"), A("WTI"))
-        ts(A("ILs"), A("ILs"), A("gc"), O.subtract)
-        copy(A("MEW", 0, 128), A("MEN"))
-        copy(A("MEW", 128, 160), A("OWN", 0, 32))
-        copy(A("ZA"), A("ZF"))
+        fill(A("one"), 1.0)
 
     def consts_c():
-        ts(A("ZH"), A("ZF"), A("wtc"), O.mult)
+        copy(A("wtc"), A("WTI"))
+        copy(A("thc"), A("THI"))
         for t in range(2):
             ts(A("OWL", 32 * t, 32 * t + 32), A("MEL", 0, 32), float(V + 512 * t), O.add)
-        ts(A("ISi"), A("ISi"), 255, O.bitwise_and)
-        for s in range(2):
-            ts(A("IS", 16 * s, 16 * s + 16), A("ISi", 16 * s, 16 * s + 16), float(P + 256 * s), O.add)
-        for t in range(2):
-            copy(A("PE", 16 * t, 16 * t + 16), A("OWN", 32 * t, 32 * t + 32, 2))
-            copy(A("PE", 32 + 16 * t, 48 + 16 * t), A("OWN", 32 * t + 1, 32 * t + 32, 2))
-        copy(A("PEH"), A("PE"))
-        tt(A("PEL"), A("PE"), A("PEH"), O.subtract)
-        fill(A("DT", 2048, 2064), -128.0)
+        ts(A("IM2"), A("IM2"), 511, O.bitwise_and)
+        ts(A("DUM"), A("MEL", 0, 32), float(DUMP), O.add)
+        ts(A("ZH"), A("ZF"), A("wtc"), O.mult)
+        ts(A("IS"), A("IM2"), float(P), O.add)
+        ts(A("nth"), A("THI"), -1.0, O.mult, 0.5, O.add)
+        ts(A("bth"), A("THI"), -256.0, O.mult, 256.0, O.add)
 
-    def consts_d(t):
-        spread("Y", "d%d" % (13 + t), "NEW%d" % t, 0, G, "CZ")
-        spread("Y", "d%d" % (13 + t), "MC%d" % t, 0, 512, "CZ")
-        spread("Y", "d%d" % (13 + t), "CMP%d" % t, 0, 256, "CZ")
-        if t == 0:
-            spread("Y", "d15", "OUTR", V, P, "CZ")
-            spread("Y", "d15", "NR", V, P, "CZ")
-        else:
-            spread("Y", "d16", "TAB1", 0, G, "CZ")
-            spread("Y", "d16", "SNDT1", 0, 576, "SNDT0")
-        d = "d%d" % (10 + t)
-        rows("Y", d, "MC%d" % t, 0, 512, 0, "OHI", 32 * t, 32 * t + 32)
-        rows("Y", d, "MC%d" % t, 0, 512, 1, "OLO", 32 * t, 32 * t + 32)
-        for i, o in ((6, 0), (0, 32)):
-            rows("Y", d, "CMP%d" % t, 0, 256, i, "PEH", o + 16 * t, o + 16 * t + 16)
-            rows("Y", d, "CMP%d" % t, 0, 256, i + 1, "PEL", o + 16 * t, o + 16 * t + 16)
-        if t == 1:
-            rows("Y", d, "TAB1", 0, V, 6, "MHI", 0, 128)
-            rows("Y", d, "TAB1", 0, V, 7, "MLO", 0, 128)
-            rows("Y", d, "TAB1", V, V + 512, 6, "OHI", 0, 32)
-            rows("Y", d, "TAB1", V, V + 512, 7, "OLO", 0, 32)
-            for i in (0, 2):
-                rows("Y", d, "TAB1", V + 512, P, i, "OHI", 32, 64)
-                rows("Y", d, "TAB1", V + 512, P, i + 1, "OLO", 32, 64)
+    def slotcol(out, src):
+        ts(A(out, 0, 16), A(src[0], src[1], src[1] + 16), float(272 - P), O.add, 528.0, O.min)
+        ts(A(out, 16, 32), A(src[0], src[1] + 16, src[1] + 32), float(16 - 256 - P), O.add)
 
-    late = []
+    def ghost_bases(t):
+        scopy(A(TAB, P, P + 256), IN(SNDT, 0, 544, "GI%d" % t, 0, 16))
+        copy(A(TAB, P + 256, G), IN(SNDT, 0, 544, "GI%d" % t, 16, 32))
 
     for t in range(2):
         n = V + 512 * t
         nc = n // 16
         h = n // 2
+        hc = nc // 2
         w = 128 + 32 * t
-        hh = (1024, 1536)[t]
-        TAB, SNDT, NEW, MC, CMP, PF = ["%s%d" % (x, t) for x in ("TAB", "SNDT", "NEW", "MC", "CMP", "PF")]
+        nchunk = n // 512
+        PF = ("PI", "PN")[t]
+        ME = ("MEN", "MEW")[t]
         BB = ["BB%d%d" % (t, k) for k in range(4)]
         WB = ["E", "W1", "W2", "W3", "W4"]
-        if t == 0:
-            b = bank()
-            wrap(b, 0, 34, "ZB", SNDT, lambda r: (16 + r, 16 + r + 544, 16))
-            for s in range(2):
-                copy(A("SNL", 16 * s, 16 * s + 16), A(b, 18 * s, 18 * s + 16))
-            for s in range(2):
-                copy(A("SNLf", 16 * s, 16 * s + 16), A(b, 18 * s, 18 * s + 16))
-        else:
-            late[0]()
-        copy(A("OBS"), IN(TAB, 0, n, "SNL", 0, 32))
-        b = bank()
-        wlist(b, 0, "ZB", "OBS", 512)
-        if t == 0:
-            scopy(A(BB[0]), IN("E", 0, n, "SNL", 0, 32))
-            consts_a()
-        else:
-            late[4]()
-        for s in range(2):
-            ts(A("gt", 16 * s, 16 * s + 16), A(b, 16 * s, 16 * s + 16), float(-(P + 256 * s) + 16), O.add, 15.0, O.max)
-        for s in range(2):
-            ts(A("GO%d" % t, 16 * s, 16 * s + 16), A("gt", 16 * s, 16 * s + 16), 272.0, O.min, float(288 * (1 - s)), O.add)
-        send("GO%d" % t, 0, 16, "GI%d" % t, 0, "gi%d" % t)
-        bl = bank()
-        wlist(bl, 0, "ZL", TAB, n)
-        br = bank()
-        wlist(br, 0, "ZR", TAB, n)
-        bb = bank()
-        wlist(bb, 0, "ZB", TAB, n)
-        if t == 1:
-            late[1]()
-            late[2]()
-            late[3]()
-            scopy(A(BB[0]), IN("E", 0, n, "SNL", 0, 32))
-        send(BB[0], 0, 256, "E", P, "ga%d0" % t)
-        if t == 0:
-            consts_a2()
-        copy(A("LL", 0, nc), A(bl, 0, nc))
-        ts(A("LM", 0, nc), A(bl, 0, nc), float(-G), O.add)
-        if t == 0:
-            consts_n()
-        copy(A("RL", 0, nc), A(br, 0, nc))
-        ts(A("RM", 0, nc), A(br, 0, nc), float(-G), O.add)
-        if t == 0:
-            consts_b()
-            slin(A("DX"), A("DR"), 0.5, 127.8)
-        copy(A(TAB, P, G), IN(SNDT, 0, 576, "GI%d" % t, 0, 32))
-        b1 = bank()
-        b2 = bank()
-        for j in range(2):
-            copy(A("OUTL", h * j, h * j + h), IN(TAB, 0, G, "LL", nc // 2 * j, nc // 2 * j + nc // 2))
-            scopy(A("OUTR", h * j, h * j + h), IN(TAB, 0, G, "RL", nc // 2 * j, nc // 2 * j + nc // 2))
-            wlist(b1, nc // 2 * j, "ZB", "OUTL", h, h * j)
-            wlist(b2, nc // 2 * j, "ZB", "OUTR", h, h * j)
-        ts(A("BL", 0, nc), A(bb, 0, nc), float(P - 1), O.min)
-        ts(A("BLm", 0, nc), A(bb, 0, nc), -2560.0, O.add)
-        copy(A("OSL"), IN("OUTL", 0, n, "SNL", 0, 32))
-        scopy(A("OSR"), IN("OUTR", 0, n, "SNL", 0, 32))
-        bs = bank()
-        wlist(bs, 0, "ZL", "OBS", 512)
-        wlist(bs, 32, "ZR", "OBS", 512)
-        b3 = bank()
-        wlist(b3, 0, "ZB", "OSL", 512)
-        wlist(b3, 32, "ZB", "OSR", 512)
-        scopy(A("OUTB", 0, n), IN(TAB, 0, G, "BL", 0, nc))
-        if t == 0:
-            slin(A("DT", 0, 2048), A("DX"), 1.0, -256.0)
 
-        def valid(bk, o, me, lm, gl, k):
-            x, y = ("ea", "pa") if gl in ("GL", "SL") else ("eb", "pb")
-            tt(A(x, 0, k), A(bk, o, o + k), A(me, 0, k), O.is_equal)
-            tt(A(y, 0, k), A(x, 0, k), A(lm, 0, k), O.mult)
-            ts(A(gl, 0, k), A(y, 0, k), float(G), O.add)
+        def flags(k, c0, c1):
+            ts(A("FL", 512 * c0, 512 * c1), A(WB[k], 512 * c0, 512 * c1), A("thc"), O.is_ge, 256.0, O.mult)
+            for c in range(c0, c1):
+                mm("ps%d" % c, 0, 512, "IDN", "FL", False, False, 512 * c)
 
-        if t == 0:
-            consts_c()
-        valid(b2, 0, "MEL", "RM", "GR", nc)
-        valid(b1, 0, "MEL", "LM", "GL", nc)
-        for k in range(4):
-            wi, wo = WB[k], WB[k + 1]
-            nchunk = n // 512
-            na = nchunk - NCH[t][k]
-            for x, c in [("R", c) for c in range(na)] + [(x, c) for c in range(na, nchunk) for x in "LR"]:
-                scopy(A("AB" if x == "R" else "AC", 512 * c, 512 * c + 512), IN(wi, 0, WW, "G" + x, 32 * c, 32 * c + 32))
+        def sflags(k, c0, c1):
+            x, y = A("M", 512 * c0, 512 * c1), A(WB[k], 512 * c0, 512 * c1)
+            call("S", lambda e: e.activation(mk(x), mk(y), F.Relu, bias=mk(A("bth")), scale=256.0), [x], [y, A("bth")])
+            for c in range(c0, c1):
+                mm("ps%d" % c, 0, 512, "IDN", "M", k == 0, False, 512 * c)
 
-            def xs(c0, c1):
-                if c0 < c1:
-                    tt(A("X", 512 * c0, 512 * c1), IN(wi, 0, WW, "GL", 32 * c0, 32 * c1), A("ED", 512 * c0, 512 * c1), O.max)
-            c0 = 0
+        def sign(out, in_, b):
+            call("S", lambda e: e.activation(mk(out), mk(in_), F.Sign, bias=mk(A(b))), [out], [in_, A(b)])
+
+        def outb(c):
+            scopy(A("OUTB", 512 * c, 512 * c + 512), IN(TAB, 0, P, "BL", 32 * c, 32 * c + 32))
+
+        def lists(j):
+            wlist("ps%d" % (5 + j), 0, "ZR", TAB, h, h * j)
+            wlist("ps%d" % (5 + j), 80, "ZL", TAB, h, h * j)
+
+        def take(bk, k, ll, rl, lm, rm):
+            copy(rl, A(bk, 0, k))
+            copy(ll, A(bk, 80, 80 + k))
+            ts(rm, rl, float(-G), O.add)
+            ts(lm, ll, float(-G), O.add)
+
+        def lists2(j):
+            take("ps%d" % (5 + j), hc, *[A(x, hc * j, hc * j + hc) for x in ("LL", "RL", "LM", "RM")])
+
+        def blist():
+            ts(A("BL", 0, nc), A("ps7", 0, nc), float(P - 1), O.min)
+            tt(A("ge", 0, nc), A("ps7", 0, nc), A("MEL", 0, nc), O.is_le)
+
+        def slists():
+            wlist("ps7", 0, "ZR", "OBS", 512)
+            wlist("ps7", 80, "ZL", "OBS", 512)
+
+        def slists2():
+            take("ps7", 32, A("SRAW", 0, 32), A("SRAW", 32, 64), A("SM", 0, 32), A("SM", 32, 64))
+
+        def outs():
+            scopy(A("OSS", 512, 1024), IN(TAB, 0, G, "SRAW", 32, 64))
+            copy(A("OSS", 0, 512), IN(TAB, 0, G, "SRAW", 0, 32))
+            wlist("ps7", 0, "ZB", "OSS", 1024)
+
+        def outlr(j):
+            c0, c1 = hc * j, hc * j + hc
+            m = 768 * j
+            scopy(A("OUTR", h * j, h * j + h), IN(TAB, 0, G, "RL", c0, c1))
+            copy(A("OUTL", h * j, h * j + h - m), IN(TAB, 0, G, "LL", c0, c1 - m // 16))
+            if m:
+                scopy(A("OUTL", n - m, n), IN(TAB, 0, G, "LL", nc - m // 16, nc))
+            wlist("ps%d" % (5 + j), 0, "ZB", "OUTR", h, h * j)
+            wlist("ps%d" % (5 + j), 80, "ZB", "OUTL", h, h * j)
+
+        def target():
+            for a in range(3):
+                tt(A("ps5", w * a, w * a + w), A("ps5", w * a, w * a + w), A(ME, 0, w), O.not_equal)
+            for a, x in enumerate(("da", "db", "dc")):
+                ts(A(x, 0, w), A("ps5", w * a, w * a + w), BIG, O.mult, float(WW * a), O.add)
+            tt(A("db", 0, w), A("db", 0, w), A("dc", 0, w), O.min)
+            tt(A("da", 0, w), A("da", 0, w), A("db", 0, w), O.min)
+            tt(A("da", 0, w), A(("PI", "ps6")[t], 0, w), A("da", 0, w), O.add)
+            hilo(A("TH", 0, w), A("TL", 0, w), A("da", 0, w))
+            rows2("Y", "d%d" % (10 + t), TAB, 0, n, 8, "TH", "TL", 0, w)
+
+        def valid(parts):
+            for bk, me, lm, tmp, gl in parts:
+                tt(bk, bk, me, O.is_equal)
+            for bk, me, lm, tmp, gl in parts:
+                tt(tmp, bk, lm, O.mult)
+            for bk, me, lm, tmp, gl in parts:
+                ts(gl, tmp, float(G), O.add)
+
+        def validlr(j):
+            c0, c1 = hc * j, hc * j + hc
+            valid([(A("ps%d" % (5 + j), o, o + hc), A("MEL", c0, c1), A(lm, c0, c1), A(tmp, c0, c1), A(gl, c0, c1))
+                   for o, lm, tmp, gl in ((0, "RM", "pa", "GR"), (80, "LM", "pb", "GL"))])
+
+        def valids():
+            valid([(A("ps7", o, o + 32), A("SNLf"), A("SM", o, o + 32), A("e1", o, o + 32), A("SG", o, o + 32)) for o in (32, 0)])
+
+        def border(k):
             if k == 0:
-                c0 = 1
-                xs(0, 1)
-                ts(A("SLM"), A(bs, 0, 32), float(-G), O.add)
-                ts(A("SRM"), A(bs, 32, 64), float(-G), O.add)
+                copy(A("AQ"), IN(WB[k], 0, WW, "SG", 32, 64))
+            for s in range(2):
+                tt(A(BB[k + 1], 256 * s, 256 * s + 256), IN(WB[k], 0, WW, "SG", 16 * s, 16 * s + 16), A("AQ", 256 * s, 256 * s + 256), O.max)
+            send(BB[k + 1], 0, 256, WB[k + 1], P, "ga%d%d" % (t, k + 1))
+
+        if t == 0:
+            wlist("ps0", 0, "ZB", SNDT, 512, 16)
+            copy(A("SNL"), A("ps0", 0, 32))
+            scopy(A(BB[0]), IN("E", 0, n, "SNL", 0, 32))
+            send(BB[0], 0, 256, "E", P, "ga00")
+            copy(A("SNLf"), A("ps0", 0, 32))
+            copy(A("OBS"), IN(TAB, 0, n, "SNL", 0, 32))
+            wlist("ps1", 0, "ZB", "OBS", 512)
+            slists()
+            lists(0)
+            lists(1)
+            consts_a()
+            slotcol("GO0", ("ps1", 0))
+            send("GO0", 0, 16, "GI0", 0, "gi0")
+            gfill("W2", V, P)
+            load("Y", "d15", "DR", 0, 2048, T["det"][:])
+            slin(A("DX"), A("DR"), 0.5, 127.8)
+            slin(A("DT", 0, 2048), A("DX"), 1.0, -256.0)
+            slists2()
+            tt(A("RSq"), A("SM", 32, 64), A("ILs"), O.is_equal)
+            tt(A("e2"), A("SM", 32, 64), A("SM", 0, 32), O.subtract)
+            copy(A("GOf"), A("GO0"))
+            tt(A("e2"), A("e2"), A("RSq"), O.mult)
+            ts(A("alt"), A("SM", 0, 32), float(G), O.add)
+            lists2(0)
+            tt(A("alt"), A("alt"), A("e2"), O.add)
+            lists2(1)
+            slotcol("GOd", ("alt", 0))
+            consts_n()
+            tt(A("GOd"), A("GOd"), A("GOf"), O.subtract)
+            consts_c()
+            ghost_bases(0)
+            outs()
+            outlr(0)
+            valids()
+            border(0)
+            gfill("W3", V, P)
+            outlr(1)
+        else:
+            scopy(A("OBS"), IN(TAB, 0, n, "SNL", 0, 32))
+            lists(0)
+            slists()
+            lists(1)
+            lists2(0)
+            copy(A("OUTL", 0, h), IN(TAB, 0, G, "LL", 0, hc))
+            scopy(A("OUTR", 0, h), IN(TAB, 0, G, "RL", 0, hc))
+            slists2()
+            outs()
+            wlist("ps5", 0, "ZB", "OUTR", h, 0)
+            wlist("ps5", 80, "ZB", "OUTL", h, 0)
+            lists2(1)
+            outlr(1)
+            valids()
+            border(0)
+        wlist("ps7", 0, "ZB", TAB, n)
+        validlr(0)
+
+        def right(k, c, f=scopy):
+            f(A("AB", 512 * c, 512 * c + 512), IN(WB[k], 0, WW, "GR", 32 * c, 32 * c + 32))
+
+        def left(k, c):
+            tt(A(WB[k + 1], 512 * c, 512 * c + 512), IN(WB[k], 0, WW, "GL", 32 * c, 32 * c + 32), A("AB", 512 * c, 512 * c + 512), O.max)
+
+        def alike():
+            tt(A("eq2", 0, 2 * w), A(PF, 0, 2 * w), A(PF, w, 3 * w), O.is_equal)
+            tt(A("eqb", 0, w), A(PF, 0, w), A(PF, 2 * w, 3 * w), O.is_equal)
+            tt(A("sg", 0, w), A(ME, 0, w), A(PF, 2 * w, 3 * w), O.is_lt)
+            ts(A("sg", 0, w), A("sg", 0, w), 2.0, O.mult, -1.0, O.add)
+
+        for k in range(3):
+            if k == 0:
                 if t == 0:
-                    tt(A("RSq"), A(bs, 32, 64), A("ILs"), O.is_equal)
-                valid(b3, 0, "SNLf", "SLM", "SL", 32)
-                valid(b3, 32, "SNLf", "SRM", "SR", 32)
-            if k < 3:
-                tt(A("M", 0, 512), IN(wi, 0, WW, "SL", 0, 32), A(BB[k]), O.max)
-                tt(A(BB[k + 1]), IN(wi, 0, WW, "SR", 0, 32), A("M", 0, 512), O.max)
-                send(BB[k + 1], 0, 256, WB[k + 1], P, "ga%d%d" % (t, k + 1))
-            xs(c0, na)
-            for c in range(nchunk):
-                lo, hi = 512 * c, 512 * c + 512
-                if c >= na:
-                    tt(A("X", lo, hi), A("ED", lo, hi), scal("AC", lo, hi), O.max)
-                tt(A(wo, lo, hi), A("X", lo, hi), scal("AB", lo, hi), O.max)
-                if k == 3 and hi <= hh:
-                    scopy(A("WD", lo, hi), A(wo, lo, hi))
+                    right(0, 0)
+                    right(0, 1)
+                    alike()
+                else:
+                    right(0, 0)
+                    right(0, 1)
+                left(0, 0)
+                validlr(1)
+                for a, z in enumerate(("ZR", "ZL", "ZB")):
+                    wnat("ps5", w * a, z, "OUTR", w)
+                if t == 0:
+                    wnat("ps6", 0, "ZR", "OBS", 32)
+                else:
+                    for a, z in enumerate(("ZR", "ZL", "ZB")):
+                        wnat("ps6", w * a, z, TAB, w)
+                for c in range(2, nchunk):
+                    right(0, c)
+                left(0, 1)
+                blist()
+            else:
+                for s in range(2):
+                    scopy(A("AQ", 256 * s, 256 * s + 256), IN(WB[k], 0, WW, "SG", 32 + 16 * s, 48 + 16 * s))
+                for c in range(nchunk):
+                    right(k, c)
+                if k == 2:
+                    flags(k, 0, 1)
+                border(k)
+                if k == 2:
+                    flags(k, 1, nchunk)
             if k == 1:
                 if t == 0:
-                    consts_d(0)
-                wlist("ps6", 0, "ZB", "OUTB", n)
-                if t == 0:
-                    for s in range(2):
-                        wrap("ps6", 160 + 16 * s, 16, "ZR", "OBS", lambda r: (256 * s + 16 * r, 256 * s + 16 * r + 16, 1))
+                    gfill("OUTL", V, P)
+                    tt(A("RSn"), A("ps6", 0, 32), A("IS"), O.is_equal)
+                target()
             if k == 2:
-                if t == 0:
-                    tt(A("RSn"), A("ps6", 160, 192), A("IS"), O.is_equal)
-                tt(A("pr", 0, nc), A("ps6", 0, nc), A("MEL", 0, nc), O.is_equal)
-                tt(A("pt", 0, nc), A("BLm", 0, nc), A("pr", 0, nc), O.mult)
-                ts(A("PB", 0, nc), A("pt", 0, nc), 2560.0, O.add)
-                tt(A("pa", 0, nc), A("MELm", 0, nc), A("BLm", 0, nc), O.is_lt)
-                tt(A("pa", 0, nc), A("pa", 0, nc), A("pr", 0, nc), O.mult)
-                ts(A("TH9", 0, nc), A("pa", 0, nc), -1000.0, O.mult, float(Q + 1000), O.add)
-            if k == 2 and t == 0:
-                consts_d(1)
-            if k < 3:
-                wnat("ps7", w * k, "ZR", ("OUTL", "OUTR", "OUTB")[k], w)
-            if k == 3:
-                for a in range(3):
-                    tt(A("F3", a * w, a * w + w), A("ps7", a * w, a * w + w), A("MEW", 0, w), O.is_equal)
-        scopy(A("AC", hh, n), IN("W4", 0, 2576, "PB", hh // 16, nc))
-        bm = bank()
-        tt(A("M", 0, hh), IN("W4", 0, 2576, "PB", 0, hh // 16), A("WD", 0, hh), O.max)
-        ts(A("FL", 0, hh), A("M", 0, hh), A("thc"), O.is_ge)
-        parts = [(lo, hi, scal("AC", lo, hi)) for lo, hi in ((hh, hh + 512), (hh + 512, n))]
-        wlist(bm, 0, "ZA", "FL", hh)
-        for lo, hi, ps in parts:
-            tt(A("M", lo, hi), A("W4", lo, hi), ps, O.max)
-            ts(A("FL", lo, hi), A("M", lo, hi), A("thc"), O.is_ge)
-        wlist(bm, hh // 16, "ZA", "FL", n - hh, hh)
-        tt(A("go", 0, nc), A(bm, 0, nc), A("TH9", 0, nc), O.is_ge)
-        b = bank()
-        b2 = bank()
-        mm(b, 0, nc, "BLK", "go")
-        mm(b2, 0, nc, "NLE", "go", True, False)
-        mm(b2, 0, nc, "N4K", "go", False, True)
-        call("V", lambda e: e.tensor_tensor_scan(mk(A("sc", 0, nc)), mk(A("ones", 0, nc)), mk(A(b, 0, nc)), 4096.0, O.mult, O.add), [A("sc", 0, nc)], [A("ones", 0, nc), A(b, 0, nc)])
-        tt(A("kk", 0, nc), A(b2, 0, nc), A("sc", 0, nc), O.add)
-        ts(A("c8", 0, nc), A("kk", 0, nc), 256.0, O.is_ge, 8192.0, O.mult)
-        tt(A("kk", 0, nc), A("kk", 0, nc), A("c8", 0, nc), O.add)
-        tt(A("c8", 0, nc), A("kk", 0, nc), A("D256", 0, nc), O.min)
+                gfill("W1", 0, n)
+                if t == 1:
+                    alike()
+                ts(A(CMP, 0, 256), A(TAB, n, n + 512, 2), A("c1"), O.add)
+            if k == 1:
+                if t == 1:
+                    scopy(A("PN"), A("ps6", 0, 480))
+                sflags(1, 0, nchunk)
+            if k == 0:
+                sflags(0, 0, nchunk)
+            for c in range(2 if k == 0 else 0, nchunk):
+                left(k, c)
+            if k == 2:
+                for c in range(nchunk):
+                    outb(c)
+        wlist("ps7", 0, "ZB", "OUTB", n)
+        rows2("Y", "d%d" % (12 + t), "OUTB", 0, n, 10, "TH", "TL", 0, w)
+        gfill("W2", 0, n)
+        hh = VPART[t]
+        for c in range(nchunk):
+            right(3, c)
+        flags(3, 0, nchunk - 1)
+        sflags(3, nchunk - 1, nchunk)
+
+        def hot(c):
+            lo, hi = 512 * c, 512 * c + 512
+            sign(A("H", lo, hi), A("ps%d" % c), "nth")
+            if lo < hh:
+                ts(A("M", lo, min(hi, hh)), A("ps%d" % c, 0, min(hi, hh) - lo), A("thc"), O.is_ge)
+
+        for c in range(nchunk):
+            left(3, c)
+            mm("ps%d" % c, 0, 512, "IDN", "W4", False, True, 512 * c)
+            if c == 1:
+                tt(A("ne", 0, nc), A("ps7", 0, nc), A("MEL", 0, nc), O.not_equal)
+                mm("ps5", 0, nc, "N4K", "ne", True, False)
+                mm("ps5", 0, nc, "N4K", "ge", False, False)
+        for c in range(nchunk):
+            hot(c)
+        parts = [(lo, min(lo + 512, n)) for lo in range(hh, n, 512)]
+        for lo, hi in parts:
+            scopy(A("AB", lo, hi), IN("H", 0, P, "BL", lo // 16, hi // 16))
+        for lo, hi in ((0, 1024), (1024, hh)):
+            tt(A("M", lo, hi), IN("H", 0, P, "BL", lo // 16, hi // 16), A("M", lo, hi), O.max)
+        for i, (lo, hi) in enumerate(parts):
+            mm("ps%d" % i, 0, hi - lo, "IDN", "H", True, False, lo)
+            mm("ps%d" % i, 0, hi - lo, "IDN", "AB", False, True, lo)
+            sign(A("M", lo, hi), A("ps%d" % i, 0, hi - lo), "one")
+        wlist("ps5", 0, "ZA", "M", 1024, 0, False, False)
+        wlist("ps5", 64, "ZA", "M", n - 1024, 1024, False, True)
+        slin(A("W3", 0, n), A("FL", 0, n), 0.0, 0.0)
+        slin(A("OS", 0, n), A("FL", 0, n), 0.0, -8.0)
+        ts(A("go", 0, hh // 16), A("ps5", 0, hh // 16), float(Q), O.is_ge)
+        ts(A("go", hh // 16, nc), A("ps5", hh // 16, nc), float(2 * Q - 16), O.is_ge)
+        mm("ps6", 0, nc, "BLK", "go")
+        mm("ps7", 0, nc, "NLE", "go", True, False)
+        mm("ps7", 0, nc, "N4K", "go", False, True)
+        call("V", lambda e: e.tensor_tensor_scan(mk(A("sc", 0, nc)), mk(A("ones", 0, nc)), mk(A("ps6", 0, nc)), 4096.0, O.mult, O.add), [A("sc", 0, nc)], [A("ones", 0, nc), A("ps6", 0, nc)])
+        tt(A("ps7", 0, nc), A("ps7", 0, nc), A("sc", 0, nc), O.add)
+        tt(A("c8", 0, nc), A("ps7", 0, nc), A("D1280", 0, nc), O.min)
         copy(A("TG", 0, nc), A("c8", 0, nc))
-        copy(IN(CMP, 0, 256 + n, "TG", 0, nc), A(TAB, 0, n))
-        b = bank()
-        wrap(b, 0, 32, "ZM", CMP, lambda r: (r >> 1, 256, 8), "ZB")
-        copy(A("TD"), A(b, 0, 32))
-        copy(IN(NEW, 0, G, "TD", 0, 32), A(MC))
-        copy(A("TF"), A(b, 0, 32))
-        bh = "ps7"
-
-        def errs():
-            scopy(A("ET"), IN("E", 0, P, "TD", 0, 32))
-            wlist(bh, 0, "ZH", "ET", 512)
-
-        if t == 1:
-            errs()
-        scopy(A("OT"), IN(TAB, 0, G, "TD", 0, 32))
-        scopy(A("ORT"), IN("OUTR", 0, P, "TD", 0, 32))
-        (copy, scopy)[t](A("NR", 0, 1024), IN(NEW, 0, G, "RL", 0, 64))
-        scopy(A("NR", 1024, n), IN(NEW, 0, G, "RL", 64, nc))
-        for lo, hi in ((0, 1024), (1024, n)):
-            copy(A("NB", lo, hi), IN(NEW, 0, G, "BL", lo // 16, hi // 16))
-            scopy(A("NL", lo, hi), IN(NEW, 0, G, "LL", lo // 16, hi // 16))
-        bn = bank()
-        wrap(bn, 0, 16, "ZM", CMP, lambda r: (16 * r, 16 * r + 16, 1))
-        wrap(bn, 16, 16, "ZB", CMP, lambda r: (16 * r, 16 * r + 16, 1))
-        bo = bank()
-        wnat(bo, 0, "ZB", NEW, w)
-        bR, bB, bL = bank(), bank(), bank()
-        wnat(bR, 0, "ZB", "NR", w)
-        wnat(bB, 0, "ZB", "NB", w)
-        wnat(bL, 0, "ZB", "NL", w)
-        scopy(A("ONT"), IN("NR", 0, P, "TD", 0, 32))
+        copy(IN(CMP, 0, 1280 + n, "TG", 0, nc), A("OUTB", 0, n))
+        wrap("ps0", 0, 32, "ZB", CMP, lambda r: (r >> 1, 256, 8), "ZM")
+        wrap("ps1", 0, 32, "ZU", CMP, lambda r: (r >> 1, 256, 8), "ZT")
+        copy(A("TD"), A("ps0", 0, 32))
+        copy(A("TF"), A("ps0", 0, 32))
+        scopy(A("ET"), IN("E", 0, P, "TD", 0, 32))
+        scopy(A("GT"), IN(TAB, 0, P, "TD", 0, 32))
         if t == 0:
-            scopy(A("ONS"), IN(NEW, 0, G, "SNL", 0, 32))
-            errs()
-        for x in range(2):
-            copy(A("TN", x, 32, 2), A(bn, 16 * x, 16 * x + 16))
-            copy(A("ON", 1 - x, 32, 2), A(bn, 16 * x, 16 * x + 16))
-        ts(A("nz", 0, w), A(bo, 0, w), 0.0, O.is_equal)
-        ts(A("zz", 0, w), A(bo, 0, w), 0.0, O.is_gt)
-        copy(A("nq", 0, w), A(bo, 0, w))
+            copy(IN("OS", 0, P, "TD", 0, 32), A(TAB, n, n + 512))
+        tt(A("e3"), A("ps1", 0, 32), A("DUM"), O.min)
+        copy(A("TR"), A("e3"))
+        wlist("ps4", 0, "ZH", "ET", 512)
+        if t == 0:
+            scopy(A("ONS"), IN("OS", 0, P, "SNL", 0, 32))
+            wnat("ps3", 0, "ZO", "OS", w)
+        copy(IN("RN", 0, DUMP + 512, "TR", 0, 32), A(TAB, n, n + 512))
+        if t == 1:
+            copy(IN("OS", 0, P, "TD", 0, 32), A(TAB, n, n + 512))
+        slin(A("E2"), A("ET"), 0.5, 127.8)
+        scopy(A("ONT"), IN("RN", 0, P, "TD", 0, 32))
+        wnat("ps5", 0, "ZM", "RN", w, 0)
+        if t == 0:
+            wlist("ps2", 0, "ZM", "ONS", 512)
+            wnat("ps2", 32, "ZM", "ONS", 32)
+        else:
+            wnat("ps3", 0, "ZO", "OS", w)
+        for a in (1, 2):
+            wnat("ps%d" % (5 + a), 0, "ZM", "RN", w, WW * a)
+        for a, z in enumerate(("ZM", "ZB", "ZR")):
+            if t == 1 or a == 2:
+                wnat("ps0", 32 * a, z, "GT", 32)
+        wnat("ps1", 0, "ZM", "ONT", 32)
 
-        def err0(t=t, n=n):
-            tt(A("hx", 0, 32), A(bh, 0, 32), A("TF"), O.add)
-            tt(A("hx", 32, 64), A(bh, 0, 32), A("OWL", 32 * t, 32 * t + 32), O.add)
+        def err0():
+            tt(A("hx", 0, 32), A("ps4", 0, 32), A("TF", 0, 32), O.add)
+            tt(A("hx", 32, 64), A("ps4", 0, 32), A("OWL", 32 * t, 32 * t + 32), O.add)
+            ts(A("em"), A("TF", 0, 32), float(n), O.is_ge, 2048.0, O.mult)
             ts(A("hy"), A("hx"), 2047, O.bitwise_and)
-            ts(A("em"), A("TF"), float(n), O.is_ge, 2048.0, O.mult)
             for x in range(2):
                 tt(A("hz", 32 * x, 32 * x + 32), A("hy", 32 * x, 32 * x + 32), A("em"), O.max)
             copy(A("HX"), A("hz"))
-            ts(A("E2"), A("ET"), 0.5, O.mult, 127.8, O.add)
-            tt(A("CL"), IN("DT", 0, 2064, "HX", 0, 32), A("E2"), O.add)
+            for x in range(2):
+                scopy(A("DG", 512 * x, 512 * x + 512), IN("DT", 0, 2064, "HX", 32 * x, 32 * x + 32))
 
-        def err1(n=n):
-            tt(A("E", n, n + 512), IN("DT", 0, 2064, "HX", 32, 64), A("E2"), O.add)
+        def err1(out):
+            mm("ps4", 0, 512, "IDN", "E2", True, False)
+            mm("ps4", 0, 512, "IDN", "DG", False, True, 512)
+            scopy(out, A("ps4"))
 
         def err2():
-            copy(IN("E", 0, P, "TD", 0, 32), A("CL"))
+            tt(IN("E", 0, P, "TD", 0, 32), A("DG", 0, 512), A("E2"), O.add)
 
-        def err3():
-            dma("Y", "d25", T["ED"][:], T["E"][:, 0:2560], [("E", 0, 2560, None)], [("ED", 0, 2560, None)])
-
-        late = [err0, err2, err1, err3]
-        if t == 1:
-            err0()
-            err2()
-            err1()
-            dma("Y", "d30", T["ye"][:], T["E"][:, 0:P], [("E", 0, P, None)], [])
-        PN = "PF%d" % (t + 1)
-        wn = w + 32
-        q = [A("q3", a * w, a * w + w) for a in range(3)]
-        pn = [A(PN, a * wn, a * wn + w) for a in range(3)]
-        nw = [A(PN, a * wn + w, a * wn + wn) for a in range(3)]
-        own = A("OWN", 32 * t, 32 * t + 32)
-        tt(q[1], A(bR, 0, w), A("F3", w, 2 * w), O.mult)
-        tt(q[2], A(bB, 0, w), A("F3", 2 * w, 3 * w), O.mult)
-        tt(A("pz", 0, w), A(bB, 0, w), A("zz", 0, w), O.mult)
-        tt(q[0], A(bL, 0, w), A("F3", 0, w), O.mult)
-        tt(A("q3", 0, 3 * w), A("q3", 0, 3 * w), A(PF), O.max)
-        tt(A("zz", 0, w), A("zz", 0, w), q[0], O.mult)
-        for a in range(3):
-            tt(pn[a], q[a], A("nz", 0, w), O.mult)
-        for a, x in ((0, "nq"), (1, "pz"), (2, "zz")):
-            tt(pn[a], pn[a], A(x, 0, w), O.add)
-        bq = bank()
-        wrap(bq, 0, 32, "ZR", "OT", lambda r: (32 * r, 32 * r + 32, 1))
-        wrap(bq, 32, 32, "ZR", "ORT", lambda r: (32 * r, 32 * r + 32, 1))
-        wrap(bq, 64, 32, "ZB", "ONT", lambda r: (32 * r, 32 * r + 32, 1))
-        copy(nw[1], A("TN"))
-        ts(A("e2"), A("TN"), float(n), O.is_ge)
-        tt(A("e3"), own, A("ON"), O.subtract)
-        tt(A("e3"), A("e3"), A("e2"), O.mult)
-        tt(nw[0], A("ON"), A("e3"), O.add)
-        tt(A("e1"), A(bq, 32, 64), A("TN"), O.is_equal)
-        tt(A("e1"), A(bq, 64, 96), A("e1"), O.mult)
-        tt(nw[2], A(bq, 0, 32), A("e1"), O.max)
-        if t == 1:
-            for a, y in enumerate(("yl", "yr", "yb")):
-                for lo, hi, c0, c1 in ((0, V, 0, 128), (V, V + 512, 128, 160), (V + 512, P, 160, 192)):
-                    dma("YSY"[a], "d31", T[y][:, lo:hi], T[PN][:, a * wn + c0:a * wn + c1], [(PN, a * wn, a * wn + wn, None)], [])
-            break
-        copy(A("HI1"), A(PN))
-        tt(A("LO1"), A(PN), A("HI1"), O.subtract)
-        for a, i in ((2, 0), (1, 2), (0, 4)):
-            for hl, x in enumerate(("HI1", "LO1")):
-                rows("YS"[hl], "d20", "TAB1", 0, V, i + hl, x, a * wn, a * wn + w)
-                rows("YS"[hl], "d20", "TAB1", V, V + 512, i + hl, x, a * wn + w, a * wn + wn)
-        bs = bank()
-        wlist(bs, 0, "ZB", "ONS", 512)
-        tt(A("sq"), A(bs, 0, 32), A("RSq"), O.mult)
-        tt(A("SNLf"), A("SNLf"), A("sq"), O.max)
-        copy(A("SNL"), A("SNLf"))
-        for s in range(2):
-            wrap("ps6", 16 * s, 16, "ZB", "ONS", lambda r: (256 * s + 16 * r, 256 * s + 16 * r + 16, 1))
-
-        def snd_rows():
-            tt(A("sq"), A("ps6", 0, 32), A("RSn"), O.mult)
+        def entries():
+            ts(A("sp"), A("ps2", 0, 32), 0.0, O.is_gt)
+            tt(A("sq"), A("ps2", 0, 32), A("RSq"), O.mult)
+            tt(A("sp"), A("sp"), A("GOd"), O.mult)
+            tt(A("SNLf"), A("SNLf"), A("sq"), O.max)
+            tt(A("sp"), A("sp"), A("GOf"), O.add)
+            tt(A("sq"), A("ps2", 32, 64), A("RSn"), O.mult)
+            copy(A("GO1"), A("sp"))
+            send("GO1", 0, 16, "GI1", 0, "gi1")
+            for i, j in ((2, 6), (3, 7), (4, 0), (5, 1)):
+                dma("G", "d21", T[TAB][i::16, V:V + 512], T["GT"][j::16, 0:512], [("GT", 0, 512, j)], [(TAB, V, V + 512, i)])
             tt(A("SN1"), A("sq"), A("SNI"), O.max)
-            copy(A("SH1"), A("SN1"))
-            tt(A("SL1"), A("SN1"), A("SH1"), O.subtract)
-            for s in range(2):
-                rows("Y", "d24", "SNDT1", 16 + 288 * s, 272 + 288 * s, 0, "SH1", 16 * s, 16 * s + 16)
-                rows("Y", "d24", "SNDT1", 16 + 288 * s, 272 + 288 * s, 1, "SL1", 16 * s, 16 * s + 16)
-        late.append(snd_rows)
+            copy(A("SNL"), A("SNLf"))
+            hilo(A("SH1"), A("SL1"), A("SN1"))
+            rows2("Y", "d24", SNDT, 16, 528, 0, "SH1", "SL1", 0, 32)
+
+        err0()
+        scopy(A("nw", 64 - 64 * t, 96), A("ps0", 64 - 64 * t, 96))
+        if t == 1:
+            err2()
+            dma("Y", "d30", T["ye"][:, 0:n], T["E"][:, 0:n], [("E", 0, n, None)], [])
+            err1(A("CR"))
+            dma("S", "d30", T["ye"][:, n:P], T["CR"][:], [("CR", 0, 512, None)], [])
+        pf = [A(PF, w * a, w * a + w) for a in range(3)]
+        px = [A("PX", w * a, w * a + w) for a in range(3)]
+        ps = [A("ps%d" % (5 + a), 0, w) for a in range(3)]
+
+        def finish(a):
+            ts(px[a], px[a], 4095, O.bitwise_and)
+            if a == 2:
+                tt(A("nw", 64, 96), A("ps1", 0, 32), A("nw", 64, 96), O.max)
+            if t == 0:
+                hilo(A("HI", w * a, w * a + w), A("LO", w * a, w * a + w), px[a])
+                rows2("YS", "d20", TAB, 0, V, (2, 4, 0)[a], "HI", "LO", a * w, a * w + w)
+                if a == 2:
+                    hilo(A("SH"), A("SL_"), A("nw", 64, 96))
+                    rows2("YS", "d20", TAB, V, V + 512, 0, "SH", "SL_", 0, 32)
+                return
+            y = ("yr", "yl", "yb")[a]
+            copy(A("PO", w * a, w * a + w), px[a])
+            b, o = loc("nw")
+            dma("S", "d31", T[y][:, n:P], T[b][:, o + 32 * a:o + 32 * a + 32], [("nw", 32 * a, 32 * a + 32, None)], [])
+            dma("Y", "d31", T[y][:, 0:n], T["PO"][:, a * w:a * w + w], [("PO", a * w, a * w + w, None)], [])
+
+        tt(A("OV", 0, w), A("ps3", 0, w), A("sg", 0, w), O.add)
+        copy(A("OV", w, 2 * w), A("ps3", 0, w))
+        tt(A("OV", 0, w), A("OV", 0, w), pf[0], O.max)
+        tt(A("da", 0, w), ps[0], A("eq2", 0, w), O.mult)
+        tt(A("db", 0, w), ps[0], A("eqb", 0, w), O.mult)
+        tt(px[0], ps[0], A("OV", 0, w), O.max)
+        tt(A("da", 0, w), A("da", 0, w), pf[1], O.max)
+        tt(A("db", 0, w), A("db", 0, w), pf[2], O.max)
+        if t == 0:
+            entries()
+        finish(0)
+        tt(A("dc", 0, w), ps[1], A("eq2", w, 2 * w), O.mult)
+        tt(ps[1], ps[1], A("da", 0, w), O.max)
+        tt(A("db", 0, w), A("db", 0, w), A("dc", 0, w), O.max)
+        ts(A("ql", 0, w), ps[1], 4096.0, O.add)
+        tt(px[1], ps[1], A("OV", w, 2 * w), O.max)
+        tt(A("dc", 0, w), A("ps3", 0, w), A("ql", 0, w), O.min)
+        tt(ps[2], ps[2], A("db", 0, w), O.max)
+        tt(px[2], ps[2], A("dc", 0, w), O.max)
+        finish(1)
+        finish(2)
+        if t == 0:
+            err2()
+            err1(A("E", V, V + 512))
+            scopy(A("BB10"), IN("E", 0, P, "SNL", 0, 32))
+            send("BB10", 0, 256, "E", P, "ga10")
+            ghost_bases(1)
     for d in sorted(dcount):
         wait("Y", (d, dcount[d], {}))
     for q in ("V", "S", "P", "G"):

@@ -1,13 +1,14 @@
 from concourse.bass import DstId, RemoteDMATransfer
 from concourse.mybir import AluOpType as O, ActivationFunctionType as F
 
-V, P, G, Q = 2048, 3072, 3584, 9
-WW = G + 16
-ZW = 143
-DUMP = 3 * WW
+V, P, G = 2048, 3072, 3584
+GH, PL, K, DW = 16, 528, 3104, 3120
 BIG = 16384.0
+JUMP = 4096.0 * 254
 bf, f4, i4, u2 = "bfloat16", "float32", "int32", "uint16"
 VPART = (1280, 1536)
+LB, RB, LM, RM, BM, BB = 0, 32, 64, 192, 320, 448
+LN = 320
 
 
 def _s(n, d):
@@ -21,13 +22,16 @@ WIDTH = {}
 
 def _tiles():
     tiles = {
-        i4: "IP 1 IG 1 II 1 IJ 1 IO 1 IM 128 IM2 32 SNI 32 THI 1 WTI 1 MEN 128 hx 64 hy 64",
-        f4: "IXX 143 IL 160 IK 128 ILs 32 IS 32 IB 12 pc 1 gc 1 jc 6 jj 1 ev 1 odf 1 one 1 nth 1 bth 1 ZF 143 MEL 160 D1280 160 MEW 160 OWL 64 mA 128 mB 128 mE 128 mD 128 wtc 1 "
-            "SN1 32 SNLf 32 LM 160 RM 160 SM 64 RSq 32 RSn 32 pa 160 pb 160 ones 160 sc 160 c8 160 "
-            "TF 32 em 32 hz 64 DUM 32 e1 64 e2 32 e3 32 sq 32 GOf 32 GOd 32 alt 32 sp 32 sg 160 ql 160 da 160 db 160 dc 160 eq2 320 eqb 160 nw 96",
-        bf: "ZA 143 ZB 143 ZR 143 ZL 143 ZM 143 ZO 143 ZT 143 ZU 143 TH 160 TL 160 ZH 143 BLK 128 NLE 128 IDN 128 N4K 128 SH 32 SL_ 32 SH1 32 SL1 32 go 160 ne 160 ge 160 "
-            "thc 1 od 1 c1 1 HB 12 LOW 256",
-        u2: "SNL 32 BL 160 LL 160 RL 160 GL 160 GR 160 SRAW 64 SG 64 TG 160 TD 32 HX 64 TR 32",
+        i4: "IP 1 IG 1 II 1 IO 1 SNI 32 THI 1 WTI 1 hx 64 hy 64",
+        f4: "pc 1 px 1 qf 1 g15 1 odf 1 one 1 bth 1 wtc 1 th2 1 OH 16 PS 8 ca 1 cb 1 s1 1 s2 1 ev 1 B16 16 BN 4 BC 2 wc 8 lowb 1 "
+            "IL 160 PHU 128 DUMPC 10 N2K 32 KL 16 KH 32 OWL 64 ILs 32 IS 32 UN 32 IDF 128 mA 128 mB 128 ones 160 sc 176 "
+            "NKU 320 CT 320 plc 320 isg 320 kg 320 UT 480 lo 320 tA 480 tB 480 UB 448 mBB 128 sg 160 sgb 160 ne 160 pre 160 sA 128 nLR 128 nLB 128 lo2 128 eRB 128 "
+            "RSq 32 RSn 32 GOf 32 GOd 32 alt 32 e2 32 PHS 32 sp 32 sq 32 SN1 32 UB2 320 LO2 320 vn 160 vs 160 N3 384 U2 384 pa 128 pb 128 "
+            "X2 480 UR2 480 U160 160 SG2 160 XF 480 UF 480 UL 160 PO 480 nw 96 TF 32 em 32 hz 64 yo 32 yk 16 z0 160 x0 160 v0 160 of 10",
+        bf: "ZA 143 ZR 143 ZL 143 ZB 143 ZO 143 ZP 143 ZV 143 ZW 143 ZN 143 ZC 143 ZF 143 ZG 143 ZE 143 ZX 143 ZQ 143 ZH 143 "
+            "BLK 128 TRI 128 ID2 128 IDN 128 N4K 128 BTH 128 SH 32 SL_ 32 SH1 32 SL1 32 go 160 nm 160 a0 160 val 160 thc 1 LOW 256 "
+            "UR 480 ye_ 32 cand 160 f2 128 GH_ 128 GL_ 128 U2R 128",
+        u2: "SNL 32 RAW 480 RAW2 480 GL 352 BL 160 TD 32 T0 16 TP 32 TR 32 HX 64 OFF 10 SP2 32",
     }
     for d, names in tiles.items():
         w = names.split()
@@ -38,11 +42,10 @@ def _tiles():
             o += (int(n) + 15) // 16 * 16
         SCRATCH["pk" + d] = _s(o, d)
     big = {
-        i4: "PI 384 PX 480",
-        f4: "OV 480 PO 480 PN 480",
-        bf: "HI 384 LO 384 TAB 3584 SNDT 544 E 3600 WALL 13360 M 2560 FL 2560 AB 2560 AQ 512 "
-            "OUTL 3072 OUTR 2560 OUTB 2560 OBS 512 OSS 1024 ONS 512 CMP 3840 "
-            "DR 2048 DX 2048 DT 2064 DG 1024 ET 512 E2 512 CR 512 GT 512 ONT 512 " + " ".join("BB%d%d 512" % (t, k) for t in range(2) for k in range(4)),
+        i4: "XP 480",
+        bf: "HI 384 LO 384 TAB 3584 CG 512 SNDT 544 SND2 544 E 3072 D0 3120 D1 3120 D2 3120 D3 3120 D4 2560 M 2560 H 2560 FL 2560 FS 2560 AB 2560 AQ 512 "
+            "OUTL 2560 OUTR 2560 OUTB 2560 OBS 512 OSS 1024 ONS 512 OS0 3584 OS1 3584 ONE 512 CW0 416 CW1 416 VW0 416 VW1 416 CF 256 MM 256 "
+            "DR 2064 DG 1024 ET 512 E1 512 E2 512 CR 512 GT 512 G0 256 ONT 512 " + " ".join("BB%d%d 512" % (t, k) for t in range(2) for k in range(4)),
         u2: "GO0 32 GO1 32 GI0 32 GI1 32",
     }
     for d, names in big.items():
@@ -50,10 +53,6 @@ def _tiles():
         for k, n in zip(w[0::2], w[1::2]):
             WIDTH[k] = int(n)
             SCRATCH[k] = _s(int(n), d)
-    for k, b, o, n in [("W%d" % k, "WALL", WW * (k - 1), WW if k < 4 else 2560) for k in (1, 2, 3, 4)] + [
-            ("RN", "WALL", 0, DUMP + 512), ("H", "OUTL", 0, P), ("OS", "OUTL", 0, P)]:
-        PACK[k] = (b, o)
-        WIDTH[k] = n
     for k in range(8):
         WIDTH["ps%d" % k] = 512
         SCRATCH["ps%d" % k] = ("psum", [128, 512], f4)
@@ -90,12 +89,12 @@ def rank_program(g, core, T, topo):
         toks = []
         for kind, regs in (("r", reads), ("w", writes)):
             for b, lo, hi, row in regs:
-                ps = b.startswith("ps")
                 for rlo, rhi, rrow, rk, rq, tok in hist.get(b, []):
-                    if rlo >= hi or lo >= rhi or (row is not None and rrow is not None and row != rrow):
-                        continue
-                    if rk == "r" and kind == "r" and not (ps and rq != q):
-                        continue
+                    if not (b.startswith("ps") and rq != q):
+                        if rlo >= hi or lo >= rhi or (row is not None and rrow is not None and row != rrow):
+                            continue
+                        if rk == "r" and kind == "r":
+                            continue
                     if rq == q and q == "P" and kind == "w":
                         continue
                     toks.append(tok)
@@ -119,6 +118,9 @@ def rank_program(g, core, T, topo):
             lo, hi = 0, WIDTH[b]
         return ("a", b, lo, hi, st)
 
+    def W(b, lo, n):
+        return ("a", b, lo, lo + n, 1)
+
     def IN(b, lo, hi, ob, c0, c1):
         return ("i", b, lo, hi, ob, c0, c1)
 
@@ -137,7 +139,8 @@ def rank_program(g, core, T, topo):
         if not isinstance(x, tuple):
             return []
         b, o = loc(x[1])
-        return [(b, 0, 512, None) if b.startswith("ps") else (b, o + x[2], o + x[3], None)]
+        step = x[0] == "a" and x[4] == 16 and ("step", (o + x[2]) % 16)
+        return [(b, o + x[2], o + x[3], step or None)]
 
     def offs(x):
         if isinstance(x, tuple) and x[0] == "i":
@@ -162,8 +165,8 @@ def rank_program(g, core, T, topo):
     def scopy(out, in_, f=F.Copy):
         call("S", lambda e: e.activation(mk(out), mk(in_), f), [out], [in_])
 
-    def slin(out, in_, scale, bias):
-        call("S", lambda e: e.activation(mk(out), mk(in_), F.Identity, bias=bias, scale=scale), [out], [in_])
+    def slin(out, in_, scale, bias, f=F.Identity):
+        call("S", lambda e: e.activation(mk(out), mk(in_), f, bias=mk(bias), scale=mk(scale)), [out], [in_, scale, bias])
 
     def fill(out, c):
         call("V", lambda e: e.memset(mk(out), c), [out], [])
@@ -176,6 +179,9 @@ def rank_program(g, core, T, topo):
             call("V", lambda e: e.tensor_scalar(mk(out), mk(a), mk(s1), None, op0), [out], [a, s1])
         else:
             call("V", lambda e: e.tensor_scalar(mk(out), mk(a), mk(s1), mk(s2), op0, op1), [out], [a, s1, s2])
+
+    def scan(out, d0, d1, init, op0, op1):
+        call("V", lambda e: e.tensor_tensor_scan(mk(out), mk(d0), mk(d1), init, op0, op1), [out], [d0, d1])
 
     def hilo(hi, lo, x):
         copy(hi, x)
@@ -209,6 +215,10 @@ def rank_program(g, core, T, topo):
         bb, o = loc(b)
         dma(q, bat, T[bb][:, o + lo:o + hi], src, [], [(b, lo, hi, None)])
 
+    def store(q, bat, dst, b, lo, hi):
+        bb, o = loc(b)
+        dma(q, bat, dst, T[bb][:, o + lo:o + hi], [(b, lo, hi, None)], [])
+
     def gfill(b, lo, hi):
         iota(A(b, lo, hi), [[0, hi - lo]], 0, 0, True)
 
@@ -225,7 +235,7 @@ def rank_program(g, core, T, topo):
                 rhs = T[sb][:, so + a:so + b] if st == 1 else T[sb][:, so + a:so + b:st]
                 i = e.matmul(T[bk][:, o:o + n], T[zb][:, zo + 15 - r:zo + 143 - r], rhs, first and r == 0, last and r == 15)
             return i
-        call("P", f, [A(bk)], [A(src, lo, hi)] + [A(x) for x in sorted(set(zs))])
+        call("P", f, [W(bk, o, n)], [A(src, lo, hi)] + [A(x) for x in sorted(set(zs))])
 
     def wlist(bk, o, z, src, n, lo=0, first=True, last=True):
         wrap(bk, o, n // 16, z, src, lambda r: (lo + r, lo + n, 16), first=first, last=last)
@@ -236,15 +246,25 @@ def rank_program(g, core, T, topo):
     def mm(bk, o, n, z, src, start=True, stop=True, s0=0):
         zb, zo = loc(z)
         sb, so = loc(src)
-        call("P", lambda e: e.matmul(T[bk][:, o:o + n], T[zb][:, zo:zo + 128], T[sb][:, so + s0:so + s0 + n], start, stop), [A(bk)], [A(z, 0, 128), A(src, s0, s0 + n)])
+        call("P", lambda e: e.matmul(T[bk][:, o:o + n], T[zb][:, zo:zo + 128], T[sb][:, so + s0:so + s0 + n], start, stop), [W(bk, o, n)], [A(z, 0, 128), A(src, s0, s0 + n)])
+
+    def unmix(src, c0, c1, banks, stop=False):
+        zb, zo = loc("ID2")
+
+        def f(e):
+            for b in banks:
+                for r in range(4 * b, 4 * b + 4):
+                    o = 128 * (r % 4)
+                    i = e.matmul(T["ps%d" % b][:, o + c0:o + c1], T[zb][:, zo:zo + 128], T[src][:, 16 * c0 + r:16 * c1:16], False, stop and r % 4 == 3)
+            return i
+        call("P", f, [A("ps%d" % b) for b in banks], [A(src, 16 * c0, 16 * c1), A("ID2")])
 
     nb = [T.cores[(rank - 1) % 4], T.cores[(rank + 1) % 4]]
     lsum = [0]
+    half = len(topo.engines(core, nb[0])) // 2
 
-    def send(src, s0, w, dst, d0, sem):
+    def send(src, w, dst, d0, sem):
         tr = []
-        dst, do = loc(dst)
-        d0 += do
         for s in range(2):
             e = topo.engines(core, nb[s])
             h = len(e) // 2
@@ -252,509 +272,710 @@ def rank_program(g, core, T, topo):
             rid, pid, _ = topo.addr(nb[s])
             lsum[0] += h
             tr.append(RemoteDMATransfer(dst_ids=[DstId(rid=rid, pnc=pid)], dma_engine_mask=m, remote_sem=T.sem[sem],
-                                        src=T[src][:, s0 + w * s:s0 + w * s + w], dst=T[dst][:, d0 + w * (1 - s):d0 + w * (1 - s) + w]))
-        deps("G", [(src, s0, s0 + 2 * w, None)], [])
+                                        src=T[src][:, w * s:w * s + w], dst=T[dst][:, d0 + w * (1 - s):d0 + w * (1 - s) + w]))
+        deps("G", [(src, 0, 2 * w, None)], [])
         g.remote_dma_fused(tr, local_sem=T.sem.sX)
         note("X", [], [(dst, d0, d0 + 2 * w, None)], (sem, 2 * h, dict(seen["G"])))
 
-    TAB, SNDT, CMP = "TAB", "SNDT", "CMP"
+    TAB, SNDT = "TAB", "SNDT"
+    OH = lambda j: W("OH", j, 1)
+    PS = lambda j: W("PS", j, 1)
+    LOW = lambda n: A("LOW", 0, n)
+
+    def both(out, o, win, hi, lst, c0, c1, cv):
+        if c1 > cv:
+            scopy(A(out, o + 16 * (cv - c0), o + 16 * (c1 - c0)), IN(win, 0, hi, lst, cv, c1))
+        if cv > c0:
+            copy(A(out, o, o + 16 * (cv - c0)), IN(win, 0, hi, lst, c0, cv))
+
+    def weights(z, col, q="V"):
+        if q == "V":
+            ts(A(z), A("ZA"), col, O.mult)
+        else:
+            slin(A(z), A("ZA"), col, 0.0)
 
     load("Y", "d1", "SNI", 0, 32, T.snd[:])
-    load("S", "d0", "PI", 256, 384, T.bs[:])
-    load("Y", "d2", "PI", 0, 128, T.rt[:])
-    load("S", "d3", "PI", 128, 256, T.lt[:])
-    load("Y", "d6", "E", 0, V, T["err"][:])
+    load("S", "d0", "XP", BM, BM + 128, T.bs[:])
+    load("Y", "d2", "XP", RM, RM + 128, T.rt[:])
+    load("S", "d2", "XP", LM, LM + 128, T.lt[:])
     iota(A("IP"), [[0, 1]], 1)
-    iota(A("IB"), [[256, 12]], 0, 0, True)
     iota(A("LOW"), [[1, 256]], 0, 0, True)
-    iota(A("IXX"), [[1, ZW]], 0, -15, True)
-    iota(A("IL"), [[16, 160]], 1, 0, True)
-    iota(A("IK"), [[1, 128]], 0, 0, True)
-    iota(A("IM"), [[1, 128]], 128)
-    iota(A("IM2"), [[1, 32]], 32)
-    iota(A("ILs"), [[256, 2], [16, 16]], 1, P - G, True)
-    iota(A("MEW"), [[1, 160]], 160, 0, True)
-    gfill("E", V, P)
-    fill(A(SNDT), -1.0)
-    ts(A("IO"), A("IP"), 1, O.bitwise_and)
+    fill(A(SNDT), -2.0)
     ts(A("II"), A("IP"), 15, O.bitwise_and)
     ts(A("IG"), A("IP"), 112, O.bitwise_and)
-    copy(A("odf"), A("IO"))
-    ts(A("ev"), A("IO"), -1.0, O.mult, 1.0, O.add)
-    ts(A("IJ"), A("II"), 1, O.arith_shift_right)
-    ts(A("HB"), A("IB"), A("ev"), O.mult)
-    copy(A("gc"), A("IG"))
-    copy(A("jj"), A("IJ"))
-
-    def own(b0, b1):
-        for b in range(b0, b1):
-            x, y = A(TAB, 256 * b, 256 * b + 256), A("HB", b, b + 1)
-            call("S", lambda e: e.activation(mk(x), mk(A("LOW")), F.Identity, bias=mk(y), scale=mk(A("odf"))), [x], [y, A("LOW"), A("odf")])
-    own(0, 8)
-    ts(A("ZF"), A("IXX"), A("gc"), O.is_equal)
-
-    def pick(j):
-        ts(A("jc", j, j + 1), A("jj"), float(j), O.is_equal)
-        ts(A(("ZB", "ZR", "ZL", "ZM", "ZT", "ZU")[j]), A("ZF"), A("jc", j, j + 1), O.mult)
+    copy(A("qf"), A("II"))
+    ts(A("g15"), A("IG"), 15.0, O.add)
+    ts(A("OH"), LOW(16), A("qf"), O.is_equal)
+    ts(A("ZA"), LOW(143), A("g15"), O.is_equal)
+    ts(A("ca"), OH(6), 128.0, O.mult, OH(9), O.add)
+    ts(A("cb"), OH(8), float(PL), O.mult)
+    ts(A("s1"), OH(8), 16.0, O.mult, OH(7), O.add)
+    tt(A("PS"), A("OH", 0, 16, 2), A("OH", 1, 16, 2), O.add)
+    ts(A("B16"), LOW(16), A("ca"), O.mult, A("cb"), O.add)
+    for r in range(16):
+        slin(W(TAB, 128 * r, 128), LOW(128), A("s1"), W("B16", r, 1))
     hilo(A("SH"), A("SL_"), A("SNI"))
-    rows2("SY", "d5", SNDT, 16, 528, 0, "SH", "SL_", 0, 32)
-    for a in (2, 0, 1):
-        hilo(A("HI", 128 * a, 128 * a + 128), A("LO", 128 * a, 128 * a + 128), A("PI", 128 * a, 128 * a + 128))
-        rows2("SY", "d4", TAB, 0, V, (2, 4, 0)[a], "HI", "LO", 128 * a, 128 * a + 128)
-    load("Y", "d9", "THI", 0, 1, T["th"][:])
-    load("Y", "d9", "WTI", 0, 1, T["wt"][:])
-    pick(0)
-    pick(1)
-    pick(2)
-    own(8, 12)
-    ts(A("MEN"), A("IM"), 2047, O.bitwise_and)
+    rows2("Y", "d5", SNDT, 16, 528, 4, "SH", "SL_", 0, 32)
+    weights("ZB", PS(2))
+    hilo(W("HI", 256, 128), W("LO", 256, 128), W("XP", BM, 128))
+    rows2("Y", "d4", TAB, 0, V, 4, "HI", "LO", 256, 384)
+    load("Y", "d6", "E", 0, V, T["err"][:])
+    ts(A("IO"), A("IP"), 1, O.bitwise_and)
+    ts(A("s2"), A("II"), 10.0, O.is_lt)
+    copy(A("odf"), A("IO"))
+    ts(A("ca"), A("qf"), 128.0, O.mult)
+    for o in (LM, RM, BM):
+        slin(W("UT", o, 128), LOW(128), 1.0, A("ca"))
+    slin(A("IL"), LOW(160), 16.0, A("qf"))
+    ts(A("ev"), A("odf"), -1.0, O.mult, A("s2"), O.add)
+    tt(A("s2"), A("s2"), A("odf"), O.mult)
+    ts(A("BN"), LOW(4), 256.0, O.mult, float(V), O.add)
+    ts(A("ev"), A("ev"), 0.0, O.max)
+    ts(A("BC"), LOW(2), 256.0, O.mult, GH + 4.0, O.add)
+    ts(A("BN"), A("BN"), A("ev"), O.mult, A("cb"), O.add)
+    ts(A("BC"), A("BC"), OH(8), O.mult)
     copy(A("pc"), A("IP"))
-    ts(A("MEL"), A("IL"), A("gc"), O.subtract)
-    ts(A("IDN"), A("IK"), A("pc"), O.is_equal)
-    ts(A("ILs"), A("ILs"), A("gc"), O.subtract)
-    for b in ("E", "W1", "W2", "W3"):
-        fill(A(b, G, WW), 0.0)
-    fill(A("W1", V, P), 0.0)
-    fill(A("DT", 2048, 2064), -128.0)
-
-    def consts_a():
-        for j in (3, 4, 5):
-            pick(j)
-        ts(A("ev"), A("jj"), 7.0, O.is_equal, 4096.0, O.mult)
-        ts(A("c1"), A("II"), 7.0, O.is_equal)
-        ts(A("od"), A("II"), 8.0, O.is_ge, BIG, O.mult)
-        tt(A("ev"), A("ev"), A("jc", 3, 4), O.add)
-        copy(A("ZA"), A("ZF"))
-        tt(A("c1"), A("c1"), A("od"), O.add)
-        ts(A("jj"), A("gc"), 160.0, O.mult)
-        ts(A("ZO"), A("ZF"), A("ev"), O.mult)
-        ts(A("MEW"), A("MEW"), A("jj"), O.subtract)
-        ts(A("N4K"), A("IK"), A("pc"), O.is_equal, -4096.0, O.mult)
-
-    def consts_n():
-        ts(A("mD"), A("IK"), A("gc"), O.subtract)
-        ts(A("mE"), A("IK"), A("pc"), O.is_gt)
-        ts(A("mA"), A("mD"), 0.0, O.is_ge)
-        ts(A("mB"), A("mD"), 16.0, O.is_ge)
-        ts(A("D1280"), A("MEL"), 1280.0, O.add)
-        tt(A("BLK"), A("mA"), A("mB"), O.subtract)
-        tt(A("NLE"), A("mE"), A("mA"), O.subtract)
-        fill(A("ones"), 1.0)
-        fill(A("one"), 1.0)
-
-    def consts_c():
-        copy(A("wtc"), A("WTI"))
-        copy(A("thc"), A("THI"))
-        for t in range(2):
-            ts(A("OWL", 32 * t, 32 * t + 32), A("MEL", 0, 32), float(V + 512 * t), O.add)
-        ts(A("IM2"), A("IM2"), 511, O.bitwise_and)
-        ts(A("DUM"), A("MEL", 0, 32), float(DUMP), O.add)
-        ts(A("ZH"), A("ZF"), A("wtc"), O.mult)
-        ts(A("IS"), A("IM2"), float(P), O.add)
-        ts(A("nth"), A("THI"), -1.0, O.mult, 0.5, O.add)
-        ts(A("bth"), A("THI"), -256.0, O.mult, 256.0, O.add)
+    weights("ZP", PS(4), "S")
+    for b in range(4):
+        slin(W(TAB, V + 256 * b, 256), LOW(256), A("s2"), W("BN", b, 1))
+    ts(W("wc", 0, 1), PS(2), float(K), O.mult, PS(4), O.add)
+    ts(A("IDF"), LOW(128), A("pc"), O.is_equal)
+    hilo(W("HI", 0, 256), W("LO", 0, 256), W("XP", LM, 256))
+    gfill("E", V, P)
+    gfill("D0", PL + V, DW)
+    gfill("D1", PL + V, DW)
+    gfill("D2", PL + V, DW)
+    gfill("D3", PL + V, DW)
 
     def slotcol(out, src):
         ts(A(out, 0, 16), A(src[0], src[1], src[1] + 16), float(272 - P), O.add, 528.0, O.min)
         ts(A(out, 16, 32), A(src[0], src[1] + 16, src[1] + 32), float(16 - 256 - P), O.add)
 
-    def ghost_bases(t):
-        scopy(A(TAB, P, P + 256), IN(SNDT, 0, 544, "GI%d" % t, 0, 16))
-        copy(A(TAB, P + 256, G), IN(SNDT, 0, 544, "GI%d" % t, 16, 32))
+    wlist("ps7", 0, "ZB", SNDT, 512, 16)
+    copy(A("SNL"), A("ps7", 0, 32))
+    for o in (LB, RB, BB):
+        copy(W("UT", o, 32), A("ps7", 0, 32))
+    copy(A("ONS"), IN(TAB, 0, V, "SNL", 0, 32))
+    rows2("Y", "d7", TAB, 0, V, 0, "HI", "LO", 128, 256)
+    rows2("Y", "d7", TAB, 0, V, 2, "HI", "LO", 0, 128)
+    wlist("ps6", BB, "ZB", "ONS", 512)
+    slin(A("NKU"), A("UT", 0, 320), float(-K), 0.0)
+    weights("ZL", PS(1), "S")
+    weights("ZR", PS(0), "S")
+    weights("ZV", W("wc", 0, 1), "S")
+    slotcol("GO0", ("ps6", BB))
+    send("GO0", 16, "GI0", 0, "gi0")
+    scopy(A("BB00"), IN("E", 0, V, "SNL", 0, 32))
+    send("BB00", 256, "D0", GH, "ga00")
+    for s in range(2):
+        slin(W("CG", 256 * s, 256), LOW(256), OH(9), W("BC", s, 1))
+        slin(W("ILs", 16 * s, 16), A("IL", 0, 16), 1.0, float(P + 256 * s))
+    for b, c in (("ONE", 1), ("ones", 1), ("one", 1), ("SND2", -1), ("CW0", 0), ("VW0", -1), ("CW1", 0), ("VW1", -1)):
+        iota(A(b), [[0, WIDTH[b]]], 0, c, True)
+    iota(A("sc", 0, 1), [[0, 1]], 0, -1, True)
+    gfill("DR", 2048, 2064)
+    load("Y", "d9", "THI", 0, 1, T["th"][:])
+    load("Y", "d9", "WTI", 0, 1, T["wt"][:])
+    wlist("ps7", 0, "ZP", "ONS", 512)
+    mm("ps5", 0, 64, "IDF", "NKU", True, False)
+    ts(W("RAW", BB, 32), W("ps6", BB, 32), float(P - 1), O.min)
+    copy(W("XP", BB, 32), W("ps6", BB, 32))
+    copy(A("RAW", LM, BM), A("XP", LM, BM))
+    ts(W("RAW", BM, 128), W("XP", BM, 128), float(P - 1), O.min)
+    for k in range(4):
+        fill(A("D%d" % k, 0, GH), 0.0)
+    copy(A("PHS"), A("ps7", 0, 32))
+    for r in range(16):
+        copy(A("D0", PL + r, PL + V, 16), W("E", 128 * r, 128))
 
-    for t in range(2):
+    def consts_a():
+        ts(A("px"), A("qf"), 32.0, O.mult)
+        ts(W("wc", 1, 1), PS(1), float(K), O.mult, PS(4), O.add)
+        ts(A("IS"), LOW(32), A("px"), O.add, float(P), O.add)
+        weights("ZW", W("wc", 1, 1), "S")
+        slin(A("U160", 128, 160), A("IS"), 1.0, float(V - P))
+        scopy(A("U160", 0, 128), W("UT", LM, 128))
+
+    def consts_b():
+        copy(A("wtc"), A("WTI"))
+        copy(A("thc"), A("THI"))
+        ts(A("bth"), A("THI"), -256.0, O.mult, 256.0, O.add)
+        ts(A("th2"), A("THI"), -2.0, O.mult)
+        ts(A("px"), A("odf"), -2.0, O.mult, A("pc"), O.add)
+        ts(A("mA"), A("IDF"), A("th2"), O.mult)
+        ts(A("px"), A("px"), 1.0, O.add)
+        ts(A("mB"), LOW(128), A("px"), O.is_equal)
+        weights("ZH", A("wtc"), "S")
+        tt(A("BTH"), A("mA"), A("mB"), O.add)
+
+    def consts_c():
+        ts(A("px"), A("g15"), -15.0, O.add)
+        ts(A("mA"), LOW(128), A("g15"), O.is_gt)
+        ts(A("mB"), LOW(128), A("pc"), O.is_ge)
+        ts(A("BLK"), LOW(128), A("px"), O.is_ge)
+        tt(A("TRI"), A("mB"), A("mA"), O.subtract)
+        tt(A("BLK"), A("BLK"), A("mA"), O.subtract)
+        ts(W("wc", 2, 1), PS(5), float(K), O.mult, PS(4), O.add)
+        ts(W("wc", 3, 1), OH(10), -4096.0, O.mult, PS(2), O.add)
+        ts(W("wc", 4, 1), OH(1), 4096.0, O.mult, OH(0), O.add)
+        ts(A("lowb"), OH(1), 255.0, O.mult, -1.0, O.add)
+        for z, col in (("ZN", W("wc", 2, 1)), ("ZC", W("wc", 3, 1)), ("ZX", W("wc", 4, 1)), ("ZO", PS(3)), ("ZF", OH(11)), ("ZG", PS(6)),
+                       ("ZE", OH(14)), ("ZQ", A("qf"))):
+            weights(z, col, "S")
+        for z, c in (("IDN", 1.0), ("ID2", 2.0), ("N4K", -4096.0)):
+            slin(A(z), A("IDF"), c, 0.0)
+        slin(A("PHU"), A("IL", 0, 128), 1.0, float(PL))
+        slin(A("DUMPC"), A("IL", 0, 10), 1.0, JUMP + 255.0)
+        ts(A("KH"), A("IL", 0, 32), A("odf"), O.subtract, 0.5, O.mult)
+        for t in range(2):
+            slin(W("OWL", 32 * t, 32), A("IL", 0, 32), 1.0, float(V + 512 * t))
+
+    def given():
+        tt(A("sg"), A("UT", BM, 480), A("XP", BM, 480), O.is_lt)
+        tt(A("ne", 0, 128), W("XP", RM, 128), W("XP", BM, 128), O.not_equal)
+        tt(A("tA", 0, 256), A("XP", LM, BM), A("UT", LM, BM), O.is_equal)
+        tt(A("nLR"), W("XP", LM, 128), W("XP", RM, 128), O.not_equal)
+        tt(A("nLB"), W("XP", LM, 128), W("XP", BM, 128), O.not_equal)
+        tt(A("sA"), A("tA", 0, 128), A("tA", 128, 256), O.mult)
+        copy(A("GOf"), A("GO0"))
+        slin(A("eRB"), A("ne", 0, 128), -1.0, 1.0)
+        slin(A("sgb"), A("sg"), 2.0, -1.0 - BIG)
+        slin(A("CT"), A("NKU"), 1.0, float(GH + 2 - P))
+
+    def given_b():
+        ts(A("plc"), A("XP", 0, 320), float(P), O.is_lt)
+        tt(A("RSq"), W("XP", RB, 32), A("ILs"), O.is_equal)
+        tt(A("e2"), W("XP", RB, 32), W("XP", LB, 32), O.subtract)
+        tt(A("ne", 128, 160), W("XP", RB, 32), W("XP", BB, 32), O.not_equal)
+        tt(A("e2"), A("e2"), A("RSq"), O.mult)
+        tt(A("ne", 128, 160), A("ne", 128, 160), A("RSq"), O.subtract)
+        tt(A("nLR"), A("nLR"), W("plc", LM, 128), O.mult)
+        tt(A("alt"), W("XP", LB, 32), A("e2"), O.add)
+        slotcol("SP2", ("alt", 0))
+        copy(A("GOd"), A("SP2"))
+        tt(A("GOd"), A("GOd"), A("GOf"), O.subtract)
+
+    def given_s():
+        slin(A("nLR"), A("nLR"), BIG, 0.0)
+        slin(A("sg"), A("sg"), 2.0, -1.0)
+        slin(A("isg"), A("plc"), -1.0, 1.0)
+        slin(A("kg"), A("plc"), float(-K), float(K))
+
+    def found_pe(x):
+        if x == 0:
+            wlist("ps7", 0, "ZB", "OUTB", V)
+            mm("ps6", 0, 320, "IDF", "NKU", True, False)
+            mm("ps6", BM, 128, "IDF", "NKU", False, False, LM)
+            wlist("ps6", BM, "ZW", "OUTB", V, 0, False, False)
+        if x == 1:
+            wlist("ps4", BM, "ZR", "OUTB", V + 512)
+            wlist("ps4", 0, "ZR", "OSS", 1024)
+            wlist("ps4", LM, "ZR", "OUTL", V)
+            wlist("ps4", RM, "ZR", "OUTR", V)
+        if x == 2:
+            wlist("ps6", 0, "ZW", "OSS", 1024, 0, False, False)
+            wlist("ps6", LM, "ZW", "OUTL", V, 0, False, False)
+            wlist("ps6", RM, "ZW", "OUTR", V, 0, False, True)
+
+    def found_0():
+        tt(A("mBB"), A("ps7", 0, 128), W("UT", BM, 128), O.is_equal)
+        tt(A("cand", 0, 128), A("mBB"), A("sg", 0, 128), O.mult)
+        rows("Y", "d10", TAB, 0, V, 10, "cand", 0, 128)
+
+    def found_a():
+        tt(A("tB"), A("ps4", 0, 480), A("UT"), O.is_equal)
+        ts(A("tA", 0, 448), A("ps6", 0, 448), float(K), O.is_lt)
+        slin(A("UR"), A("tB"), BIG, 0.0)
+        slin(A("pa"), W("tB", BM, 128), -BIG, BIG)
+        tt(A("pb"), A("PHU"), A("sA"), O.mult)
+        tt(A("ps6", 0, 448), A("ps6", 0, 448), A("tA", 0, 448), O.mult)
+        slin(A("sA"), A("sA"), BIG, 0.0)
+        rows("Y", "d11", TAB, 0, V, 11, "UR", RM, RM + 128)
+
+    def found_c():
+        tt(W("ps7", 0, 128), W("ps6", BM, 128), A("eRB"), O.mult)
+        tt(A("f2"), A("pa"), A("eRB"), O.mult)
+        tt(W("ps7", 0, 128), W("ps7", 0, 128), A("pb"), O.add)
+        rows("Y", "d11", TAB, 0, V, 14, "f2", 0, 128)
+        copy(A("GH_"), W("ps7", 0, 128))
+        tt(A("GL_"), W("ps7", 0, 128), A("GH_"), O.subtract)
+        rows2("Y", "d11", TAB, 0, V, 12, "GH_", "GL_", 0, 128)
+
+    later = [
+        lambda: ts(A("ps7", 128, 448), A("ps5", 0, 320), float(K), O.is_lt),
+        lambda: tt(A("tA", 0, 320), A("ps7", 128, 448), A("plc"), O.mult),
+        lambda: tt(A("lo"), A("ps5", 0, 320), A("tA", 0, 320), O.mult),
+        lambda: tt(A("ps6", 0, 448), A("ps6", 0, 448), A("UR", 0, 448), O.max),
+        lambda: tt(A("UB", 0, 320), A("ps6", 0, 320), A("kg"), O.max),
+        lambda: copy(W("UB", BM, 128), W("ps6", BM, 128)),
+        lambda: tt(A("pre"), A("UR", BM, 480), A("ne"), O.mult),
+        lambda: tt(A("ps6", 0, 320), A("XP", 0, 320), A("CT"), O.add),
+        lambda: tt(A("lo2"), W("lo", LM, 128), A("nLB"), O.mult),
+        lambda: tt(A("CT"), A("ps6", 0, 320), A("isg"), O.mult),
+        lambda: tt(A("pre"), A("pre"), A("sgb"), O.add),
+    ]
+
+    def meanwhile(k):
+        for f in later[:k]:
+            f()
+        del later[:k]
+
+    consts_a()
+    given()
+    copy(A("OBS"), IN(TAB, 0, V, "SNL", 0, 32))
+    scopy(A("OUTB", 0, V), IN(TAB, 0, P, "RAW", BM, BB))
+    wlist("ps4", LB, "ZL", "OBS", 512)
+    wlist("ps4", RB, "ZR", "OBS", 512)
+    wnat("ps4", 64, "ZR", "OBS", 32)
+    consts_c()
+    copy(A("RAW", 0, 64), A("ps4", 0, 64))
+    copy(A("XP", 0, 64), A("ps4", 0, 64))
+    found_pe(0)
+    consts_b()
+    tt(A("RSn"), A("ps4", 64, 96), A("IS"), O.is_equal)
+    tt(A(TAB, P, G), IN(SNDT, 0, 544, "GI0", 0, 32), A("CG"), O.add)
+    both("OSS", 0, TAB, G, "RAW", 0, 64, 32)
+    wlist("ps5", 0, "ZV", "OSS", 1024, 0, False, True)
+    scopy(A("OUTR", 0, V), IN(TAB, 0, G, "RAW", RM, BM))
+    ts(A("GL", 0, 64), A("ps5", 0, 64), float(K), O.min)
+
+    DB = ["D0", "D1", "D2", "D3", "D4"]
+
+    def border(t, k, first="S"):
+        out = "BB%d%d" % (t, k + 1)
+        for s in range(2):
+            (scopy if first == "S" else copy)(W("AQ", 256 * s, 256), IN(DB[k], 0, DW, "GL", RB + 16 * s, RB + 16 * s + 16))
+        for s in range(2):
+            tt(W(out, 256 * s, 256), IN(DB[k], 0, DW, "GL", LB + 16 * s, LB + 16 * s + 16), W("AQ", 256 * s, 256), O.max)
+        send(out, 256, DB[k + 1], GH, "ga%d%d" % (t, k + 1))
+
+    def inner(t, k, at=None):
+        cuts = (0, 32, 64, 96, 128) if k in (1, 2) else (0, 8, 32, 64, 96, 128)
+        o = PL if k < 3 else 0
+        m = 0 if k in (1, 2) else 16
+        for c0, c1 in zip(cuts, cuts[1:]):
+            scopy(A("AB", 16 * c0, 16 * c1), IN(DB[k], 0, DW, "GL", RM + c0, RM + c1))
+        if t:
+            scopy(A(DB[k + 1], o + V + 16 * m, o + V + 512), IN(DB[k], 0, DW, "GL", LN + m, LN + 32))
+            if m:
+                copy(W(DB[k + 1], o + V, 16 * m), IN(DB[k], 0, DW, "GL", LN, LN + m))
+        for c0, c1 in zip(cuts, cuts[1:]):
+            tt(A(DB[k + 1], o + 16 * c0, o + 16 * c1), IN(DB[k], 0, DW, "GL", LM + c0, LM + c1), A("AB", 16 * c0, 16 * c1), O.max)
+            if at and c1 == 64:
+                at()
+
+    def flags(t, k, q, part=3):
+        n = V + 512 * t
+        b = "FL" if q == "V" else "FS"
+        if part & 1 and q == "V":
+            ts(A(b, 0, n), W(DB[k], PL, n), A("thc"), O.is_ge, 256.0, O.mult)
+        if part & 1 and q == "S":
+            slin(A(b, 0, n), W(DB[k], PL, n), 256.0, A("bth"), F.Relu)
+        if part & 2:
+            unmix(b, 0, 128, range(4))
+            if t:
+                mm("ps4", 0, 512, "ID2", b, False, False, V)
+
+    def opensums(t):
+        for c in range(4 + t):
+            mm("ps%d" % c, 0, 512, "BTH", "ONE", True, False)
+
+    CNT = ("ps4", "ps5")
+
+    def partners(t, part=7):
         n = V + 512 * t
         nc = n // 16
-        h = n // 2
-        hc = nc // 2
-        w = 128 + 32 * t
-        nchunk = n // 512
-        PF = ("PI", "PN")[t]
-        ME = ("MEN", "MEW")[t]
-        BB = ["BB%d%d" % (t, k) for k in range(4)]
-        WB = ["E", "W1", "W2", "W3", "W4"]
+        if part & 1:
+            wlist("ps7", 0, "ZC", TAB, n)
+        if part & 4:
+            ts(A("BL", 0, nc), A("ps7", 0, nc), 4096.0, O.add, float(n - 1), O.min)
+            ts(A("nm", 0, nc), A("ps7", 0, nc), 0.0, O.is_ge)
+        if part & 2:
+            mm(CNT[t], 0, nc, "N4K", "nm", True, False)
 
-        def flags(k, c0, c1):
-            ts(A("FL", 512 * c0, 512 * c1), A(WB[k], 512 * c0, 512 * c1), A("thc"), O.is_ge, 256.0, O.mult)
-            for c in range(c0, c1):
-                mm("ps%d" % c, 0, 512, "IDN", "FL", False, False, 512 * c)
-
-        def sflags(k, c0, c1):
-            x, y = A("M", 512 * c0, 512 * c1), A(WB[k], 512 * c0, 512 * c1)
-            call("S", lambda e: e.activation(mk(x), mk(y), F.Relu, bias=mk(A("bth")), scale=256.0), [x], [y, A("bth")])
-            for c in range(c0, c1):
-                mm("ps%d" % c, 0, 512, "IDN", "M", k == 0, False, 512 * c)
-
-        def sign(out, in_, b):
-            call("S", lambda e: e.activation(mk(out), mk(in_), F.Sign, bias=mk(A(b))), [out], [in_, A(b)])
-
-        def outb(c):
-            scopy(A("OUTB", 512 * c, 512 * c + 512), IN(TAB, 0, P, "BL", 32 * c, 32 * c + 32))
-
-        def lists(j):
-            wlist("ps%d" % (5 + j), 0, "ZR", TAB, h, h * j)
-            wlist("ps%d" % (5 + j), 80, "ZL", TAB, h, h * j)
-
-        def take(bk, k, ll, rl, lm, rm):
-            copy(rl, A(bk, 0, k))
-            copy(ll, A(bk, 80, 80 + k))
-            ts(rm, rl, float(-G), O.add)
-            ts(lm, ll, float(-G), O.add)
-
-        def lists2(j):
-            take("ps%d" % (5 + j), hc, *[A(x, hc * j, hc * j + hc) for x in ("LL", "RL", "LM", "RM")])
-
-        def blist():
-            ts(A("BL", 0, nc), A("ps7", 0, nc), float(P - 1), O.min)
-            tt(A("ge", 0, nc), A("ps7", 0, nc), A("MEL", 0, nc), O.is_le)
-
-        def slists():
-            wlist("ps7", 0, "ZR", "OBS", 512)
-            wlist("ps7", 80, "ZL", "OBS", 512)
-
-        def slists2():
-            take("ps7", 32, A("SRAW", 0, 32), A("SRAW", 32, 64), A("SM", 0, 32), A("SM", 32, 64))
-
-        def outs():
-            scopy(A("OSS", 512, 1024), IN(TAB, 0, G, "SRAW", 32, 64))
-            copy(A("OSS", 0, 512), IN(TAB, 0, G, "SRAW", 0, 32))
-            wlist("ps7", 0, "ZB", "OSS", 1024)
-
-        def outlr(j):
-            c0, c1 = hc * j, hc * j + hc
-            m = 768 * j
-            scopy(A("OUTR", h * j, h * j + h), IN(TAB, 0, G, "RL", c0, c1))
-            copy(A("OUTL", h * j, h * j + h - m), IN(TAB, 0, G, "LL", c0, c1 - m // 16))
-            if m:
-                scopy(A("OUTL", n - m, n), IN(TAB, 0, G, "LL", nc - m // 16, nc))
-            wlist("ps%d" % (5 + j), 0, "ZB", "OUTR", h, h * j)
-            wlist("ps%d" % (5 + j), 80, "ZB", "OUTL", h, h * j)
-
-        def target():
-            for a in range(3):
-                tt(A("ps5", w * a, w * a + w), A("ps5", w * a, w * a + w), A(ME, 0, w), O.not_equal)
-            for a, x in enumerate(("da", "db", "dc")):
-                ts(A(x, 0, w), A("ps5", w * a, w * a + w), BIG, O.mult, float(WW * a), O.add)
-            tt(A("db", 0, w), A("db", 0, w), A("dc", 0, w), O.min)
-            tt(A("da", 0, w), A("da", 0, w), A("db", 0, w), O.min)
-            tt(A("da", 0, w), A(("PI", "ps6")[t], 0, w), A("da", 0, w), O.add)
-            hilo(A("TH", 0, w), A("TL", 0, w), A("da", 0, w))
-            rows2("Y", "d%d" % (10 + t), TAB, 0, n, 8, "TH", "TL", 0, w)
-
-        def valid(parts):
-            for bk, me, lm, tmp, gl in parts:
-                tt(bk, bk, me, O.is_equal)
-            for bk, me, lm, tmp, gl in parts:
-                tt(tmp, bk, lm, O.mult)
-            for bk, me, lm, tmp, gl in parts:
-                ts(gl, tmp, float(G), O.add)
-
-        def validlr(j):
-            c0, c1 = hc * j, hc * j + hc
-            valid([(A("ps%d" % (5 + j), o, o + hc), A("MEL", c0, c1), A(lm, c0, c1), A(tmp, c0, c1), A(gl, c0, c1))
-                   for o, lm, tmp, gl in ((0, "RM", "pa", "GR"), (80, "LM", "pb", "GL"))])
-
-        def valids():
-            valid([(A("ps7", o, o + 32), A("SNLf"), A("SM", o, o + 32), A("e1", o, o + 32), A("SG", o, o + 32)) for o in (32, 0)])
-
-        def border(k):
-            if k == 0:
-                copy(A("AQ"), IN(WB[k], 0, WW, "SG", 32, 64))
-            for s in range(2):
-                tt(A(BB[k + 1], 256 * s, 256 * s + 256), IN(WB[k], 0, WW, "SG", 16 * s, 16 * s + 16), A("AQ", 256 * s, 256 * s + 256), O.max)
-            send(BB[k + 1], 0, 256, WB[k + 1], P, "ga%d%d" % (t, k + 1))
-
-        if t == 0:
-            wlist("ps0", 0, "ZB", SNDT, 512, 16)
-            copy(A("SNL"), A("ps0", 0, 32))
-            scopy(A(BB[0]), IN("E", 0, n, "SNL", 0, 32))
-            send(BB[0], 0, 256, "E", P, "ga00")
-            copy(A("SNLf"), A("ps0", 0, 32))
-            copy(A("OBS"), IN(TAB, 0, n, "SNL", 0, 32))
-            wlist("ps1", 0, "ZB", "OBS", 512)
-            slists()
-            lists(0)
-            lists(1)
-            consts_a()
-            slotcol("GO0", ("ps1", 0))
-            send("GO0", 0, 16, "GI0", 0, "gi0")
-            gfill("W2", V, P)
-            load("Y", "d15", "DR", 0, 2048, T["det"][:])
-            slin(A("DX"), A("DR"), 0.5, 127.8)
-            slin(A("DT", 0, 2048), A("DX"), 1.0, -256.0)
-            slists2()
-            tt(A("RSq"), A("SM", 32, 64), A("ILs"), O.is_equal)
-            tt(A("e2"), A("SM", 32, 64), A("SM", 0, 32), O.subtract)
-            copy(A("GOf"), A("GO0"))
-            tt(A("e2"), A("e2"), A("RSq"), O.mult)
-            ts(A("alt"), A("SM", 0, 32), float(G), O.add)
-            lists2(0)
-            tt(A("alt"), A("alt"), A("e2"), O.add)
-            lists2(1)
-            slotcol("GOd", ("alt", 0))
-            consts_n()
-            tt(A("GOd"), A("GOd"), A("GOf"), O.subtract)
-            consts_c()
-            ghost_bases(0)
-            outs()
-            outlr(0)
-            valids()
-            border(0)
-            gfill("W3", V, P)
-            outlr(1)
-        else:
-            scopy(A("OBS"), IN(TAB, 0, n, "SNL", 0, 32))
-            lists(0)
-            slists()
-            lists(1)
-            lists2(0)
-            copy(A("OUTL", 0, h), IN(TAB, 0, G, "LL", 0, hc))
-            scopy(A("OUTR", 0, h), IN(TAB, 0, G, "RL", 0, hc))
-            slists2()
-            outs()
-            wlist("ps5", 0, "ZB", "OUTR", h, 0)
-            wlist("ps5", 80, "ZB", "OUTL", h, 0)
-            lists2(1)
-            outlr(1)
-            valids()
-            border(0)
-        wlist("ps7", 0, "ZB", TAB, n)
-        validlr(0)
-
-        def right(k, c, f=scopy):
-            f(A("AB", 512 * c, 512 * c + 512), IN(WB[k], 0, WW, "GR", 32 * c, 32 * c + 32))
-
-        def left(k, c):
-            tt(A(WB[k + 1], 512 * c, 512 * c + 512), IN(WB[k], 0, WW, "GL", 32 * c, 32 * c + 32), A("AB", 512 * c, 512 * c + 512), O.max)
-
-        def alike():
-            tt(A("eq2", 0, 2 * w), A(PF, 0, 2 * w), A(PF, w, 3 * w), O.is_equal)
-            tt(A("eqb", 0, w), A(PF, 0, w), A(PF, 2 * w, 3 * w), O.is_equal)
-            tt(A("sg", 0, w), A(ME, 0, w), A(PF, 2 * w, 3 * w), O.is_lt)
-            ts(A("sg", 0, w), A("sg", 0, w), 2.0, O.mult, -1.0, O.add)
-
-        for k in range(3):
-            if k == 0:
-                if t == 0:
-                    right(0, 0)
-                    right(0, 1)
-                    alike()
-                else:
-                    right(0, 0)
-                    right(0, 1)
-                left(0, 0)
-                validlr(1)
-                for a, z in enumerate(("ZR", "ZL", "ZB")):
-                    wnat("ps5", w * a, z, "OUTR", w)
-                if t == 0:
-                    wnat("ps6", 0, "ZR", "OBS", 32)
-                else:
-                    for a, z in enumerate(("ZR", "ZL", "ZB")):
-                        wnat("ps6", w * a, z, TAB, w)
-                for c in range(2, nchunk):
-                    right(0, c)
-                left(0, 1)
-                blist()
-            else:
-                for s in range(2):
-                    scopy(A("AQ", 256 * s, 256 * s + 256), IN(WB[k], 0, WW, "SG", 32 + 16 * s, 48 + 16 * s))
-                for c in range(nchunk):
-                    right(k, c)
-                if k == 2:
-                    flags(k, 0, 1)
-                border(k)
-                if k == 2:
-                    flags(k, 1, nchunk)
-            if k == 1:
-                if t == 0:
-                    gfill("OUTL", V, P)
-                    tt(A("RSn"), A("ps6", 0, 32), A("IS"), O.is_equal)
-                target()
-            if k == 2:
-                gfill("W1", 0, n)
-                if t == 1:
-                    alike()
-                ts(A(CMP, 0, 256), A(TAB, n, n + 512, 2), A("c1"), O.add)
-            if k == 1:
-                if t == 1:
-                    scopy(A("PN"), A("ps6", 0, 480))
-                sflags(1, 0, nchunk)
-            if k == 0:
-                sflags(0, 0, nchunk)
-            for c in range(2 if k == 0 else 0, nchunk):
-                left(k, c)
-            if k == 2:
-                for c in range(nchunk):
-                    outb(c)
-        wlist("ps7", 0, "ZB", "OUTB", n)
-        rows2("Y", "d%d" % (12 + t), "OUTB", 0, n, 10, "TH", "TL", 0, w)
-        gfill("W2", 0, n)
+    def select(t):
+        n = V + 512 * t
+        nc = n // 16
         hh = VPART[t]
-        for c in range(nchunk):
-            right(3, c)
-        flags(3, 0, nchunk - 1)
-        sflags(3, nchunk - 1, nchunk)
-
-        def hot(c):
-            lo, hi = 512 * c, 512 * c + 512
-            sign(A("H", lo, hi), A("ps%d" % c), "nth")
-            if lo < hh:
-                ts(A("M", lo, min(hi, hh)), A("ps%d" % c, 0, min(hi, hh) - lo), A("thc"), O.is_ge)
-
-        for c in range(nchunk):
-            left(3, c)
-            mm("ps%d" % c, 0, 512, "IDN", "W4", False, True, 512 * c)
-            if c == 1:
-                tt(A("ne", 0, nc), A("ps7", 0, nc), A("MEL", 0, nc), O.not_equal)
-                mm("ps5", 0, nc, "N4K", "ne", True, False)
-                mm("ps5", 0, nc, "N4K", "ge", False, False)
-        for c in range(nchunk):
-            hot(c)
+        inner(t, 3, lambda: unmix("D4", 0, 64, range(4)))
+        if t:
+            mm("ps4", 0, 512, "ID2", "D4", False, True, V)
+            scopy(W("H", V, 512), A("ps4"), F.Sign)
+        for b in range(4):
+            unmix("D4", 64, 128, [b], True)
+        for b in range(4):
+            if b % 2:
+                ts(W("H", 512 * b, 512), A("ps%d" % b), 1.0, O.min, -1.0, O.max)
+            else:
+                scopy(W("H", 512 * b, 512), A("ps%d" % b), F.Sign)
         parts = [(lo, min(lo + 512, n)) for lo in range(hh, n, 512)]
         for lo, hi in parts:
-            scopy(A("AB", lo, hi), IN("H", 0, P, "BL", lo // 16, hi // 16))
+            scopy(A("AB", lo, hi), IN("H", 0, n, "BL", lo // 16, hi // 16))
+        copy(A("M", 0, hh), A("H", 0, hh))
         for lo, hi in ((0, 1024), (1024, hh)):
-            tt(A("M", lo, hi), IN("H", 0, P, "BL", lo // 16, hi // 16), A("M", lo, hi), O.max)
+            tt(A("M", lo, hi), IN("H", 0, n, "BL", lo // 16, hi // 16), A("M", lo, hi), O.max)
         for i, (lo, hi) in enumerate(parts):
-            mm("ps%d" % i, 0, hi - lo, "IDN", "H", True, False, lo)
-            mm("ps%d" % i, 0, hi - lo, "IDN", "AB", False, True, lo)
-            sign(A("M", lo, hi), A("ps%d" % i, 0, hi - lo), "one")
-        wlist("ps5", 0, "ZA", "M", 1024, 0, False, False)
-        wlist("ps5", 64, "ZA", "M", n - 1024, 1024, False, True)
-        slin(A("W3", 0, n), A("FL", 0, n), 0.0, 0.0)
-        slin(A("OS", 0, n), A("FL", 0, n), 0.0, -8.0)
-        ts(A("go", 0, hh // 16), A("ps5", 0, hh // 16), float(Q), O.is_ge)
-        ts(A("go", hh // 16, nc), A("ps5", hh // 16, nc), float(2 * Q - 16), O.is_ge)
-        mm("ps6", 0, nc, "BLK", "go")
-        mm("ps7", 0, nc, "NLE", "go", True, False)
-        mm("ps7", 0, nc, "N4K", "go", False, True)
-        call("V", lambda e: e.tensor_tensor_scan(mk(A("sc", 0, nc)), mk(A("ones", 0, nc)), mk(A("ps6", 0, nc)), 4096.0, O.mult, O.add), [A("sc", 0, nc)], [A("ones", 0, nc), A("ps6", 0, nc)])
-        tt(A("ps7", 0, nc), A("ps7", 0, nc), A("sc", 0, nc), O.add)
-        tt(A("c8", 0, nc), A("ps7", 0, nc), A("D1280", 0, nc), O.min)
-        copy(A("TG", 0, nc), A("c8", 0, nc))
-        copy(IN(CMP, 0, 1280 + n, "TG", 0, nc), A("OUTB", 0, n))
-        wrap("ps0", 0, 32, "ZB", CMP, lambda r: (r >> 1, 256, 8), "ZM")
-        wrap("ps1", 0, 32, "ZU", CMP, lambda r: (r >> 1, 256, 8), "ZT")
-        copy(A("TD"), A("ps0", 0, 32))
-        copy(A("TF"), A("ps0", 0, 32))
+            mm("ps%d" % i, 0, hi - lo, "ID2", "H", True, False, lo)
+            mm("ps%d" % i, 0, hi - lo, "ID2", "AB", False, True, lo)
+            slin(A("M", lo, hi), A("ps%d" % i, 0, hi - lo), 1.0, A("one"), F.Sign)
+        wlist(CNT[t], 0, "ZA", "M", 1024, 0, False, False)
+        wlist(CNT[t], 64, "ZA", "M", n - 1024, 1024, False, True)
+        meanwhile(2)
+        ts(A("go", 0, nc), A(CNT[t], 0, nc), 2.0, O.is_ge)
+        mm("ps2", 0, nc, "BLK", "go")
+        mm("ps3", 0, nc, "TRI", "go")
+        meanwhile(1)
+        ts(A("ps2", 256, 256 + nc), A("ps2", 0, nc), 0.0, O.is_equal, 4096.0, O.mult)
+        scan(A("sc", 1, nc + 1), A("ones", 0, nc), A("ps2", 0, nc), -1.0, O.mult, O.add)
+        tt(A("ps3", 0, nc), A("ps3", 0, nc), A("go", 0, nc), O.mult)
+        tt(A("x0", 0, nc), A("ps2", 256, 256 + nc), A("sc", 0, nc), O.add)
+        ts(A("a0", 0, nc), A("x0", 0, nc), 255.0, O.min, A("lowb"), O.max)
+        wlist("ps0", 0, "ZX", "a0", nc)
+        tt(A("val", 0, nc), A("ps3", 0, nc), A("sc", 0, nc), O.add)
+        ts(A("ye_"), A("KH"), W("sc", nc, 1), O.is_gt, -1.0, O.mult)
+        mm("ps1", 0, 32, "N4K", "ye_", True, False)
+        meanwhile(1)
+        k = nc // 16
+        tt(A("of", 0, k), A("ps0", 0, k), A("DUMPC", 0, k), O.min)
+        ts(A("OFF", 0, k), A("of", 0, k), 1.0 - JUMP, O.add)
+        cw, vw = "CW%d" % t, "VW%d" % t
+        copy(IN(cw, 0, 416, "OFF", 0, k), LOW(nc))
+        copy(IN(vw, 0, 416, "OFF", 0, k), A("val", 0, nc))
+        scan(A("CF"), A(cw, 0, 256), A(cw, 0, 256), 0.0, O.max, O.max)
+        scan(A("ps3", 0, 256), A(vw, 0, 256), A(vw, 0, 256), -1.0, O.max, O.max)
+        wlist("ps2", 0, "ZA", "CF", 256, 0, True, False)
+        tt(A("MM"), A("ps3", 0, 256), LOW(256), O.is_equal)
+        wlist("ps2", 0, "ZQ", "MM", 256, 0, False, True)
+        meanwhile(1)
+        copy(A("T0"), A("ps2", 0, 16))
+        copy(A("G0"), IN(TAB, 0, P, "T0", 0, 16))
+        wrap("ps1", 0, 32, "ZO", "G0", lambda r: (r >> 1, 256, 8), "ZB", False, True)
+        meanwhile(9)
+        tt(A("TF"), A("ps1", 0, 32), W("OWL", 32 * t, 32), O.min)
+        copy(A("TD"), A("TF"))
         scopy(A("ET"), IN("E", 0, P, "TD", 0, 32))
         scopy(A("GT"), IN(TAB, 0, P, "TD", 0, 32))
-        if t == 0:
-            copy(IN("OS", 0, P, "TD", 0, 32), A(TAB, n, n + 512))
-        tt(A("e3"), A("ps1", 0, 32), A("DUM"), O.min)
-        copy(A("TR"), A("e3"))
+        copy(IN("OS%d" % t, 0, P, "TD", 0, 32), W(TAB, n, 512))
         wlist("ps4", 0, "ZH", "ET", 512)
-        if t == 0:
-            scopy(A("ONS"), IN("OS", 0, P, "SNL", 0, 32))
-            wnat("ps3", 0, "ZO", "OS", w)
-        copy(IN("RN", 0, DUMP + 512, "TR", 0, 32), A(TAB, n, n + 512))
-        if t == 1:
-            copy(IN("OS", 0, P, "TD", 0, 32), A(TAB, n, n + 512))
-        slin(A("E2"), A("ET"), 0.5, 127.8)
-        scopy(A("ONT"), IN("RN", 0, P, "TD", 0, 32))
-        wnat("ps5", 0, "ZM", "RN", w, 0)
-        if t == 0:
-            wlist("ps2", 0, "ZM", "ONS", 512)
-            wnat("ps2", 32, "ZM", "ONS", 32)
+
+    def err0(t):
+        n = V + 512 * t
+        tt(A("hx", 0, 32), A("ps4", 0, 32), A("TF"), O.add)
+        tt(A("hx", 32, 64), A("ps4", 0, 32), W("OWL", 32 * t, 32), O.add)
+        ts(A("em"), A("TF"), float(n), O.is_ge, 2048.0, O.mult)
+        ts(A("hy"), A("hx"), 2047, O.bitwise_and)
+        for x in range(2):
+            tt(W("hz", 32 * x, 32), W("hy", 32 * x, 32), A("em"), O.max)
+        copy(A("HX"), A("hz"))
+
+    def halves():
+        ts(A("E1"), A("ET"), 0.5, O.mult, 127.8, O.add)
+        ts(A("E2"), A("E1"), -256.0, O.add)
+
+    def details(x):
+        slin(W("DG", 512 * x, 512), IN("DR", 0, 2064, "HX", 32 * x, 32 * x + 32), 0.5, 127.8)
+
+    def err1(bk, out):
+        mm(bk, 0, 512, "IDN", "E2", True, False)
+        mm(bk, 0, 512, "IDN", "DG", False, True, 512)
+        scopy(out, A(bk))
+
+    def levels(t, extra):
+        for k in range(3):
+            if k:
+                border(t, k)
+            extra(k, 0)
+            inner(t, k)
+            extra(k, 1)
+
+    border(0, 0, "V")
+    gfill("OS0", 0, 1536)
+    mm("ps5", LM, 256, "IDF", "NKU", True, False, LM)
+    both("OUTL", 0, TAB, G, "RAW", LM, RM, LM + 64)
+    scopy(A("OUTB", V, V + 512), IN(TAB, 0, P, "RAW", BB, BB + 32))
+    wlist("ps5", RM, "ZV", "OUTR", V, 0, False, False)
+    wlist("ps5", LM, "ZV", "OUTL", V, 0, False, True)
+    found_0()
+    flags(0, 0, "V", 1)
+    ts(A("GL", LM, BM), A("ps5", LM, BM), float(K), O.min)
+    given_b()
+
+    def extra0(k, x):
+        if (k, x) == (0, 0):
+            found_pe(1)
+            opensums(0)
+            flags(0, 0, "V", 2)
+            found_pe(2)
+        if (k, x) == (0, 1):
+            given_s()
+        if (k, x) == (1, 0):
+            gfill("OS0", 1536, P)
+            partners(0, 1)
+        if (k, x) == (1, 1):
+            flags(0, 1, "S")
+            found_a()
+            partners(0, 6)
+            found_c()
+        if (k, x) == (2, 0):
+            gfill("OS1", 0, 1792)
+        if (k, x) == (2, 1):
+            flags(0, 2, "S")
+            flags(0, 3, "V")
+            meanwhile(6)
+    levels(0, extra0)
+    gfill("OS1", 1792, G)
+    wait("Y", ("ga03", 2 * half, {}))
+    load("Y", "d15", "DR", 0, 2048, T["det"][:])
+    select(0)
+
+    OS = "OS0"
+    scopy(A("ONS"), IN(OS, 0, P, "SNL", 0, 32))
+    wlist("ps1", 0, "ZP", "GT", 512)
+    wlist("ps2", 0, "ZP", "ONS", 512)
+    wnat("ps3", 0, "ZO", "ONS", 32)
+    err0(0)
+    details(1)
+    details(0)
+    halves()
+    err1("ps4", W("D0", PL + V, 512))
+    ts(A("TP"), A("ps1", 0, 32), float(-PL), O.add)
+    ts(A("sp"), A("ps2", 0, 32), 0.0, O.is_gt)
+    tt(A("sq"), A("ps2", 0, 32), A("RSq"), O.mult)
+    tt(A("sp"), A("sp"), A("GOd"), O.mult)
+    tt(A("sq"), A("sq"), A("PHS"), O.max)
+    tt(A("sp"), A("sp"), A("GOf"), O.add)
+    ts(A("SP2"), A("sq"), float(-PL), O.add)
+    copy(A("GO1"), A("sp"))
+    send("GO1", 16, "GI1", 0, "gi1")
+    tt(A("sq"), A("ps3", 0, 32), A("RSn"), O.mult)
+    tt(A("SN1"), A("sq"), A("SNI"), O.max)
+    hilo(A("SH1"), A("SL1"), A("SN1"))
+    rows2("Y", "d24", "SND2", 16, 528, 10, "SH1", "SL1", 0, 32)
+    tt(IN("D0", PL, PL + V + 512, "TP", 0, 32), A("DG", 0, 512), A("E2"), O.add)
+    scopy(A("BB10"), IN("D0", PL, PL + V + 512, "SP2", 0, 32))
+    send("BB10", 256, "D0", GH, "ga10")
+    wlist("ps1", 32, "ZR", "GT", 512)
+    wnat("ps0", 0, "ZP", OS, 128)
+    for i, j in ((0, 6), (1, 7), (2, 4), (3, 5)):
+        dma("Y", "d21", T[TAB][i::16, V:V + 512], T["GT"][j::16, 0:512], [("GT", 0, 512, j)], [(TAB, V, V + 512, i)])
+    mm("ps7", 0, 64, "IDF", "CT", True, False)
+    wlist("ps3", 0, "ZG", "GT", 512)
+    mm("ps5", LM, 256, "IDF", "CT", True, False, LM)
+    CAP, CPS = W("ps6", 384, 128), W("ps6", 256, 128)
+    ts(A("TR"), A("ps1", 32, 64), float(P - 1), O.min)
+    scopy(A("ONT"), IN(OS, 0, P, "TR", 0, 32))
+    scopy(A("OUTB", 0, 1024), IN(OS, 0, P, "RAW", BM, BM + 64))
+    for a, z in enumerate(("ZB", "ZO", "ZR", "ZF", "ZE")):
+        wnat("ps1", 32 * a, z, "GT", 32)
+    wnat("ps1", 160, "ZO", "ONT", 32)
+    for o in (LB, RB):
+        ts(W("tA", o, 32), A("ps2", 0, 32), 0.0, O.is_equal, BIG, O.mult)
+    tt(A("e2"), A("ps2", 0, 32), A("pre", 128, 160), O.add)
+    tt(A("UB2", 0, 64), A("UB", 0, 64), A("tA", 0, 64), O.min)
+    tt(A("LO2", 0, 64), A("lo", 0, 64), A("tA", 0, 64), O.min)
+    ts(CAP, A("ps0", 0, 128), 0.0, O.is_equal, BIG, O.mult)
+    tt(W("LO2", RB, 32), W("LO2", RB, 32), A("e2"), O.max)
+    tt(A("pa"), A("ps0", 0, 128), A("pre", 0, 128), O.add)
+    ts(A("vn", 0, 128), A("ps0", 0, 128), float(-PL), O.add)
+    for o in (LM, RM):
+        tt(W("UB2", o, 128), CAP, W("UB", o, 128), O.min)
+        tt(W("LO2", o, 128), CAP, W("lo", o, 128), O.min)
+    copy(W("GL", LN, 32), A("ps3", 0, 32))
+    tt(W("LO2", RM, 128), W("LO2", RM, 128), A("pa"), O.max)
+    for r in range(16):
+        copy(W("E", 128 * r, 128), A("D0", PL + r, PL + V, 16))
+    copy(W("E", V, 512), W("D0", PL + V, 512))
+    both(OS, P, "SND2", 544, "GI1", 0, 32, 16)
+    both("OSS", 0, OS, G, "RAW", 0, 64, 32)
+    wlist("ps7", 0, "ZN", "OSS", 1024, 0, False, True)
+    scopy(A("OUTR", 0, V), IN(OS, 0, G, "RAW", RM, BM))
+
+    def newlists(bk, lo, hi):
+        tt(A(bk, lo, hi), A(bk, lo, hi), A("UB2", lo, hi), O.min)
+        tt(A(bk, lo, hi), A(bk, lo, hi), A("LO2", lo, hi), O.max)
+        copy(A("GL", lo, hi), A(bk, lo, hi))
+
+    X2 = lambda a, o=0, n=128: W("X2", 160 * a + o, n)
+    UR2 = lambda a, o=0, n=128: W("UR2", 160 * a + o, n)
+    N3 = lambda a: W("N3", 128 * a, 128)
+    U2 = lambda a: W("U2", 128 * a, 128)
+    T1, T2 = W("ps6", 0, 128), W("ps6", 128, 128)
+
+    def renamed():
+        ts(A("tA", 0, 384), A("ps6", 0, 384), 0.0, O.is_le, BIG, O.mult)
+        tt(A("pa"), A("ps6", 256, 384), W("UB", BM, 128), O.min)
+        tt(A("pb"), A("ps6", 0, 128), W("UB", LM, 128), O.min)
+        tt(A("ps6", 0, 384), A("ps6", 0, 384), A("UR", LM, BB), O.min)
+        tt(A("pa"), A("pa"), A("mBB"), O.max)
+        tt(A("N3"), A("ps6", 0, 384), A("XP", LM, BB), O.max)
+        tt(A("pa"), CAP, A("pa"), O.min)
+        ts(CPS, A("vn", 0, 128), 0.0, O.is_gt, BIG, O.mult)
+        tt(T1, CAP, N3(2), O.min)
+        tt(T2, A("pb"), A("lo2"), O.max)
+        tt(A("tB", 0, 128), CPS, N3(0), O.min)
+        tt(A("pb"), T2, A("nLR"), O.min)
+        tt(X2(2), T1, A("tB", 0, 128), O.max)
+        tt(T2, CPS, A("pb"), O.min)
+        copy(W("HI", 256, 128), X2(2))
+        tt(A("SG2", 0, 128), A("U160", 0, 128), X2(2), O.is_lt)
+        tt(T2, T2, A("pa"), O.max)
+        tt(W("LO", 256, 128), X2(2), W("HI", 256, 128), O.subtract)
+        tt(A("cand", 0, 128), T2, A("SG2", 0, 128), O.min)
+        rows2("Y", "d20", TAB, 0, V, 4, "HI", "LO", 256, 384)
+        rows("Y", "d20", TAB, 0, V, 10, "cand", 0, 128)
+
+    def renamed2():
+        tt(A("vs", 0, 128), A("vn", 0, 128), A("sg", 0, 128), O.add)
+        tt(T2, CAP, N3(1), O.min)
+        tt(A("U2"), A("tA", 0, 384), A("UR", LM, BB), O.min)
+        tt(T2, T2, A("vs", 0, 128), O.max)
+        tt(A("U2R"), CAP, U2(1), O.min)
+        copy(W("HI", 128, 128), T2)
+        copy(X2(1), T2)
+        tt(W("LO", 128, 128), T2, W("HI", 128, 128), O.subtract)
+        rows("Y", "d22", TAB, 0, V, 11, "U2R", 0, 128)
+        rows2("Y", "d22", TAB, 0, V, 0, "HI", "LO", 128, 256)
+
+    def fresh():
+        n1 = lambda a: W("ps1", 32 * a, 32)
+        copy(A("e2"), n1(3))
+        copy(X2(0, 128, 32), n1(0))
+        copy(X2(1, 128, 32), n1(1))
+        tt(A("sq"), n1(5), A("e2"), O.min)
+        ts(A("sp"), n1(5), 0.0, O.is_le, BIG, O.mult)
+        tt(X2(2, 128, 32), n1(2), A("sq"), O.max)
+        tt(A("sp"), n1(3), A("sp"), O.min)
+        fill(UR2(0, 128, 32), BIG)
+        tt(A("SG2", 128, 160), A("U160", 128, 160), X2(2, 128, 32), O.is_lt)
+        tt(UR2(2, 128, 32), n1(4), A("sp"), O.max)
+        fill(UR2(1, 128, 32), 0.0)
+        ts(A("sq"), A("sq"), 0.0, O.max)
+        hilo(A("SH"), A("SL_"), X2(2, 128, 32))
+        tt(A("cand", 128, 160), A("sq"), A("SG2", 128, 160), O.min)
+        rows2("Y", "d23", TAB, V, V + 512, 4, "SH", "SL_", 0, 32)
+        rows("Y", "d23", TAB, V, V + 512, 10, "cand", 128, 160)
+
+    copy(A("OUTL", 0, 1024), IN(OS, 0, G, "RAW", LM, LM + 64))
+    newlists("ps7", 0, 64)
+    border(1, 0, "V")
+    scopy(A("OUTL", 1024, V), IN(OS, 0, G, "RAW", LM + 64, RM))
+    scopy(A("OUTB", 1024, V), IN(OS, 0, P, "RAW", BM + 64, BB))
+    wlist("ps5", RM, "ZN", "OUTR", V, 0, False, False)
+    wlist("ps5", LM, "ZN", "OUTL", V, 0, False, True)
+    for a, x in enumerate(("OUTL", "OUTR", "OUTB")):
+        wlist("ps6", 128 * a, "ZO", x, V)
+    fresh()
+    newlists("ps5", LM, BM)
+    flags(1, 0, "V", 1)
+    opensums(1)
+    flags(1, 0, "V", 2)
+
+    later += [
+        lambda: tt(T1, CAP, N3(0), O.min),
+        lambda: tt(A("pb"), CAP, U2(2), O.min),
+        lambda: tt(X2(0), T1, A("vn", 0, 128), O.max),
+        lambda: tt(T1, U2(0), A("nLR"), O.min),
+        lambda: tt(UR2(0), CPS, U2(0), O.max),
+        lambda: tt(A("pa"), T1, A("sA"), O.max),
+        lambda: [copy(W("RAW2", 160 * a + 128, 32), W("ps7", 256 + 32 * a, 32)) for a in range(3)],
+        lambda: [tt(T1, CPS, A("pa"), O.min), copy(W("RAW2", 0, 128), X2(0)), tt(UR2(2), T1, A("pb"), O.max)],
+        lambda: [copy(W("RAW2", 160 * a, 128), X2(a)) for a in (1, 2)],
+    ]
+
+    def extra1(k, x):
+        if (k, x) == (1, 1):
+            flags(1, 1, "S")
+            renamed()
+        if (k, x) == (2, 1):
+            partners(1, 1)
+            for a, z in enumerate(("ZL", "ZR", "ZB")):
+                wlist("ps7", 256 + 32 * a, z, TAB, 512, V)
+            flags(1, 2, "S")
+            flags(1, 3, "V")
+            partners(1, 6)
+            renamed2()
+            slin(UR2(1), A("U2R"), 1.0, 0.0)
+            slin(A("SG2"), A("SG2"), 2.0, -1.0)
+            meanwhile(4)
+    levels(1, extra1)
+    select(1)
+
+    OS = "OS1"
+    n = V + 512
+    def pull(x, a, c0, c1, f):
+        f(A(x, 16 * c0, 16 * c1), IN(OS, 0, G, "RAW2", 160 * a + c0, 160 * a + c1))
+
+    def tile(bk, x, c0, c1):
+        if c0 < 128:
+            wlist(bk, c0, "ZO", x, 16 * (c1 - c0), 16 * c0)
         else:
-            wnat("ps3", 0, "ZO", "OS", w)
-        for a in (1, 2):
-            wnat("ps%d" % (5 + a), 0, "ZM", "RN", w, WW * a)
-        for a, z in enumerate(("ZM", "ZB", "ZR")):
-            if t == 1 or a == 2:
-                wnat("ps0", 32 * a, z, "GT", 32)
-        wnat("ps1", 0, "ZM", "ONT", 32)
+            wnat(bk, 128, "ZO", x, 32, V)
 
-        def err0():
-            tt(A("hx", 0, 32), A("ps4", 0, 32), A("TF", 0, 32), O.add)
-            tt(A("hx", 32, 64), A("ps4", 0, 32), A("OWL", 32 * t, 32 * t + 32), O.add)
-            ts(A("em"), A("TF", 0, 32), float(n), O.is_ge, 2048.0, O.mult)
-            ts(A("hy"), A("hx"), 2047, O.bitwise_and)
-            for x in range(2):
-                tt(A("hz", 32 * x, 32 * x + 32), A("hy", 32 * x, 32 * x + 32), A("em"), O.max)
-            copy(A("HX"), A("hz"))
-            for x in range(2):
-                scopy(A("DG", 512 * x, 512 * x + 512), IN("DT", 0, 2064, "HX", 32 * x, 32 * x + 32))
-
-        def err1(out):
-            mm("ps4", 0, 512, "IDN", "E2", True, False)
-            mm("ps4", 0, 512, "IDN", "DG", False, True, 512)
-            scopy(out, A("ps4"))
-
-        def err2():
-            tt(IN("E", 0, P, "TD", 0, 32), A("DG", 0, 512), A("E2"), O.add)
-
-        def entries():
-            ts(A("sp"), A("ps2", 0, 32), 0.0, O.is_gt)
-            tt(A("sq"), A("ps2", 0, 32), A("RSq"), O.mult)
-            tt(A("sp"), A("sp"), A("GOd"), O.mult)
-            tt(A("SNLf"), A("SNLf"), A("sq"), O.max)
-            tt(A("sp"), A("sp"), A("GOf"), O.add)
-            tt(A("sq"), A("ps2", 32, 64), A("RSn"), O.mult)
-            copy(A("GO1"), A("sp"))
-            send("GO1", 0, 16, "GI1", 0, "gi1")
-            for i, j in ((2, 6), (3, 7), (4, 0), (5, 1)):
-                dma("G", "d21", T[TAB][i::16, V:V + 512], T["GT"][j::16, 0:512], [("GT", 0, 512, j)], [(TAB, V, V + 512, i)])
-            tt(A("SN1"), A("sq"), A("SNI"), O.max)
-            copy(A("SNL"), A("SNLf"))
-            hilo(A("SH1"), A("SL1"), A("SN1"))
-            rows2("Y", "d24", SNDT, 16, 528, 0, "SH1", "SL1", 0, 32)
-
-        err0()
-        scopy(A("nw", 64 - 64 * t, 96), A("ps0", 64 - 64 * t, 96))
-        if t == 1:
-            err2()
-            dma("Y", "d30", T["ye"][:, 0:n], T["E"][:, 0:n], [("E", 0, n, None)], [])
-            err1(A("CR"))
-            dma("S", "d30", T["ye"][:, n:P], T["CR"][:], [("CR", 0, 512, None)], [])
-        pf = [A(PF, w * a, w * a + w) for a in range(3)]
-        px = [A("PX", w * a, w * a + w) for a in range(3)]
-        ps = [A("ps%d" % (5 + a), 0, w) for a in range(3)]
-
-        def finish(a):
-            ts(px[a], px[a], 4095, O.bitwise_and)
-            if a == 2:
-                tt(A("nw", 64, 96), A("ps1", 0, 32), A("nw", 64, 96), O.max)
-            if t == 0:
-                hilo(A("HI", w * a, w * a + w), A("LO", w * a, w * a + w), px[a])
-                rows2("YS", "d20", TAB, 0, V, (2, 4, 0)[a], "HI", "LO", a * w, a * w + w)
-                if a == 2:
-                    hilo(A("SH"), A("SL_"), A("nw", 64, 96))
-                    rows2("YS", "d20", TAB, V, V + 512, 0, "SH", "SL_", 0, 32)
-                return
-            y = ("yr", "yl", "yb")[a]
-            copy(A("PO", w * a, w * a + w), px[a])
-            b, o = loc("nw")
-            dma("S", "d31", T[y][:, n:P], T[b][:, o + 32 * a:o + 32 * a + 32], [("nw", 32 * a, 32 * a + 32, None)], [])
-            dma("Y", "d31", T[y][:, 0:n], T["PO"][:, a * w:a * w + w], [("PO", a * w, a * w + w, None)], [])
-
-        tt(A("OV", 0, w), A("ps3", 0, w), A("sg", 0, w), O.add)
-        copy(A("OV", w, 2 * w), A("ps3", 0, w))
-        tt(A("OV", 0, w), A("OV", 0, w), pf[0], O.max)
-        tt(A("da", 0, w), ps[0], A("eq2", 0, w), O.mult)
-        tt(A("db", 0, w), ps[0], A("eqb", 0, w), O.mult)
-        tt(px[0], ps[0], A("OV", 0, w), O.max)
-        tt(A("da", 0, w), A("da", 0, w), pf[1], O.max)
-        tt(A("db", 0, w), A("db", 0, w), pf[2], O.max)
-        if t == 0:
-            entries()
-        finish(0)
-        tt(A("dc", 0, w), ps[1], A("eq2", w, 2 * w), O.mult)
-        tt(ps[1], ps[1], A("da", 0, w), O.max)
-        tt(A("db", 0, w), A("db", 0, w), A("dc", 0, w), O.max)
-        ts(A("ql", 0, w), ps[1], 4096.0, O.add)
-        tt(px[1], ps[1], A("OV", w, 2 * w), O.max)
-        tt(A("dc", 0, w), A("ps3", 0, w), A("ql", 0, w), O.min)
-        tt(ps[2], ps[2], A("db", 0, w), O.max)
-        tt(px[2], ps[2], A("dc", 0, w), O.max)
-        finish(1)
-        finish(2)
-        if t == 0:
-            err2()
-            err1(A("E", V, V + 512))
-            scopy(A("BB10"), IN("E", 0, P, "SNL", 0, 32))
-            send("BB10", 0, 256, "E", P, "ga10")
-            ghost_bases(1)
+    def out(a, q):
+        y = ("yl", "yr", "yb")[a]
+        store(q[0], "d31", T[y][:, 0:V], "PO", 160 * a, 160 * a + 128)
+        store(q[1], "d31", T[y][:, V:n], "PO", 160 * a + 128, 160 * a + 160)
+    wlist("ps1", 0, "ZR", "GT", 512)
+    wnat("ps0", 0, "ZO", OS, 128)
+    wnat("ps0", 128, "ZO", OS, 32, V)
+    pull("OUTL", 0, 128, 160, scopy)
+    err0(1)
+    details(0)
+    details(1)
+    halves()
+    copy(A("TR"), A("ps1", 0, 32))
+    tile("ps5", "OUTL", 128, 160)
+    pull("OUTR", 1, 128, 160, copy)
+    tt(IN("E", 0, P, "TD", 0, 32), A("DG", 0, 512), A("E2"), O.add)
+    store("Y", "d30", T["ye"][:, 0:n], "E", 0, n)
+    scopy(A("ONT"), IN(OS, 0, G, "TR", 0, 32))
+    err1("ps4", A("CR"))
+    store("Y", "d30", T["ye"][:, n:P], "CR", 0, 512)
+    pull("OUTL", 0, 0, 128, scopy)
+    for a, z in enumerate(("ZB", "ZO", "ZR", "ZF")):
+        wnat("ps2", 32 * a, z, "GT", 32)
+    wnat("ps2", 128, "ZO", "ONT", 32)
+    tile("ps6", "OUTR", 128, 160)
+    tile("ps5", "OUTL", 0, 128)
+    pull("OUTB", 2, 128, 160, scopy)
+    pull("OUTB", 2, 0, 64, scopy)
+    pull("OUTB", 2, 64, 128, scopy)
+    CAP, CPS = W("ps3", 0, 160), W("ps3", 160, 160)
+    z0, z5, z6, z7 = [A("ps%d" % b, 0, 160) for b in (0, 5, 6, 7)]
+    ts(CAP, z0, 0.0, O.is_equal, BIG, O.mult)
+    ts(CPS, z0, 0.0, O.is_gt, BIG, O.mult)
+    tt(A("vs"), z0, A("SG2"), O.add)
+    for a in (1, 2):
+        tt(X2(a, 0, 160), CAP, X2(a, 0, 160), O.min)
+        tt(UR2(a, 0, 160), CAP, UR2(a, 0, 160), O.min)
+    tt(A("vs"), CPS, A("vs"), O.min)
+    copy(A("e2"), A("ps2", 96, 128))
+    copy(A("nw"), A("ps2", 0, 96))
+    tt(A("e2"), A("ps2", 128, 160), A("e2"), O.min)
+    tt(X2(1, 0, 160), X2(1, 0, 160), A("vs"), O.max)
+    tt(A("nw", 64, 96), A("nw", 64, 96), A("e2"), O.max)
+    for a, y in enumerate(("yl", "yr", "yb")):
+        store("Y", "d32", T[y][:, n:P], "nw", 32 * a, 32 * a + 32)
+    pull("OUTR", 1, 0, 64, copy)
+    tile("ps6", "OUTR", 0, 64)
+    tile("ps7", "OUTB", 128, 160)
+    tile("ps7", "OUTB", 0, 64)
+    tt(z5, z5, UR2(0, 0, 160), O.min)
+    tt(A("vn"), z5, X2(0, 0, 160), O.max)
+    tt(A("vs"), CAP, A("vn"), O.min)
+    tt(A("vn"), CPS, A("vn"), O.min)
+    tt(W("PO", 0, 160), z0, A("vs"), O.max)
+    tt(X2(2, 0, 160), X2(2, 0, 160), A("vn"), O.max)
+    out(0, "YY")
+    pull("OUTR", 1, 64, 128, copy)
+    tile("ps7", "OUTB", 64, 128)
+    tile("ps6", "OUTR", 64, 128)
+    tt(z7, z7, UR2(2, 0, 160), O.min)
+    tt(W("PO", 320, 160), z7, X2(2, 0, 160), O.max)
+    out(2, "YS")
+    tt(z6, z6, UR2(1, 0, 160), O.min)
+    tt(W("PO", 160, 160), z6, X2(1, 0, 160), O.max)
+    out(1, "YS")
     for d in sorted(dcount):
         wait("Y", (d, dcount[d], {}))
     for q in ("V", "S", "P", "G"):

@@ -3,11 +3,16 @@ from concourse.mybir import AluOpType as O, ActivationFunctionType as F
 
 V, P, G = 2048, 3072, 3584
 GH, PL, K, DW = 16, 528, 3104, 3120
+SL, SB, DUMP = 3072, 5632, 8192
 BIG = 16384.0
 JUMP = 4096.0 * 254
 bf, f4, i4, u2 = "bfloat16", "float32", "int32", "uint16"
 VPART = (1280, 1536)
 LB, RB, LM, RM, BM, BB = 0, 32, 64, 192, 320, 448
+CYCLE, GATHER, SCATTER = 0.00083, 1.3, 2.2
+WAKE, START, SLACK = 0.25, 1.4, 0.02
+ROOM, SPARE = 1.25, 0.2
+AHEAD = 400
 LN = 320
 
 
@@ -24,14 +29,14 @@ def _tiles():
     tiles = {
         i4: "IP 1 IG 1 II 1 IO 1 SNI 32 THI 1 WTI 1 hx 64 hy 64",
         f4: "pc 1 px 1 qf 1 g15 1 odf 1 one 1 bth 1 wtc 1 th2 1 OH 16 PS 8 ca 1 cb 1 s1 1 s2 1 ev 1 B16 16 BN 4 BC 2 wc 8 lowb 1 "
-            "IL 160 PHU 128 DUMPC 10 N2K 32 KL 16 KH 32 OWL 64 ILs 32 IS 32 UN 32 IDF 128 mA 128 mB 128 ones 160 sc 176 "
+            "IL 160 PHU 128 DUMPC 10 DUM 32 KH 32 OWL 64 ILs 32 IDF 128 mA 128 mB 128 ones 160 sc 176 "
             "NKU 320 CT 320 plc 320 isg 320 kg 320 UT 480 lo 320 tA 480 tB 480 UB 448 mBB 128 sg 160 sgb 160 ne 160 pre 160 sA 128 nLR 128 nLB 128 lo2 128 eRB 128 "
-            "RSq 32 RSn 32 GOf 32 GOd 32 alt 32 e2 32 PHS 32 sp 32 sq 32 SN1 32 UB2 320 LO2 320 vn 160 vs 160 N3 384 U2 384 pa 128 pb 128 "
-            "X2 480 UR2 480 U160 160 SG2 160 XF 480 UF 480 UL 160 PO 480 nw 96 TF 32 em 32 hz 64 yo 32 yk 16 z0 160 x0 160 v0 160 of 10",
-        bf: "ZA 143 ZR 143 ZL 143 ZB 143 ZO 143 ZP 143 ZV 143 ZW 143 ZN 143 ZC 143 ZF 143 ZG 143 ZE 143 ZX 143 ZQ 143 ZH 143 "
-            "BLK 128 TRI 128 ID2 128 IDN 128 N4K 128 BTH 128 SH 32 SL_ 32 SH1 32 SL1 32 go 160 nm 160 a0 160 val 160 thc 1 LOW 256 "
-            "UR 480 ye_ 32 cand 160 f2 128 GH_ 128 GL_ 128 U2R 128",
-        u2: "SNL 32 RAW 480 RAW2 480 GL 352 BL 160 TD 32 T0 16 TP 32 TR 32 HX 64 OFF 10 SP2 32",
+            "RSq 32 GOf 32 GOd 32 alt 32 e2 32 PHS 32 sp 32 sq 32 UB2 320 LO2 320 vn 160 vs 160 N3 384 mLR 128 pa 128 pb 128 "
+            "X2 480 EQ 480 U160 160 SG2 160 PO 480 nw 96 TF 32 yo 32 of 10 pd 128 e3 32 s3 32 v2 160 v3 160",
+        bf: "ZA 143 ZR 143 ZL 143 ZB 143 ZO 143 ZP 143 ZV 143 ZW 143 ZN 143 ZC 143 ZF 143 ZG 143 ZT 143 ZX 143 ZQ 143 ZH 143 "
+            "BLK 128 TRI 128 ID2 128 IDN 128 N4K 128 BTH 128 SH 32 SL_ 32 go 160 nm 160 a0 160 val 160 thc 1 LOW 256 "
+            "z0 160 UR 480 ye_ 32 cand 160 GH_ 128 GL_ 128",
+        u2: "SNL 32 RAW 480 GL 352 BL 160 TD 32 T0 16 TP 32 TR 32 HX 64 OFF 10 SP2 32",
     }
     for d, names in tiles.items():
         w = names.split()
@@ -43,9 +48,10 @@ def _tiles():
         SCRATCH["pk" + d] = _s(o, d)
     big = {
         i4: "XP 480",
-        bf: "HI 384 LO 384 TAB 3584 CG 512 SNDT 544 SND2 544 E 3072 D0 3120 D1 3120 D2 3120 D3 3120 D4 2560 M 2560 H 2560 FL 2560 FS 2560 AB 2560 AQ 512 "
-            "OUTL 2560 OUTR 2560 OUTB 2560 OBS 512 OSS 1024 ONS 512 OS0 3584 OS1 3584 ONE 512 CW0 416 CW1 416 VW0 416 VW1 416 CF 256 MM 256 "
-            "DR 2064 DG 1024 ET 512 E1 512 E2 512 CR 512 GT 512 G0 256 ONT 512 " + " ".join("BB%d%d 512" % (t, k) for t in range(2) for k in range(4)),
+        f4: "NW 512",
+        bf: "HI 384 LO 384 TAB 3600 CG 512 SNDT 544 SND2 544 E 3072 D0 3120 D1 3120 D2 3120 D3 3120 D4 2560 M 2560 H 2560 FL 2560 FS 2560 AB 2560 AQ 512 "
+            "OUTL 2048 OUTR 2048 OUTB 2560 OBS 512 OSS 1024 ONS 512 OS0 3584 OS1 3072 RN 8704 ONE 512 CW0 416 CW1 416 VW0 416 VW1 416 CF 256 MM 256 "
+            "DR 2048 DG 1024 ET 512 E1 512 E2 512 CR 512 GT 512 G0 256 ONT 512 " + " ".join("BB%d%d 512" % (t, k) for t in range(2) for k in range(4)),
         u2: "GO0 32 GO1 32 GI0 32 GI1 32",
     }
     for d, names in big.items():
@@ -60,6 +66,41 @@ def _tiles():
 
 _tiles()
 SEMAPHORES = ["sV", "sS", "sP", "sG", "sX", "gi0", "gi1"] + ["ga%d%d" % (t, k) for t in range(2) for k in range(4)] + ["d%d" % k for k in range(40)]
+
+
+ORDER = []
+
+
+def arrange(calls):
+    end, free, rings, todo = {}, {}, 0.0, list(range(len(calls)))
+    place = [i if c[6] else 1e6 + i for i, c in enumerate(calls)]
+    for i in reversed(todo):
+        for j in calls[i][3]:
+            place[j] = min(place[j], place[i] - 0.001)
+    while todo:
+        soon, best, first, ready = {}, None, {}, set()
+        for i in todo[:AHEAD]:
+            t = free.get(calls[i][0], 0.0)
+            ready.add(i)
+            for j, w in calls[i][3].items():
+                if j not in end:
+                    ready.discard(i)
+                    t = max(t, soon[j] + (calls[j][2] + WAKE if w else calls[j][1]))
+                elif w:
+                    t = max(t, end[j] + WAKE)
+            soon[i] = t
+        for i in sorted(soon, key=lambda i: place[i]):
+            q, t = calls[i][0], soon[i]
+            if i in ready and (best is None or t < soon[best] - 1e-9) and t + ROOM * calls[i][1] + (SPARE if t > free.get(q, 0.0) else 0.0) <= first.get(q, 1e9) + SLACK:
+                best = i
+            first[q] = min(first.get(q, 1e9), t)
+        q, busy, done = calls[best][:3]
+        end[best] = soon[best] + done
+        if done > busy + 1:
+            end[best] = rings = max(rings, soon[best] + START) + done - START
+        free[q] = soon[best] + busy
+        todo.remove(best)
+    return end
 
 
 def rank_program(g, core, T, topo):
@@ -85,30 +126,62 @@ def rank_program(g, core, T, topo):
             if seen[q].get(s, 0) < v:
                 seen[q][s] = v
 
-    def deps(q, reads, writes):
-        toks = []
+    def meets(book, q, reads, writes):
         for kind, regs in (("r", reads), ("w", writes)):
             for b, lo, hi, row in regs:
-                for rlo, rhi, rrow, rk, rq, tok in hist.get(b, []):
+                for rlo, rhi, rrow, rk, rq, tok in book.get(b, []):
+                    if rq == q == "P" and kind == "w":
+                        yield tok, False
+                        continue
                     if not (b.startswith("ps") and rq != q):
                         if rlo >= hi or lo >= rhi or (row is not None and rrow is not None and row != rrow):
                             continue
                         if rk == "r" and kind == "r":
                             continue
-                    if rq == q and q == "P" and kind == "w":
-                        continue
-                    toks.append(tok)
-        toks.sort(key=lambda t: -t[1])
-        for t in toks:
+                    yield tok, True
+
+    def deps(q, reads, writes):
+        for t in sorted((t for t, w in meets(hist, q, reads, writes) if w), key=lambda t: -t[1]):
             wait(q, t)
 
-    def note(q, reads, writes, tok):
+    def note(q, reads, writes, tok, book=hist):
         for kind, regs in (("w", writes), ("r", reads)):
             for b, lo, hi, row in regs:
-                h = hist.setdefault(b, [])
+                h = book.setdefault(b, [])
                 if kind == "w" and row is None:
                     h[:] = [r for r in h if not (lo <= r[0] and r[1] <= hi)]
                 h.append((lo, hi, row, kind, q, tok))
+
+    calls = []
+    plan, last, urgent = {}, {}, [True]
+
+    def aside(*parts):
+        urgent[0] = False
+        for f in parts:
+            f()
+        urgent[0] = True
+
+    def collect(q, busy, done, reads, writes, issue, batch=None, lands=(), after=()):
+        pre = {}
+        for j, w in list(meets(plan, q, reads, writes)) + list(meets(plan, "X", [], lands)) + [(j, True) for j in after]:
+            pre[j] = pre.get(j, False) or w
+        for j in list(pre):
+            if calls[j][4] and calls[j][4] != batch:
+                pre.update({i: True for i, c in enumerate(calls) if c[4] == calls[j][4]})
+        if batch or lands:
+            if q in last:
+                pre.setdefault(last[q], False)
+            last[q] = len(calls)
+        calls.append((q, busy, done, pre, batch, issue, urgent[0]))
+        note(q, reads, writes, len(calls) - 1, plan)
+        note("X", [], lands, len(calls) - 1, plan)
+        return len(calls) - 1
+
+    def issue_all():
+        if not ORDER:
+            ORDER.extend(arrange(calls))
+        for i in ORDER:
+            calls[i][5]()
 
     def loc(b):
         return PACK.get(b, (b, 0))
@@ -148,16 +221,34 @@ def rank_program(g, core, T, topo):
             return [(ob, oo + x[5], oo + x[6], None)]
         return []
 
-    def call(q, fn, outs, ins):
+    def cycles(q, outs, ins, two):
+        x = outs[0]
+        n = 16 * (x[6] - x[5]) if x[0] == "i" else len(range(x[2], x[3], x[4]))
+        ts_ = [y for y in outs + ins if isinstance(y, tuple)]
+        if x[0] == "i":
+            return 60 + SCATTER * n
+        if any(y[0] == "i" for y in ts_):
+            return 70 + GATHER * n
+        if q == "G":
+            return 160 + 2 * n
+        if two:
+            return max(64, n if any(y[1].startswith("ps") for y in ins) else 2 * n)
+        return max(64, n / 2 if q == "V" and all(SCRATCH[loc(y[1])[0]][2] in (bf, u2) for y in ts_) else n)
+
+    def call(q, fn, outs, ins, two=False, cost=None):
         reads = [r for x in ins for r in regs(x) + offs(x)] + [r for x in outs for r in offs(x)]
         writes = [r for x in outs for r in regs(x)]
-        deps(q, reads, writes)
-        sem = "s" + q
-        count[q] += 1
-        fn(eng[q]).then_inc(T.sem[sem], 1)
-        ck = dict(seen[q])
-        ck[sem] = count[q]
-        note(q, reads, writes, (sem, count[q], ck))
+
+        def issue():
+            deps(q, reads, writes)
+            sem = "s" + q
+            count[q] += 1
+            fn(eng[q]).then_inc(T.sem[sem], 1)
+            ck = dict(seen[q])
+            ck[sem] = count[q]
+            note(q, reads, writes, (sem, count[q], ck))
+        t = CYCLE * (cost or cycles(q, outs, ins, two))
+        collect(q, t, t, reads, writes, issue)
 
     def copy(out, in_):
         call("V", lambda e: e.tensor_copy(mk(out), mk(in_)), [out], [in_])
@@ -172,7 +263,7 @@ def rank_program(g, core, T, topo):
         call("V", lambda e: e.memset(mk(out), c), [out], [])
 
     def tt(out, a, b, op):
-        call("V", lambda e: e.tensor_tensor(mk(out), mk(a), mk(b), op), [out], [a, b])
+        call("V", lambda e: e.tensor_tensor(mk(out), mk(a), mk(b), op), [out], [a, b], True)
 
     def ts(out, a, s1, op0, s2=None, op1=None):
         if op1 is None:
@@ -193,14 +284,20 @@ def rank_program(g, core, T, topo):
         else:
             call("G", lambda e: e.iota(mk(out), pat, base, cm), [out], [])
 
-    def dma(q, bat, out, in_, rd, wr):
-        assert bat not in closed
+    def dma(q, bat, out, in_, rd, wr, after=None):
+        lo, hi = (rd + wr)[0][1:3]
         rd = [(loc(b)[0], loc(b)[1] + lo, loc(b)[1] + hi, row) for b, lo, hi, row in rd]
         wr = [(loc(b)[0], loc(b)[1] + lo, loc(b)[1] + hi, row) for b, lo, hi, row in wr]
-        deps(q, rd, wr)
-        eng[q].dma_start(out, in_).then_inc(T.sem[bat], 16)
-        dcount[bat] = dcount.get(bat, 0) + 16
-        note(q, rd, wr, (bat, dcount[bat], dict(seen[q])))
+
+        def issue():
+            assert bat not in closed
+            if after:
+                wait(q, (after[1], 2 * half, {}))
+            deps(q, rd, wr)
+            eng[q].dma_start(out, in_).then_inc(T.sem[bat], 16)
+            dcount[bat] = dcount.get(bat, 0) + 16
+            note(q, rd, wr, (bat, dcount[bat], dict(seen[q])))
+        collect(q, 0.1, START + (0.4 if hi - lo <= 512 else 2.0), rd, wr, issue, bat, after=after[:1] if after else ())
 
     def rows(q, bat, dst, lo, hi, row, tile, c0, c1):
         b, o = loc(tile)
@@ -211,9 +308,9 @@ def rank_program(g, core, T, topo):
         rows(q[0], bat, dst, lo, hi, row, th, c0, c1)
         rows(q[-1], bat, dst, lo, hi, row + 1, tl, c0, c1)
 
-    def load(q, bat, b, lo, hi, src):
+    def load(q, bat, b, lo, hi, src, after=None):
         bb, o = loc(b)
-        dma(q, bat, T[bb][:, o + lo:o + hi], src, [], [(b, lo, hi, None)])
+        dma(q, bat, T[bb][:, o + lo:o + hi], src, [], [(b, lo, hi, None)], after)
 
     def store(q, bat, dst, b, lo, hi):
         bb, o = loc(b)
@@ -235,7 +332,7 @@ def rank_program(g, core, T, topo):
                 rhs = T[sb][:, so + a:so + b] if st == 1 else T[sb][:, so + a:so + b:st]
                 i = e.matmul(T[bk][:, o:o + n], T[zb][:, zo + 15 - r:zo + 143 - r], rhs, first and r == 0, last and r == 15)
             return i
-        call("P", f, [W(bk, o, n)], [A(src, lo, hi)] + [A(x) for x in sorted(set(zs))])
+        call("P", f, [W(bk, o, n)], [A(src, lo, hi)] + [A(x) for x in sorted(set(zs))], cost=8 * max(64, n))
 
     def wlist(bk, o, z, src, n, lo=0, first=True, last=True):
         wrap(bk, o, n // 16, z, src, lambda r: (lo + r, lo + n, 16), first=first, last=last)
@@ -246,7 +343,8 @@ def rank_program(g, core, T, topo):
     def mm(bk, o, n, z, src, start=True, stop=True, s0=0):
         zb, zo = loc(z)
         sb, so = loc(src)
-        call("P", lambda e: e.matmul(T[bk][:, o:o + n], T[zb][:, zo:zo + 128], T[sb][:, so + s0:so + s0 + n], start, stop), [W(bk, o, n)], [A(z, 0, 128), A(src, s0, s0 + n)])
+        call("P", lambda e: e.matmul(T[bk][:, o:o + n], T[zb][:, zo:zo + 128], T[sb][:, so + s0:so + s0 + n], start, stop), [W(bk, o, n)], [A(z, 0, 128), A(src, s0, s0 + n)],
+             cost=max(64, n) * (2 if z == "IDF" else 0.5))
 
     def unmix(src, c0, c1, banks, stop=False):
         zb, zo = loc("ID2")
@@ -257,10 +355,11 @@ def rank_program(g, core, T, topo):
                     o = 128 * (r % 4)
                     i = e.matmul(T["ps%d" % b][:, o + c0:o + c1], T[zb][:, zo:zo + 128], T[src][:, 16 * c0 + r:16 * c1:16], False, stop and r % 4 == 3)
             return i
-        call("P", f, [A("ps%d" % b) for b in banks], [A(src, 16 * c0, 16 * c1), A("ID2")])
+        call("P", f, [A("ps%d" % b) for b in banks], [A(src, 16 * c0, 16 * c1), A("ID2")], cost=2 * len(banks) * (c1 - c0))
 
     nb = [T.cores[(rank - 1) % 4], T.cores[(rank + 1) % 4]]
     lsum = [0]
+    sent = {}
     half = len(topo.engines(core, nb[0])) // 2
 
     def send(src, w, dst, d0, sem):
@@ -273,9 +372,13 @@ def rank_program(g, core, T, topo):
             lsum[0] += h
             tr.append(RemoteDMATransfer(dst_ids=[DstId(rid=rid, pnc=pid)], dma_engine_mask=m, remote_sem=T.sem[sem],
                                         src=T[src][:, w * s:w * s + w], dst=T[dst][:, d0 + w * (1 - s):d0 + w * (1 - s) + w]))
-        deps("G", [(src, 0, 2 * w, None)], [])
-        g.remote_dma_fused(tr, local_sem=T.sem.sX)
-        note("X", [], [(dst, d0, d0 + 2 * w, None)], (sem, 2 * h, dict(seen["G"])))
+        rd, lands = [(src, 0, 2 * w, None)], [(dst, d0, d0 + 2 * w, None)]
+
+        def issue():
+            deps("G", rd, [])
+            g.remote_dma_fused(tr, local_sem=T.sem.sX)
+            note("X", [], lands, (sem, 2 * h, dict(seen["G"])))
+        sent[sem] = collect("G", 0.6, START + (3.5 if w > 16 else 2.5 if sent else 3.2), rd, [], issue, lands=lands)
 
     TAB, SNDT = "TAB", "SNDT"
     OH = lambda j: W("OH", j, 1)
@@ -313,39 +416,41 @@ def rank_program(g, core, T, topo):
     tt(A("PS"), A("OH", 0, 16, 2), A("OH", 1, 16, 2), O.add)
     ts(A("B16"), LOW(16), A("ca"), O.mult, A("cb"), O.add)
     for r in range(16):
-        slin(W(TAB, 128 * r, 128), LOW(128), A("s1"), W("B16", r, 1))
+        if r < 10:
+            slin(W(TAB, 128 * r, 128), LOW(128), A("s1"), W("B16", r, 1))
+        else:
+            ts(W(TAB, 128 * r, 128), LOW(128), A("s1"), O.mult, W("B16", r, 1), O.add)
     hilo(A("SH"), A("SL_"), A("SNI"))
     rows2("Y", "d5", SNDT, 16, 528, 4, "SH", "SL_", 0, 32)
     weights("ZB", PS(2))
     hilo(W("HI", 256, 128), W("LO", 256, 128), W("XP", BM, 128))
     rows2("Y", "d4", TAB, 0, V, 4, "HI", "LO", 256, 384)
     load("Y", "d6", "E", 0, V, T["err"][:])
-    ts(A("IO"), A("IP"), 1, O.bitwise_and)
-    ts(A("s2"), A("II"), 10.0, O.is_lt)
-    copy(A("odf"), A("IO"))
-    ts(A("ca"), A("qf"), 128.0, O.mult)
-    for o in (LM, RM, BM):
-        slin(W("UT", o, 128), LOW(128), 1.0, A("ca"))
-    slin(A("IL"), LOW(160), 16.0, A("qf"))
-    ts(A("ev"), A("odf"), -1.0, O.mult, A("s2"), O.add)
-    tt(A("s2"), A("s2"), A("odf"), O.mult)
-    ts(A("BN"), LOW(4), 256.0, O.mult, float(V), O.add)
-    ts(A("ev"), A("ev"), 0.0, O.max)
-    ts(A("BC"), LOW(2), 256.0, O.mult, GH + 4.0, O.add)
-    ts(A("BN"), A("BN"), A("ev"), O.mult, A("cb"), O.add)
-    ts(A("BC"), A("BC"), OH(8), O.mult)
-    copy(A("pc"), A("IP"))
-    weights("ZP", PS(4), "S")
-    for b in range(4):
-        slin(W(TAB, V + 256 * b, 256), LOW(256), A("s2"), W("BN", b, 1))
-    ts(W("wc", 0, 1), PS(2), float(K), O.mult, PS(4), O.add)
-    ts(A("IDF"), LOW(128), A("pc"), O.is_equal)
     hilo(W("HI", 0, 256), W("LO", 0, 256), W("XP", LM, 256))
-    gfill("E", V, P)
-    gfill("D0", PL + V, DW)
-    gfill("D1", PL + V, DW)
-    gfill("D2", PL + V, DW)
-    gfill("D3", PL + V, DW)
+
+    def consts_0():
+        ts(A("IO"), A("IP"), 1, O.bitwise_and)
+        ts(A("s2"), A("II"), 10.0, O.is_lt)
+        copy(A("odf"), A("IO"))
+        ts(A("px"), A("qf"), 128.0, O.mult)
+        for o in (LM, RM, BM):
+            slin(W("UT", o, 128), LOW(128), 1.0, A("px"))
+        slin(A("IL"), LOW(160), 16.0, A("qf"))
+        ts(A("ev"), A("odf"), -1.0, O.mult, A("s2"), O.add)
+        tt(A("s2"), A("s2"), A("odf"), O.mult)
+        ts(A("BN"), LOW(4), 256.0, O.mult, float(V), O.add)
+        ts(A("ev"), A("ev"), 0.0, O.max)
+        ts(A("BC"), LOW(2), 256.0, O.mult, GH + 4.0, O.add)
+        ts(A("BN"), A("BN"), A("ev"), O.mult, A("cb"), O.add)
+        ts(A("BC"), A("BC"), OH(8), O.mult)
+        for o, c in ((0, float(SL)), (2, BIG)):
+            ts(W("wc", 6 + o // 2, 1), OH(14), c, O.mult)
+            ts(W("BN", o, 2), W("BN", o, 2), W("wc", 6 + o // 2, 1), O.add)
+        copy(A("pc"), A("IP"))
+        for b in range(4):
+            slin(W(TAB, V + 256 * b, 256), LOW(256), A("s2"), W("BN", b, 1))
+        ts(W("wc", 0, 1), PS(2), float(K), O.mult, PS(4), O.add)
+        ts(A("IDF"), LOW(128), A("pc"), O.is_equal)
 
     def slotcol(out, src):
         ts(A(out, 0, 16), A(src[0], src[1], src[1] + 16), float(272 - P), O.add, 528.0, O.min)
@@ -353,48 +458,50 @@ def rank_program(g, core, T, topo):
 
     wlist("ps7", 0, "ZB", SNDT, 512, 16)
     copy(A("SNL"), A("ps7", 0, 32))
-    for o in (LB, RB, BB):
-        copy(W("UT", o, 32), A("ps7", 0, 32))
     copy(A("ONS"), IN(TAB, 0, V, "SNL", 0, 32))
     rows2("Y", "d7", TAB, 0, V, 0, "HI", "LO", 128, 256)
     rows2("Y", "d7", TAB, 0, V, 2, "HI", "LO", 0, 128)
     wlist("ps6", BB, "ZB", "ONS", 512)
-    slin(A("NKU"), A("UT", 0, 320), float(-K), 0.0)
-    weights("ZL", PS(1), "S")
-    weights("ZR", PS(0), "S")
-    weights("ZV", W("wc", 0, 1), "S")
     slotcol("GO0", ("ps6", BB))
     send("GO0", 16, "GI0", 0, "gi0")
     scopy(A("BB00"), IN("E", 0, V, "SNL", 0, 32))
     send("BB00", 256, "D0", GH, "ga00")
-    for s in range(2):
-        slin(W("CG", 256 * s, 256), LOW(256), OH(9), W("BC", s, 1))
-        slin(W("ILs", 16 * s, 16), A("IL", 0, 16), 1.0, float(P + 256 * s))
-    for b, c in (("ONE", 1), ("ones", 1), ("one", 1), ("SND2", -1), ("CW0", 0), ("VW0", -1), ("CW1", 0), ("VW1", -1)):
-        iota(A(b), [[0, WIDTH[b]]], 0, c, True)
-    iota(A("sc", 0, 1), [[0, 1]], 0, -1, True)
-    gfill("DR", 2048, 2064)
     load("Y", "d9", "THI", 0, 1, T["th"][:])
     load("Y", "d9", "WTI", 0, 1, T["wt"][:])
-    wlist("ps7", 0, "ZP", "ONS", 512)
+    consts_0()
+    for o in (LB, RB, BB):
+        scopy(W("UT", o, 32), A("ps7", 0, 32))
+    weights("ZL", PS(1), "S")
+    weights("ZR", PS(0), "S")
+    copy(A("OBS"), IN(TAB, 0, V, "SNL", 0, 32))
+    wlist("ps4", LB, "ZL", "OBS", 512)
+    wlist("ps4", RB, "ZR", "OBS", 512)
+    copy(A("RAW", 0, 64), A("ps4", 0, 64))
+    slin(A("NKU"), A("UT", 0, 320), float(-K), 0.0)
+    weights("ZV", W("wc", 0, 1), "S")
     mm("ps5", 0, 64, "IDF", "NKU", True, False)
-    ts(W("RAW", BB, 32), W("ps6", BB, 32), float(P - 1), O.min)
-    copy(W("XP", BB, 32), W("ps6", BB, 32))
-    copy(A("RAW", LM, BM), A("XP", LM, BM))
-    ts(W("RAW", BM, 128), W("XP", BM, 128), float(P - 1), O.min)
+    for s in range(2):
+        slin(W("CG", 256 * s, 256), LOW(256), OH(9), W("BC", s, 1))
+    gfill("D0", PL + V, DW)
     for k in range(4):
-        fill(A("D%d" % k, 0, GH), 0.0)
-    copy(A("PHS"), A("ps7", 0, 32))
+        gfill("D%d" % k, 0, GH)
     for r in range(16):
         copy(A("D0", PL + r, PL + V, 16), W("E", 128 * r, 128))
+    copy(A("RAW", LM, BM), A("XP", LM, BM))
+    ts(W("RAW", BM, 128), W("XP", BM, 128), float(P - 1), O.min)
+    ts(W("RAW", BB, 32), W("ps6", BB, 32), float(P - 1), O.min)
+    copy(W("XP", BB, 32), W("ps6", BB, 32))
+    copy(A("XP", 0, 64), A("ps4", 0, 64))
+    scopy(A("OUTB", 0, V), IN(TAB, 0, P, "RAW", BM, BB))
 
     def consts_a():
         ts(A("px"), A("qf"), 32.0, O.mult)
         ts(W("wc", 1, 1), PS(1), float(K), O.mult, PS(4), O.add)
-        ts(A("IS"), LOW(32), A("px"), O.add, float(P), O.add)
+        ts(A("U160", 128, 160), LOW(32), A("px"), O.add, float(V), O.add)
         weights("ZW", W("wc", 1, 1), "S")
-        slin(A("U160", 128, 160), A("IS"), 1.0, float(V - P))
         scopy(A("U160", 0, 128), W("UT", LM, 128))
+        for s in range(2):
+            slin(W("ILs", 16 * s, 16), A("IL", 0, 16), 1.0, float(P + 256 * s))
 
     def consts_b():
         copy(A("wtc"), A("WTI"))
@@ -419,8 +526,9 @@ def rank_program(g, core, T, topo):
         ts(W("wc", 3, 1), OH(10), -4096.0, O.mult, PS(2), O.add)
         ts(W("wc", 4, 1), OH(1), 4096.0, O.mult, OH(0), O.add)
         ts(A("lowb"), OH(1), 255.0, O.mult, -1.0, O.add)
+        tt(W("wc", 5, 1), OH(14), PS(6), O.add)
         for z, col in (("ZN", W("wc", 2, 1)), ("ZC", W("wc", 3, 1)), ("ZX", W("wc", 4, 1)), ("ZO", PS(3)), ("ZF", OH(11)), ("ZG", PS(6)),
-                       ("ZE", OH(14)), ("ZQ", A("qf"))):
+                       ("ZT", W("wc", 5, 1)), ("ZQ", A("qf"))):
             weights(z, col, "S")
         for z, c in (("IDN", 1.0), ("ID2", 2.0), ("N4K", -4096.0)):
             slin(A(z), A("IDF"), c, 0.0)
@@ -429,6 +537,7 @@ def rank_program(g, core, T, topo):
         ts(A("KH"), A("IL", 0, 32), A("odf"), O.subtract, 0.5, O.mult)
         for t in range(2):
             slin(W("OWL", 32 * t, 32), A("IL", 0, 32), 1.0, float(V + 512 * t))
+        slin(A("DUM"), A("IL", 0, 32), 1.0, float(DUMP))
 
     def given():
         tt(A("sg"), A("UT", BM, 480), A("XP", BM, 480), O.is_lt)
@@ -453,7 +562,6 @@ def rank_program(g, core, T, topo):
         tt(A("alt"), W("XP", LB, 32), A("e2"), O.add)
         slotcol("SP2", ("alt", 0))
         copy(A("GOd"), A("SP2"))
-        tt(A("GOd"), A("GOd"), A("GOf"), O.subtract)
 
     def given_s():
         slin(A("nLR"), A("nLR"), BIG, 0.0)
@@ -486,17 +594,13 @@ def rank_program(g, core, T, topo):
         tt(A("tB"), A("ps4", 0, 480), A("UT"), O.is_equal)
         ts(A("tA", 0, 448), A("ps6", 0, 448), float(K), O.is_lt)
         slin(A("UR"), A("tB"), BIG, 0.0)
-        slin(A("pa"), W("tB", BM, 128), -BIG, BIG)
         tt(A("pb"), A("PHU"), A("sA"), O.mult)
         tt(A("ps6", 0, 448), A("ps6", 0, 448), A("tA", 0, 448), O.mult)
-        slin(A("sA"), A("sA"), BIG, 0.0)
         rows("Y", "d11", TAB, 0, V, 11, "UR", RM, RM + 128)
 
     def found_c():
         tt(W("ps7", 0, 128), W("ps6", BM, 128), A("eRB"), O.mult)
-        tt(A("f2"), A("pa"), A("eRB"), O.mult)
         tt(W("ps7", 0, 128), W("ps7", 0, 128), A("pb"), O.add)
-        rows("Y", "d11", TAB, 0, V, 14, "f2", 0, 128)
         copy(A("GH_"), W("ps7", 0, 128))
         tt(A("GL_"), W("ps7", 0, 128), A("GH_"), O.subtract)
         rows2("Y", "d11", TAB, 0, V, 12, "GH_", "GL_", 0, 128)
@@ -505,6 +609,7 @@ def rank_program(g, core, T, topo):
         lambda: ts(A("ps7", 128, 448), A("ps5", 0, 320), float(K), O.is_lt),
         lambda: tt(A("tA", 0, 320), A("ps7", 128, 448), A("plc"), O.mult),
         lambda: tt(A("lo"), A("ps5", 0, 320), A("tA", 0, 320), O.mult),
+        lambda: ts(A("mLR"), W("ps6", RM, 128), 0.0, O.is_gt, BIG, O.mult),
         lambda: tt(A("ps6", 0, 448), A("ps6", 0, 448), A("UR", 0, 448), O.max),
         lambda: tt(A("UB", 0, 320), A("ps6", 0, 320), A("kg"), O.max),
         lambda: copy(W("UB", BM, 128), W("ps6", BM, 128)),
@@ -520,19 +625,6 @@ def rank_program(g, core, T, topo):
             f()
         del later[:k]
 
-    consts_a()
-    given()
-    copy(A("OBS"), IN(TAB, 0, V, "SNL", 0, 32))
-    scopy(A("OUTB", 0, V), IN(TAB, 0, P, "RAW", BM, BB))
-    wlist("ps4", LB, "ZL", "OBS", 512)
-    wlist("ps4", RB, "ZR", "OBS", 512)
-    wnat("ps4", 64, "ZR", "OBS", 32)
-    consts_c()
-    copy(A("RAW", 0, 64), A("ps4", 0, 64))
-    copy(A("XP", 0, 64), A("ps4", 0, 64))
-    found_pe(0)
-    consts_b()
-    tt(A("RSn"), A("ps4", 64, 96), A("IS"), O.is_equal)
     tt(A(TAB, P, G), IN(SNDT, 0, 544, "GI0", 0, 32), A("CG"), O.add)
     both("OSS", 0, TAB, G, "RAW", 0, 64, 32)
     wlist("ps5", 0, "ZV", "OSS", 1024, 0, False, True)
@@ -552,28 +644,28 @@ def rank_program(g, core, T, topo):
     def inner(t, k, at=None):
         cuts = (0, 32, 64, 96, 128) if k in (1, 2) else (0, 8, 32, 64, 96, 128)
         o = PL if k < 3 else 0
-        m = 0 if k in (1, 2) else 16
+        m = (16, 0, 0, 32)[k]
         for c0, c1 in zip(cuts, cuts[1:]):
             scopy(A("AB", 16 * c0, 16 * c1), IN(DB[k], 0, DW, "GL", RM + c0, RM + c1))
-        if t:
+        if t and m < 32:
             scopy(A(DB[k + 1], o + V + 16 * m, o + V + 512), IN(DB[k], 0, DW, "GL", LN + m, LN + 32))
-            if m:
-                copy(W(DB[k + 1], o + V, 16 * m), IN(DB[k], 0, DW, "GL", LN, LN + m))
+        if t and m:
+            copy(W(DB[k + 1], o + V, 16 * m), IN(DB[k], 0, DW, "GL", LN, LN + m))
         for c0, c1 in zip(cuts, cuts[1:]):
             tt(A(DB[k + 1], o + 16 * c0, o + 16 * c1), IN(DB[k], 0, DW, "GL", LM + c0, LM + c1), A("AB", 16 * c0, 16 * c1), O.max)
             if at and c1 == 64:
                 at()
 
-    def flags(t, k, q, part=3):
-        n = V + 512 * t
-        b = "FL" if q == "V" else "FS"
-        if part & 1 and q == "V":
-            ts(A(b, 0, n), W(DB[k], PL, n), A("thc"), O.is_ge, 256.0, O.mult)
-        if part & 1 and q == "S":
-            slin(A(b, 0, n), W(DB[k], PL, n), 256.0, A("bth"), F.Relu)
-        if part & 2:
-            unmix(b, 0, 128, range(4))
-            if t:
+    def flags(t, k, q):
+        b = "FL" if k % 2 else "FS"
+        for lo, hi in ((0, 1024), (1024, V), (V, V + 512))[:2 + t]:
+            if q == "V":
+                ts(A(b, lo, hi), A(DB[k], PL + lo, PL + hi), A("thc"), O.is_ge, 256.0, O.mult)
+            else:
+                slin(A(b, lo, hi), A(DB[k], PL + lo, PL + hi), 256.0, A("bth"), F.Relu)
+            if lo < V:
+                unmix(b, lo // 16, hi // 16, range(4))
+            else:
                 mm("ps4", 0, 512, "ID2", b, False, False, V)
 
     def opensums(t):
@@ -593,7 +685,7 @@ def rank_program(g, core, T, topo):
         if part & 2:
             mm(CNT[t], 0, nc, "N4K", "nm", True, False)
 
-    def select(t):
+    def select(t, rest=None):
         n = V + 512 * t
         nc = n // 16
         hh = VPART[t]
@@ -611,7 +703,8 @@ def rank_program(g, core, T, topo):
         parts = [(lo, min(lo + 512, n)) for lo in range(hh, n, 512)]
         for lo, hi in parts:
             scopy(A("AB", lo, hi), IN("H", 0, n, "BL", lo // 16, hi // 16))
-        copy(A("M", 0, hh), A("H", 0, hh))
+        for lo, hi in ((0, 1024), (1024, hh)):
+            copy(A("M", lo, hi), A("H", lo, hi))
         for lo, hi in ((0, 1024), (1024, hh)):
             tt(A("M", lo, hi), IN("H", 0, n, "BL", lo // 16, hi // 16), A("M", lo, hi), O.max)
         for i, (lo, hi) in enumerate(parts):
@@ -620,21 +713,23 @@ def rank_program(g, core, T, topo):
             slin(A("M", lo, hi), A("ps%d" % i, 0, hi - lo), 1.0, A("one"), F.Sign)
         wlist(CNT[t], 0, "ZA", "M", 1024, 0, False, False)
         wlist(CNT[t], 64, "ZA", "M", n - 1024, 1024, False, True)
-        meanwhile(2)
+        if rest:
+            rest()
         ts(A("go", 0, nc), A(CNT[t], 0, nc), 2.0, O.is_ge)
         mm("ps2", 0, nc, "BLK", "go")
         mm("ps3", 0, nc, "TRI", "go")
-        meanwhile(1)
-        ts(A("ps2", 256, 256 + nc), A("ps2", 0, nc), 0.0, O.is_equal, 4096.0, O.mult)
+        ts(A("z0", 0, nc), A("ps2", 0, nc), 0.0, O.is_equal, 256.0, O.mult)
         scan(A("sc", 1, nc + 1), A("ones", 0, nc), A("ps2", 0, nc), -1.0, O.mult, O.add)
+        wlist("ps0", 0, "ZA", "z0", nc, 0, True, False)
         tt(A("ps3", 0, nc), A("ps3", 0, nc), A("go", 0, nc), O.mult)
-        tt(A("x0", 0, nc), A("ps2", 256, 256 + nc), A("sc", 0, nc), O.add)
-        ts(A("a0", 0, nc), A("x0", 0, nc), 255.0, O.min, A("lowb"), O.max)
-        wlist("ps0", 0, "ZX", "a0", nc)
+        ts(A("a0", 0, nc), A("sc", 0, nc), 255.0, O.min, A("lowb"), O.max)
+        wlist("ps0", 0, "ZX", "a0", nc, 0, False, True)
         tt(A("val", 0, nc), A("ps3", 0, nc), A("sc", 0, nc), O.add)
-        ts(A("ye_"), A("KH"), W("sc", nc, 1), O.is_gt, -1.0, O.mult)
-        mm("ps1", 0, 32, "N4K", "ye_", True, False)
-        meanwhile(1)
+        ts(A("ye_", 0, 16), A("IL", 0, 16), W("sc", nc, 1), O.is_gt, -1.0, O.mult)
+        ts(A("yo"), A("KH"), W("sc", nc, 1), O.is_gt)
+        mm("ps2", 256, 16, "N4K", "ye_", True, False)
+        tt(A("yo"), A("yo"), W("OWL", 32 * t, 32), O.mult)
+        mm("ps1", 0, 32, "IDF", "yo", True, False)
         k = nc // 16
         tt(A("of", 0, k), A("ps0", 0, k), A("DUMPC", 0, k), O.min)
         ts(A("OFF", 0, k), A("of", 0, k), 1.0 - JUMP, O.add)
@@ -643,131 +738,140 @@ def rank_program(g, core, T, topo):
         copy(IN(vw, 0, 416, "OFF", 0, k), A("val", 0, nc))
         scan(A("CF"), A(cw, 0, 256), A(cw, 0, 256), 0.0, O.max, O.max)
         scan(A("ps3", 0, 256), A(vw, 0, 256), A(vw, 0, 256), -1.0, O.max, O.max)
-        wlist("ps2", 0, "ZA", "CF", 256, 0, True, False)
+        wlist("ps2", 256, "ZA", "CF", 256, 0, False, False)
         tt(A("MM"), A("ps3", 0, 256), LOW(256), O.is_equal)
-        wlist("ps2", 0, "ZQ", "MM", 256, 0, False, True)
-        meanwhile(1)
-        copy(A("T0"), A("ps2", 0, 16))
-        copy(A("G0"), IN(TAB, 0, P, "T0", 0, 16))
+        wlist("ps2", 256, "ZQ", "MM", 256, 0, False, True)
+        ts(A("T0"), A("ps2", 256, 272), float(G), O.min)
+        copy(A("G0"), IN(TAB, 0, G + 16, "T0", 0, 16))
         wrap("ps1", 0, 32, "ZO", "G0", lambda r: (r >> 1, 256, 8), "ZB", False, True)
-        meanwhile(9)
-        tt(A("TF"), A("ps1", 0, 32), W("OWL", 32 * t, 32), O.min)
-        copy(A("TD"), A("TF"))
-        scopy(A("ET"), IN("E", 0, P, "TD", 0, 32))
-        scopy(A("GT"), IN(TAB, 0, P, "TD", 0, 32))
+        copy(A("TD"), A("ps1", 0, 32))
+        copy(A("TF"), A("ps1", 0, 32))
+        for x, win in (("ET", "E"), ("GT", TAB)):
+            scopy(A(x), IN(win, 0, P, "TD", 0, 32))
         copy(IN("OS%d" % t, 0, P, "TD", 0, 32), W(TAB, n, 512))
-        wlist("ps4", 0, "ZH", "ET", 512)
 
     def err0(t):
-        n = V + 512 * t
         tt(A("hx", 0, 32), A("ps4", 0, 32), A("TF"), O.add)
         tt(A("hx", 32, 64), A("ps4", 0, 32), W("OWL", 32 * t, 32), O.add)
-        ts(A("em"), A("TF"), float(n), O.is_ge, 2048.0, O.mult)
         ts(A("hy"), A("hx"), 2047, O.bitwise_and)
-        for x in range(2):
-            tt(W("hz", 32 * x, 32), W("hy", 32 * x, 32), A("em"), O.max)
-        copy(A("HX"), A("hz"))
+        copy(A("HX"), A("hy"))
 
     def halves():
         ts(A("E1"), A("ET"), 0.5, O.mult, 127.8, O.add)
         ts(A("E2"), A("E1"), -256.0, O.add)
 
     def details(x):
-        slin(W("DG", 512 * x, 512), IN("DR", 0, 2064, "HX", 32 * x, 32 * x + 32), 0.5, 127.8)
+        slin(W("DG", 512 * x, 512), IN("DR", 0, V, "HX", 32 * x, 32 * x + 32), 0.5, 127.8)
 
     def err1(bk, out):
         mm(bk, 0, 512, "IDN", "E2", True, False)
         mm(bk, 0, 512, "IDN", "DG", False, True, 512)
-        scopy(out, A(bk))
+        scopy(out, A(bk), F.Relu)
 
     def levels(t, extra):
         for k in range(3):
             if k:
                 border(t, k)
-            extra(k, 0)
+            extra(k)
             inner(t, k)
-            extra(k, 1)
+            for j, q in ((), ((0, "S"), (1, "S")), ((2, "S"), (3, "V")))[k]:
+                flags(t, j, q)
+        extra(3)
 
     border(0, 0, "V")
-    gfill("OS0", 0, 1536)
+    for k in (1, 2, 3):
+        gfill("D%d" % k, PL + V, DW)
     mm("ps5", LM, 256, "IDF", "NKU", True, False, LM)
-    both("OUTL", 0, TAB, G, "RAW", LM, RM, LM + 64)
-    scopy(A("OUTB", V, V + 512), IN(TAB, 0, P, "RAW", BB, BB + 32))
-    wlist("ps5", RM, "ZV", "OUTR", V, 0, False, False)
-    wlist("ps5", LM, "ZV", "OUTL", V, 0, False, True)
-    found_0()
-    flags(0, 0, "V", 1)
+    def sides(win, z):
+        for c in range(0, 96, 16):
+            copy(W("OUTL", 16 * c, 256), IN(win, 0, G, "RAW", LM + c, LM + c + 16))
+        scopy(A("OUTL", 1536, V), IN(win, 0, G, "RAW", LM + 96, RM))
+        wlist("ps5", RM, z, "OUTR", V, 0, False, False)
+        wlist("ps5", LM, z, "OUTL", 1024, 0, False, False)
+        wlist("ps5", LM + 64, z, "OUTL", 1024, 1024, False, True)
+    sides(TAB, "ZV")
     ts(A("GL", LM, BM), A("ps5", LM, BM), float(K), O.min)
-    given_b()
 
-    def extra0(k, x):
-        if (k, x) == (0, 0):
+    def fills(t):
+        for b, c in (("CW%d" % t, 0), ("VW%d" % t, -1)):
+            iota(A(b), [[0, WIDTH[b]]], 0, c, True)
+        for c in range(0, P, 1024):
+            gfill("OS%d" % t, c, c + 1024)
+
+    def extra0(k):
+        if k == 1:
+            scopy(A("OUTB", V, V + 512), IN(TAB, 0, P, "RAW", BB, BB + 32))
+            weights("ZP", PS(4), "S")
+            wlist("ps7", 0, "ZP", "ONS", 512)
+            copy(A("PHS"), A("ps7", 0, 32))
+            consts_a()
+            iota(A("ONE"), [[0, 512]], 0, 1, True)
+            consts_c()
+            consts_b()
+            given()
+            found_pe(0)
+            found_0()
             found_pe(1)
             opensums(0)
-            flags(0, 0, "V", 2)
             found_pe(2)
-        if (k, x) == (0, 1):
-            given_s()
-        if (k, x) == (1, 0):
-            gfill("OS0", 1536, P)
             partners(0, 1)
-        if (k, x) == (1, 1):
-            flags(0, 1, "S")
+        if k == 2:
             found_a()
             partners(0, 6)
             found_c()
-        if (k, x) == (2, 0):
-            gfill("OS1", 0, 1792)
-        if (k, x) == (2, 1):
-            flags(0, 2, "S")
-            flags(0, 3, "V")
-            meanwhile(6)
+        if k == 3:
+            iota(A("SND2"), [[0, 544]], 0, -1, True)
+            rows2("Y", "d24", "SND2", 16, 528, 10, "SH", "SL_", 0, 32)
+            for b in ("ones", "one"):
+                iota(A(b), [[0, WIDTH[b]]], 0, 1, True)
+            iota(A("sc", 0, 1), [[0, 1]], 0, -1, True)
+            gfill(TAB, G, G + 16)
+            iota(A("E", V, P), [[0, P - V]], 0, -256, True)
+            fills(0)
     levels(0, extra0)
-    gfill("OS1", 1792, G)
-    wait("Y", ("ga03", 2 * half, {}))
-    load("Y", "d15", "DR", 0, 2048, T["det"][:])
+    load("Y", "d15", "DR", 0, 2048, T["det"][:], (sent["ga03"], "ga03"))
     select(0)
+    aside(given_b, given_s, lambda: meanwhile(99))
 
     OS = "OS0"
+    wlist("ps4", 0, "ZH", "ET", 512)
     scopy(A("ONS"), IN(OS, 0, P, "SNL", 0, 32))
-    wlist("ps1", 0, "ZP", "GT", 512)
     wlist("ps2", 0, "ZP", "ONS", 512)
-    wnat("ps3", 0, "ZO", "ONS", 32)
+    wlist("ps1", 0, "ZP", "GT", 512)
     err0(0)
-    details(1)
     details(0)
+    details(1)
     halves()
-    err1("ps4", W("D0", PL + V, 512))
     ts(A("TP"), A("ps1", 0, 32), float(-PL), O.add)
-    ts(A("sp"), A("ps2", 0, 32), 0.0, O.is_gt)
+    tt(A("sp"), A("ps2", 0, 32), A("GOd"), O.min)
+    tt(A("s3"), A("GOf"), A("ps2", 0, 32), O.subtract)
     tt(A("sq"), A("ps2", 0, 32), A("RSq"), O.mult)
-    tt(A("sp"), A("sp"), A("GOd"), O.mult)
+    tt(A("sp"), A("sp"), A("s3"), O.max)
     tt(A("sq"), A("sq"), A("PHS"), O.max)
-    tt(A("sp"), A("sp"), A("GOf"), O.add)
-    ts(A("SP2"), A("sq"), float(-PL), O.add)
     copy(A("GO1"), A("sp"))
     send("GO1", 16, "GI1", 0, "gi1")
-    tt(A("sq"), A("ps3", 0, 32), A("RSn"), O.mult)
-    tt(A("SN1"), A("sq"), A("SNI"), O.max)
-    hilo(A("SH1"), A("SL1"), A("SN1"))
-    rows2("Y", "d24", "SND2", 16, 528, 10, "SH1", "SL1", 0, 32)
     tt(IN("D0", PL, PL + V + 512, "TP", 0, 32), A("DG", 0, 512), A("E2"), O.add)
+    ts(A("SP2"), A("sq"), float(-PL), O.add)
+    err1("ps4", W("D0", PL + V, 512))
     scopy(A("BB10"), IN("D0", PL, PL + V + 512, "SP2", 0, 32))
     send("BB10", 256, "D0", GH, "ga10")
     wlist("ps1", 32, "ZR", "GT", 512)
     wnat("ps0", 0, "ZP", OS, 128)
-    for i, j in ((0, 6), (1, 7), (2, 4), (3, 5)):
+    for i, j in ((0, 6), (1, 7), (12, 6), (13, 7)):
         dma("Y", "d21", T[TAB][i::16, V:V + 512], T["GT"][j::16, 0:512], [("GT", 0, 512, j)], [(TAB, V, V + 512, i)])
     mm("ps7", 0, 64, "IDF", "CT", True, False)
     wlist("ps3", 0, "ZG", "GT", 512)
     mm("ps5", LM, 256, "IDF", "CT", True, False, LM)
     CAP, CPS = W("ps6", 384, 128), W("ps6", 256, 128)
-    ts(A("TR"), A("ps1", 32, 64), float(P - 1), O.min)
-    scopy(A("ONT"), IN(OS, 0, P, "TR", 0, 32))
-    scopy(A("OUTB", 0, 1024), IN(OS, 0, P, "RAW", BM, BM + 64))
-    for a, z in enumerate(("ZB", "ZO", "ZR", "ZF", "ZE")):
-        wnat("ps1", 32 * a, z, "GT", 32)
-    wnat("ps1", 160, "ZO", "ONT", 32)
+    def newtiles():
+        ts(A("TR"), A("ps1", 32, 64), float(P - 1), O.min)
+        scopy(A("ONT"), IN(OS, 0, P, "TR", 0, 32))
+        for a, z in enumerate(("ZB", "ZO", "ZR", "ZF")):
+            wnat("ps1", 32 * a, z, "GT", 32)
+        wnat("ps1", 160, "ZO", "ONT", 32)
+        for r in range(16):
+            copy(W("E", 128 * r, 128), A("D0", PL + r, PL + V, 16))
+        copy(W("E", V, 512), W("D0", PL + V, 512))
     for o in (LB, RB):
         ts(W("tA", o, 32), A("ps2", 0, 32), 0.0, O.is_equal, BIG, O.mult)
     tt(A("e2"), A("ps2", 0, 32), A("pre", 128, 160), O.add)
@@ -782,9 +886,6 @@ def rank_program(g, core, T, topo):
         tt(W("LO2", o, 128), CAP, W("lo", o, 128), O.min)
     copy(W("GL", LN, 32), A("ps3", 0, 32))
     tt(W("LO2", RM, 128), W("LO2", RM, 128), A("pa"), O.max)
-    for r in range(16):
-        copy(W("E", 128 * r, 128), A("D0", PL + r, PL + V, 16))
-    copy(W("E", V, 512), W("D0", PL + V, 512))
     both(OS, P, "SND2", 544, "GI1", 0, 32, 16)
     both("OSS", 0, OS, G, "RAW", 0, 64, 32)
     wlist("ps7", 0, "ZN", "OSS", 1024, 0, False, True)
@@ -796,13 +897,11 @@ def rank_program(g, core, T, topo):
         copy(A("GL", lo, hi), A(bk, lo, hi))
 
     X2 = lambda a, o=0, n=128: W("X2", 160 * a + o, n)
-    UR2 = lambda a, o=0, n=128: W("UR2", 160 * a + o, n)
     N3 = lambda a: W("N3", 128 * a, 128)
-    U2 = lambda a: W("U2", 128 * a, 128)
     T1, T2 = W("ps6", 0, 128), W("ps6", 128, 128)
 
     def renamed():
-        ts(A("tA", 0, 384), A("ps6", 0, 384), 0.0, O.is_le, BIG, O.mult)
+        ts(A("tA", 0, 128), A("ps6", 128, 256), 0.0, O.is_le, BIG, O.mult)
         tt(A("pa"), A("ps6", 256, 384), W("UB", BM, 128), O.min)
         tt(A("pb"), A("ps6", 0, 128), W("UB", LM, 128), O.min)
         tt(A("ps6", 0, 384), A("ps6", 0, 384), A("UR", LM, BB), O.min)
@@ -827,155 +926,152 @@ def rank_program(g, core, T, topo):
     def renamed2():
         tt(A("vs", 0, 128), A("vn", 0, 128), A("sg", 0, 128), O.add)
         tt(T2, CAP, N3(1), O.min)
-        tt(A("U2"), A("tA", 0, 384), A("UR", LM, BB), O.min)
+        tt(A("tA", 0, 128), CAP, A("tA", 0, 128), O.min)
         tt(T2, T2, A("vs", 0, 128), O.max)
-        tt(A("U2R"), CAP, U2(1), O.min)
         copy(W("HI", 128, 128), T2)
         copy(X2(1), T2)
         tt(W("LO", 128, 128), T2, W("HI", 128, 128), O.subtract)
-        rows("Y", "d22", TAB, 0, V, 11, "U2R", 0, 128)
         rows2("Y", "d22", TAB, 0, V, 0, "HI", "LO", 128, 256)
+
+    def target():
+        tt(T1, A("tA", 0, 128), A("mLR"), O.min)
+        tt(A("pa"), A("tA", 0, 128), W("UR", RM, 128), O.min)
+        ts(A("pd"), W("GL", RM, 128), float(PL), O.is_lt, BIG, O.mult)
+        copy(A("pb"), CPS)
+        slin(A("pa"), A("pa"), -1.0, BIG)
+        slin(A("pd"), A("pd"), 1.0, float(SB))
+        tt(A("pb"), T1, A("pb"), O.max)
+        tt(T1, A("pa"), A("pd"), O.min)
+        slin(A("pb"), A("pb"), -1.0, BIG + SL)
+        tt(A("pb"), T1, A("pb"), O.min)
+        tt(T2, T2, A("pb"), O.add)
+        copy(A("GH_"), T2)
+        tt(A("GL_"), T2, A("GH_"), O.subtract)
+        rows2("Y", "d25", TAB, 0, V, 12, "GH_", "GL_", 0, 128)
 
     def fresh():
         n1 = lambda a: W("ps1", 32 * a, 32)
         copy(A("e2"), n1(3))
-        copy(X2(0, 128, 32), n1(0))
-        copy(X2(1, 128, 32), n1(1))
+        scopy(X2(0, 128, 32), n1(0))
+        scopy(X2(1, 128, 32), n1(1))
         tt(A("sq"), n1(5), A("e2"), O.min)
-        ts(A("sp"), n1(5), 0.0, O.is_le, BIG, O.mult)
         tt(X2(2, 128, 32), n1(2), A("sq"), O.max)
-        tt(A("sp"), n1(3), A("sp"), O.min)
-        fill(UR2(0, 128, 32), BIG)
         tt(A("SG2", 128, 160), A("U160", 128, 160), X2(2, 128, 32), O.is_lt)
-        tt(UR2(2, 128, 32), n1(4), A("sp"), O.max)
-        fill(UR2(1, 128, 32), 0.0)
         ts(A("sq"), A("sq"), 0.0, O.max)
         hilo(A("SH"), A("SL_"), X2(2, 128, 32))
         tt(A("cand", 128, 160), A("sq"), A("SG2", 128, 160), O.min)
         rows2("Y", "d23", TAB, V, V + 512, 4, "SH", "SL_", 0, 32)
         rows("Y", "d23", TAB, V, V + 512, 10, "cand", 128, 160)
 
-    copy(A("OUTL", 0, 1024), IN(OS, 0, G, "RAW", LM, LM + 64))
     newlists("ps7", 0, 64)
     border(1, 0, "V")
-    scopy(A("OUTL", 1024, V), IN(OS, 0, G, "RAW", LM + 64, RM))
-    scopy(A("OUTB", 1024, V), IN(OS, 0, P, "RAW", BM + 64, BB))
-    wlist("ps5", RM, "ZN", "OUTR", V, 0, False, False)
-    wlist("ps5", LM, "ZN", "OUTL", V, 0, False, True)
-    for a, x in enumerate(("OUTL", "OUTR", "OUTB")):
-        wlist("ps6", 128 * a, "ZO", x, V)
-    fresh()
+    sides(OS, "ZN")
     newlists("ps5", LM, BM)
-    flags(1, 0, "V", 1)
-    opensums(1)
-    flags(1, 0, "V", 2)
 
-    later += [
-        lambda: tt(T1, CAP, N3(0), O.min),
-        lambda: tt(A("pb"), CAP, U2(2), O.min),
-        lambda: tt(X2(0), T1, A("vn", 0, 128), O.max),
-        lambda: tt(T1, U2(0), A("nLR"), O.min),
-        lambda: tt(UR2(0), CPS, U2(0), O.max),
-        lambda: tt(A("pa"), T1, A("sA"), O.max),
-        lambda: [copy(W("RAW2", 160 * a + 128, 32), W("ps7", 256 + 32 * a, 32)) for a in range(3)],
-        lambda: [tt(T1, CPS, A("pa"), O.min), copy(W("RAW2", 0, 128), X2(0)), tt(UR2(2), T1, A("pb"), O.max)],
-        lambda: [copy(W("RAW2", 160 * a, 128), X2(a)) for a in (1, 2)],
-    ]
+    def others():
+        for c in range(0, 128, 32):
+            scopy(W("OUTB", 16 * c, 512), IN(OS, 0, P, "RAW", BM + c, BM + c + 32))
+        newtiles()
+        for a, x in enumerate(("OUTL", "OUTR", "OUTB")):
+            wlist("ps6", 128 * a, "ZO", x, V)
+        fresh()
+        opensums(1)
 
-    def extra1(k, x):
-        if (k, x) == (1, 1):
-            flags(1, 1, "S")
+    XA = lambda a: X2(a, 0, 160)
+    EQ = lambda a: W("EQ", 160 * a, 160)
+
+    def alike():
+        tt(T1, CAP, N3(0), O.min)
+        tt(X2(0), T1, A("vn", 0, 128), O.max)
+        for a, (x, y) in enumerate(((1, 0), (1, 2), (0, 2))):
+            tt(EQ(a), XA(x), XA(y), O.is_equal)
+        slin(A("SG2"), A("SG2"), 2.0, -1.0)
+
+    def extra1(k):
+        if k == 1:
+            others()
+        if k == 2:
             renamed()
-        if (k, x) == (2, 1):
             partners(1, 1)
-            for a, z in enumerate(("ZL", "ZR", "ZB")):
-                wlist("ps7", 256 + 32 * a, z, TAB, 512, V)
-            flags(1, 2, "S")
-            flags(1, 3, "V")
-            partners(1, 6)
+        if k == 3:
             renamed2()
-            slin(UR2(1), A("U2R"), 1.0, 0.0)
-            slin(A("SG2"), A("SG2"), 2.0, -1.0)
-            meanwhile(4)
+            aside(lambda: partners(1, 6), target, alike)
+            fills(1)
+            for c in range(0, DUMP + 512, 1088):
+                gfill("RN", c, c + 1088)
     levels(1, extra1)
     select(1)
 
-    OS = "OS1"
     n = V + 512
-    def pull(x, a, c0, c1, f):
-        f(A(x, 16 * c0, 16 * c1), IN(OS, 0, G, "RAW2", 160 * a + c0, 160 * a + c1))
 
-    def tile(bk, x, c0, c1):
-        if c0 < 128:
-            wlist(bk, c0, "ZO", x, 16 * (c1 - c0), 16 * c0)
-        else:
-            wnat(bk, 128, "ZO", x, 32, V)
+    def tile(bk, x, o):
+        wnat(bk, 0, "ZO", x, 128, o)
+        wnat(bk, 128, "ZO", x, 32, o + V)
 
     def out(a, q):
         y = ("yl", "yr", "yb")[a]
-        store(q[0], "d31", T[y][:, 0:V], "PO", 160 * a, 160 * a + 128)
-        store(q[1], "d31", T[y][:, V:n], "PO", 160 * a + 128, 160 * a + 160)
-    wlist("ps1", 0, "ZR", "GT", 512)
-    wnat("ps0", 0, "ZO", OS, 128)
-    wnat("ps0", 128, "ZO", OS, 32, V)
-    pull("OUTL", 0, 128, 160, scopy)
+        store(q, "d31", T[y][:, 0:V], "PO", 160 * a, 160 * a + 128)
+        store("S", "d31", T[y][:, V:n], "PO", 160 * a + 128, 160 * a + 160)
+
+    def row(bk, r, z, src, start, stop):
+        zb, zo = loc(z)
+        call("P", lambda e: e.matmul(T[bk][:, 0:512], T[zb][:, zo + 15 - r:zo + 143 - r], T[src][:, 0:512], start, stop), [A(bk)], [A(z), A(src)], cost=256)
+    wlist("ps4", 0, "ZH", "ET", 512)
+    wlist("ps1", 0, "ZT", "GT", 512)
     err0(1)
+    tt(A("e3"), A("ps1", 0, 32), A("DUM"), O.min)
+    copy(A("TR"), A("e3"))
     details(0)
     details(1)
     halves()
-    copy(A("TR"), A("ps1", 0, 32))
-    tile("ps5", "OUTL", 128, 160)
-    pull("OUTR", 1, 128, 160, copy)
+    copy(IN("RN", 0, DUMP + 512, "TR", 0, 32), W(TAB, n, 512))
     tt(IN("E", 0, P, "TD", 0, 32), A("DG", 0, 512), A("E2"), O.add)
     store("Y", "d30", T["ye"][:, 0:n], "E", 0, n)
-    scopy(A("ONT"), IN(OS, 0, G, "TR", 0, 32))
+    tile("ps0", "OS1", 0)
+    for a, z in enumerate(("ZB", "ZO", "ZR")):
+        row("ps2", a, z, "GT", a == 0, a == 2)
+    scopy(A("ONT"), IN("RN", 0, P, "TD", 0, 32))
+    tile("ps6", "RN", 0)
     err1("ps4", A("CR"))
     store("Y", "d30", T["ye"][:, n:P], "CR", 0, 512)
-    pull("OUTL", 0, 0, 128, scopy)
-    for a, z in enumerate(("ZB", "ZO", "ZR", "ZF")):
-        wnat("ps2", 32 * a, z, "GT", 32)
-    wnat("ps2", 128, "ZO", "ONT", 32)
-    tile("ps6", "OUTR", 128, 160)
-    tile("ps5", "OUTL", 0, 128)
-    pull("OUTB", 2, 128, 160, scopy)
-    pull("OUTB", 2, 0, 64, scopy)
-    pull("OUTB", 2, 64, 128, scopy)
-    CAP, CPS = W("ps3", 0, 160), W("ps3", 160, 160)
+    scopy(A("NW"), A("ps2"))
+    tile("ps5", "RN", SL)
+    row("ps1", 2, "ZO", "ONT", True, True)
+    tile("ps7", "RN", SB)
+    CAP, CPS, T1 = W("ps3", 0, 160), W("ps3", 160, 160), W("ps3", 320, 160)
     z0, z5, z6, z7 = [A("ps%d" % b, 0, 160) for b in (0, 5, 6, 7)]
-    ts(CAP, z0, 0.0, O.is_equal, BIG, O.mult)
+    ts(A("v2"), z0, 0.0, O.is_equal, BIG, O.mult)
     ts(CPS, z0, 0.0, O.is_gt, BIG, O.mult)
     tt(A("vs"), z0, A("SG2"), O.add)
-    for a in (1, 2):
-        tt(X2(a, 0, 160), CAP, X2(a, 0, 160), O.min)
-        tt(UR2(a, 0, 160), CAP, UR2(a, 0, 160), O.min)
+    ts(CAP, z0, 0.0, O.is_equal, BIG, O.mult)
     tt(A("vs"), CPS, A("vs"), O.min)
-    copy(A("e2"), A("ps2", 96, 128))
-    copy(A("nw"), A("ps2", 0, 96))
-    tt(A("e2"), A("ps2", 128, 160), A("e2"), O.min)
-    tt(X2(1, 0, 160), X2(1, 0, 160), A("vs"), O.max)
-    tt(A("nw", 64, 96), A("nw", 64, 96), A("e2"), O.max)
+    tt(T1, CAP, XA(1), O.min)
+    tt(XA(2), CAP, XA(2), O.min)
+    tt(XA(1), T1, A("vs"), O.max)
+    tt(EQ(0), z6, EQ(0), O.mult)
+    tt(EQ(1), z6, EQ(1), O.mult)
+    tt(z6, z6, A("v2"), O.min)
+    tt(T1, EQ(0), XA(0), O.max)
+    tt(W("PO", 160, 160), z6, XA(1), O.max)
+    out(1, "Y")
+    copy(A("vn"), T1)
+    tt(A("NW"), A("ps1"), A("NW"), O.max)
     for a, y in enumerate(("yl", "yr", "yb")):
-        store("Y", "d32", T[y][:, n:P], "nw", 32 * a, 32 * a + 32)
-    pull("OUTR", 1, 0, 64, copy)
-    tile("ps6", "OUTR", 0, 64)
-    tile("ps7", "OUTB", 128, 160)
-    tile("ps7", "OUTB", 0, 64)
-    tt(z5, z5, UR2(0, 0, 160), O.min)
-    tt(A("vn"), z5, X2(0, 0, 160), O.max)
+        dma("S", "d32", T[y][:, n:P], T["NW"][a::16, 0:512], [("NW", 0, 512, None)], [])
+    tt(EQ(2), z5, EQ(2), O.mult)
+    tt(A("vn"), z5, A("vn"), O.max)
+    tt(T1, EQ(1), EQ(2), O.max)
     tt(A("vs"), CAP, A("vn"), O.min)
-    tt(A("vn"), CPS, A("vn"), O.min)
+    tt(A("v3"), CPS, A("vn"), O.min)
+    tt(T1, T1, A("v2"), O.min)
     tt(W("PO", 0, 160), z0, A("vs"), O.max)
-    tt(X2(2, 0, 160), X2(2, 0, 160), A("vn"), O.max)
-    out(0, "YY")
-    pull("OUTR", 1, 64, 128, copy)
-    tile("ps7", "OUTB", 64, 128)
-    tile("ps6", "OUTR", 64, 128)
-    tt(z7, z7, UR2(2, 0, 160), O.min)
-    tt(W("PO", 320, 160), z7, X2(2, 0, 160), O.max)
-    out(2, "YS")
-    tt(z6, z6, UR2(1, 0, 160), O.min)
-    tt(W("PO", 160, 160), z6, X2(1, 0, 160), O.max)
-    out(1, "YS")
+    out(0, "Y")
+    tt(T1, T1, XA(2), O.max)
+    tt(z7, z7, A("v2"), O.min)
+    tt(A("v3"), T1, A("v3"), O.max)
+    tt(W("PO", 320, 160), z7, A("v3"), O.max)
+    out(2, "Y")
+    issue_all()
     for d in sorted(dcount):
         wait("Y", (d, dcount[d], {}))
     for q in ("V", "S", "P", "G"):

from concourse.bass import DstId, RemoteDMATransfer
from concourse.mybir import AluOpType as O, ActivationFunctionType as F

V, P, G = 2048, 3072, 3584
GH, PL, K, DW = 16, 528, 3104, 3120
SL, SB, DUMP = 3072, 5632, 8192
BIG = 16384.0
JUMP = 4096.0 * 254
bf, f4, i4, u2 = "bfloat16", "float32", "int32", "uint16"
VPART = (1280, 1536)
LB, RB, LM, RM, BM, BB = 0, 32, 64, 192, 320, 448
CYCLE, GATHER, SCATTER = 0.00083, 1.3, 2.2
WAKE, START, SLACK = 0.25, 1.4, 0.02
ROOM, SPARE = 1.25, 0.2
AHEAD = 400
LN = 320


def _s(n, d):
    return ("sbuf", [128, n], d)


SCRATCH = {}
PACK = {}
WIDTH = {}


def _tiles():
    tiles = {
        i4: "IP 1 IG 1 II 1 IO 1 SNI 32 THI 1 WTI 1 hx 64 hy 64",
        f4: "pc 1 px 1 qf 1 g15 1 odf 1 one 1 bth 1 wtc 1 th2 1 OH 16 PS 8 ca 1 cb 1 s1 1 s2 1 ev 1 B16 16 BN 4 BC 2 wc 8 lowb 1 "
            "IL 160 PHU 128 DUMPC 10 DUM 32 KH 32 OWL 64 ILs 32 IDF 128 mA 128 mB 128 ones 160 sc 176 "
            "NKU 320 CT 320 plc 320 isg 320 kg 320 UT 480 lo 320 tA 480 tB 480 UB 448 mBB 128 sg 160 sgb 160 ne 160 pre 160 sA 128 nLR 128 nLB 128 lo2 128 eRB 128 "
            "RSq 32 GOf 32 GOd 32 alt 32 e2 32 PHS 32 sp 32 sq 32 UB2 320 LO2 320 vn 160 vs 160 N3 384 mLR 128 pa 128 pb 128 "
            "X2 480 EQ 480 U160 160 SG2 160 PO 480 nw 96 TF 32 yo 32 of 10 pd 128 e3 32 s3 32 v2 160 v3 160",
        bf: "ZA 143 ZR 143 ZL 143 ZB 143 ZO 143 ZP 143 ZV 143 ZW 143 ZN 143 ZC 143 ZF 143 ZG 143 ZT 143 ZX 143 ZQ 143 ZH 143 "
            "BLK 128 TRI 128 ID2 128 IDN 128 N4K 128 BTH 128 SH 32 SL_ 32 go 160 nm 160 a0 160 val 160 thc 1 LOW 256 "
            "z0 160 UR 480 ye_ 32 cand 160 GH_ 128 GL_ 128",
        u2: "SNL 32 RAW 480 GL 352 BL 160 TD 32 T0 16 TP 32 TR 32 HX 64 OFF 10 SP2 32",
    }
    for d, names in tiles.items():
        w = names.split()
        o = 0
        for k, n in zip(w[0::2], w[1::2]):
            PACK[k] = ("pk" + d, o)
            WIDTH[k] = int(n)
            o += (int(n) + 15) // 16 * 16
        SCRATCH["pk" + d] = _s(o, d)
    big = {
        i4: "XP 480",
        f4: "NW 512",
        bf: "HI 384 LO 384 TAB 3600 CG 512 SNDT 544 SND2 544 E 3072 D0 3120 D1 3120 D2 3120 D3 3120 D4 2560 M 2560 H 2560 FL 2560 FS 2560 AB 2560 AQ 512 "
            "OUTL 2048 OUTR 2048 OUTB 2560 OBS 512 OSS 1024 ONS 512 OS0 3584 OS1 3072 RN 8704 ONE 512 CW0 416 CW1 416 VW0 416 VW1 416 CF 256 MM 256 "
            "DR 2048 DG 1024 ET 512 E1 512 E2 512 CR 512 GT 512 G0 256 ONT 512 " + " ".join("BB%d%d 512" % (t, k) for t in range(2) for k in range(4)),
        u2: "GO0 32 GO1 32 GI0 32 GI1 32",
    }
    for d, names in big.items():
        w = names.split()
        for k, n in zip(w[0::2], w[1::2]):
            WIDTH[k] = int(n)
            SCRATCH[k] = _s(int(n), d)
    for k in range(8):
        WIDTH["ps%d" % k] = 512
        SCRATCH["ps%d" % k] = ("psum", [128, 512], f4)


_tiles()
SEMAPHORES = ["sV", "sS", "sP", "sG", "sX", "gi0", "gi1"] + ["ga%d%d" % (t, k) for t in range(2) for k in range(4)] + ["d%d" % k for k in range(40)]


ORDER = []


def arrange(calls):
    end, free, rings, todo = {}, {}, 0.0, list(range(len(calls)))
    place = [i if c[6] else 1e6 + i for i, c in enumerate(calls)]
    for i in reversed(todo):
        for j in calls[i][3]:
            place[j] = min(place[j], place[i] - 0.001)
    while todo:
        soon, best, first, ready = {}, None, {}, set()
        for i in todo[:AHEAD]:
            t = free.get(calls[i][0], 0.0)
            ready.add(i)
            for j, w in calls[i][3].items():
                if j not in end:
                    ready.discard(i)
                    t = max(t, soon[j] + (calls[j][2] + WAKE if w else calls[j][1]))
                elif w:
                    t = max(t, end[j] + WAKE)
            soon[i] = t
        for i in sorted(soon, key=lambda i: place[i]):
            q, t = calls[i][0], soon[i]
            if i in ready and (best is None or t < soon[best] - 1e-9) and t + ROOM * calls[i][1] + (SPARE if t > free.get(q, 0.0) else 0.0) <= first.get(q, 1e9) + SLACK:
                best = i
            first[q] = min(first.get(q, 1e9), t)
        q, busy, done = calls[best][:3]
        end[best] = soon[best] + done
        if done > busy + 1:
            end[best] = rings = max(rings, soon[best] + START) + done - START
        free[q] = soon[best] + busy
        todo.remove(best)
    return end


def rank_program(g, core, T, topo):
    rank = T.rank_of(core)
    if rank is None:
        return
    eng = {"V": g.vector, "S": g.scalar, "P": g.tensor, "G": g, "Y": g.sync}
    count = {"V": 0, "S": 0, "P": 0, "G": 0}
    seen = {q: {} for q in eng}
    hist = {}
    dcount = {}
    closed = set()

    def wait(q, tok):
        sem, val, clock = tok
        if sem in dcount:
            val = dcount[sem]
            closed.add(sem)
        if seen[q].get(sem, 0) < val:
            eng[q].wait_ge(T.sem[sem], val)
            seen[q][sem] = val
        for s, v in clock.items():
            if seen[q].get(s, 0) < v:
                seen[q][s] = v

    def meets(book, q, reads, writes):
        for kind, regs in (("r", reads), ("w", writes)):
            for b, lo, hi, row in regs:
                for rlo, rhi, rrow, rk, rq, tok in book.get(b, []):
                    if rq == q == "P" and kind == "w":
                        yield tok, False
                        continue
                    if not (b.startswith("ps") and rq != q):
                        if rlo >= hi or lo >= rhi or (row is not None and rrow is not None and row != rrow):
                            continue
                        if rk == "r" and kind == "r":
                            continue
                    yield tok, True

    def deps(q, reads, writes):
        for t in sorted((t for t, w in meets(hist, q, reads, writes) if w), key=lambda t: -t[1]):
            wait(q, t)

    def note(q, reads, writes, tok, book=hist):
        for kind, regs in (("w", writes), ("r", reads)):
            for b, lo, hi, row in regs:
                h = book.setdefault(b, [])
                if kind == "w" and row is None:
                    h[:] = [r for r in h if not (lo <= r[0] and r[1] <= hi)]
                h.append((lo, hi, row, kind, q, tok))

    calls = []
    plan, last, urgent = {}, {}, [True]

    def aside(*parts):
        urgent[0] = False
        for f in parts:
            f()
        urgent[0] = True

    def collect(q, busy, done, reads, writes, issue, batch=None, lands=(), after=()):
        pre = {}
        for j, w in list(meets(plan, q, reads, writes)) + list(meets(plan, "X", [], lands)) + [(j, True) for j in after]:
            pre[j] = pre.get(j, False) or w
        for j in list(pre):
            if calls[j][4] and calls[j][4] != batch:
                pre.update({i: True for i, c in enumerate(calls) if c[4] == calls[j][4]})
        if batch or lands:
            if q in last:
                pre.setdefault(last[q], False)
            last[q] = len(calls)
        calls.append((q, busy, done, pre, batch, issue, urgent[0]))
        note(q, reads, writes, len(calls) - 1, plan)
        note("X", [], lands, len(calls) - 1, plan)
        return len(calls) - 1

    def issue_all():
        if not ORDER:
            ORDER.extend(arrange(calls))
        for i in ORDER:
            calls[i][5]()

    def loc(b):
        return PACK.get(b, (b, 0))

    def A(b, lo=None, hi=None, st=1):
        if lo is None:
            lo, hi = 0, WIDTH[b]
        return ("a", b, lo, hi, st)

    def W(b, lo, n):
        return ("a", b, lo, lo + n, 1)

    def IN(b, lo, hi, ob, c0, c1):
        return ("i", b, lo, hi, ob, c0, c1)

    def mk(x):
        if not isinstance(x, tuple):
            return x
        b, o = loc(x[1])
        if x[0] == "a":
            if x[4] == 1:
                return T[b][:, o + x[2]:o + x[3]]
            return T[b][:, o + x[2]:o + x[3]:x[4]]
        ob, oo = loc(x[4])
        return T[b][:, o + x[2]:o + x[3]].indirect(T[ob][:, oo + x[5]:oo + x[6]])

    def regs(x):
        if not isinstance(x, tuple):
            return []
        b, o = loc(x[1])
        step = x[0] == "a" and x[4] == 16 and ("step", (o + x[2]) % 16)
        return [(b, o + x[2], o + x[3], step or None)]

    def offs(x):
        if isinstance(x, tuple) and x[0] == "i":
            ob, oo = loc(x[4])
            return [(ob, oo + x[5], oo + x[6], None)]
        return []

    def cycles(q, outs, ins, two):
        x = outs[0]
        n = 16 * (x[6] - x[5]) if x[0] == "i" else len(range(x[2], x[3], x[4]))
        ts_ = [y for y in outs + ins if isinstance(y, tuple)]
        if x[0] == "i":
            return 60 + SCATTER * n
        if any(y[0] == "i" for y in ts_):
            return 70 + GATHER * n
        if q == "G":
            return 160 + 2 * n
        if two:
            return max(64, n if any(y[1].startswith("ps") for y in ins) else 2 * n)
        return max(64, n / 2 if q == "V" and all(SCRATCH[loc(y[1])[0]][2] in (bf, u2) for y in ts_) else n)

    def call(q, fn, outs, ins, two=False, cost=None):
        reads = [r for x in ins for r in regs(x) + offs(x)] + [r for x in outs for r in offs(x)]
        writes = [r for x in outs for r in regs(x)]

        def issue():
            deps(q, reads, writes)
            sem = "s" + q
            count[q] += 1
            fn(eng[q]).then_inc(T.sem[sem], 1)
            ck = dict(seen[q])
            ck[sem] = count[q]
            note(q, reads, writes, (sem, count[q], ck))
        t = CYCLE * (cost or cycles(q, outs, ins, two))
        collect(q, t, t, reads, writes, issue)

    def copy(out, in_):
        call("V", lambda e: e.tensor_copy(mk(out), mk(in_)), [out], [in_])

    def scopy(out, in_, f=F.Copy):
        call("S", lambda e: e.activation(mk(out), mk(in_), f), [out], [in_])

    def slin(out, in_, scale, bias, f=F.Identity):
        call("S", lambda e: e.activation(mk(out), mk(in_), f, bias=mk(bias), scale=mk(scale)), [out], [in_, scale, bias])

    def fill(out, c):
        call("V", lambda e: e.memset(mk(out), c), [out], [])

    def tt(out, a, b, op):
        call("V", lambda e: e.tensor_tensor(mk(out), mk(a), mk(b), op), [out], [a, b], True)

    def ts(out, a, s1, op0, s2=None, op1=None):
        if op1 is None:
            call("V", lambda e: e.tensor_scalar(mk(out), mk(a), mk(s1), None, op0), [out], [a, s1])
        else:
            call("V", lambda e: e.tensor_scalar(mk(out), mk(a), mk(s1), mk(s2), op0, op1), [out], [a, s1, s2])

    def scan(out, d0, d1, init, op0, op1):
        call("V", lambda e: e.tensor_tensor_scan(mk(out), mk(d0), mk(d1), init, op0, op1), [out], [d0, d1])

    def hilo(hi, lo, x):
        copy(hi, x)
        tt(lo, x, hi, O.subtract)

    def iota(out, pat, cm, base=0, flag=False):
        if flag:
            call("G", lambda e: e.iota(mk(out), pat, base, cm, allow_small_or_imprecise_dtypes=True), [out], [])
        else:
            call("G", lambda e: e.iota(mk(out), pat, base, cm), [out], [])

    def dma(q, bat, out, in_, rd, wr, after=None):
        lo, hi = (rd + wr)[0][1:3]
        rd = [(loc(b)[0], loc(b)[1] + lo, loc(b)[1] + hi, row) for b, lo, hi, row in rd]
        wr = [(loc(b)[0], loc(b)[1] + lo, loc(b)[1] + hi, row) for b, lo, hi, row in wr]

        def issue():
            assert bat not in closed
            if after:
                wait(q, (after[1], 2 * half, {}))
            deps(q, rd, wr)
            eng[q].dma_start(out, in_).then_inc(T.sem[bat], 16)
            dcount[bat] = dcount.get(bat, 0) + 16
            note(q, rd, wr, (bat, dcount[bat], dict(seen[q])))
        collect(q, 0.1, START + (0.4 if hi - lo <= 512 else 2.0), rd, wr, issue, bat, after=after[:1] if after else ())

    def rows(q, bat, dst, lo, hi, row, tile, c0, c1):
        b, o = loc(tile)
        db, do = loc(dst)
        dma(q, bat, T[db][row::16, do + lo:do + hi], T[b][:, o + c0:o + c1], [(tile, c0, c1, None)], [(dst, lo, hi, row)])

    def rows2(q, bat, dst, lo, hi, row, th, tl, c0, c1):
        rows(q[0], bat, dst, lo, hi, row, th, c0, c1)
        rows(q[-1], bat, dst, lo, hi, row + 1, tl, c0, c1)

    def load(q, bat, b, lo, hi, src, after=None):
        bb, o = loc(b)
        dma(q, bat, T[bb][:, o + lo:o + hi], src, [], [(b, lo, hi, None)], after)

    def store(q, bat, dst, b, lo, hi):
        bb, o = loc(b)
        dma(q, bat, dst, T[bb][:, o + lo:o + hi], [(b, lo, hi, None)], [])

    def gfill(b, lo, hi):
        iota(A(b, lo, hi), [[0, hi - lo]], 0, 0, True)

    def wrap(bk, o, n, z, src, sl, w=None, first=True, last=True):
        zs = [z, w or z]
        sb, so = loc(src)
        lo = min(sl(r)[0] for r in range(16))
        hi = max(sl(r)[1] for r in range(16))

        def f(e):
            for r in range(16):
                zb, zo = loc(zs[r % 2])
                a, b, st = sl(r)
                rhs = T[sb][:, so + a:so + b] if st == 1 else T[sb][:, so + a:so + b:st]
                i = e.matmul(T[bk][:, o:o + n], T[zb][:, zo + 15 - r:zo + 143 - r], rhs, first and r == 0, last and r == 15)
            return i
        call("P", f, [W(bk, o, n)], [A(src, lo, hi)] + [A(x) for x in sorted(set(zs))], cost=8 * max(64, n))

    def wlist(bk, o, z, src, n, lo=0, first=True, last=True):
        wrap(bk, o, n // 16, z, src, lambda r: (lo + r, lo + n, 16), first=first, last=last)

    def wnat(bk, o, z, src, w, s0=0):
        wrap(bk, o, w, z, src, lambda r: (s0 + w * r, s0 + w * r + w, 1))

    def mm(bk, o, n, z, src, start=True, stop=True, s0=0):
        zb, zo = loc(z)
        sb, so = loc(src)
        call("P", lambda e: e.matmul(T[bk][:, o:o + n], T[zb][:, zo:zo + 128], T[sb][:, so + s0:so + s0 + n], start, stop), [W(bk, o, n)], [A(z, 0, 128), A(src, s0, s0 + n)],
             cost=max(64, n) * (2 if z == "IDF" else 0.5))

    def unmix(src, c0, c1, banks, stop=False):
        zb, zo = loc("ID2")

        def f(e):
            for b in banks:
                for r in range(4 * b, 4 * b + 4):
                    o = 128 * (r % 4)
                    i = e.matmul(T["ps%d" % b][:, o + c0:o + c1], T[zb][:, zo:zo + 128], T[src][:, 16 * c0 + r:16 * c1:16], False, stop and r % 4 == 3)
            return i
        call("P", f, [A("ps%d" % b) for b in banks], [A(src, 16 * c0, 16 * c1), A("ID2")], cost=2 * len(banks) * (c1 - c0))

    nb = [T.cores[(rank - 1) % 4], T.cores[(rank + 1) % 4]]
    lsum = [0]
    sent = {}
    half = len(topo.engines(core, nb[0])) // 2

    def send(src, w, dst, d0, sem):
        tr = []
        for s in range(2):
            e = topo.engines(core, nb[s])
            h = len(e) // 2
            m = sum(1 << x for x in (e[:h], e[h:])[s])
            rid, pid, _ = topo.addr(nb[s])
            lsum[0] += h
            tr.append(RemoteDMATransfer(dst_ids=[DstId(rid=rid, pnc=pid)], dma_engine_mask=m, remote_sem=T.sem[sem],
                                        src=T[src][:, w * s:w * s + w], dst=T[dst][:, d0 + w * (1 - s):d0 + w * (1 - s) + w]))
        rd, lands = [(src, 0, 2 * w, None)], [(dst, d0, d0 + 2 * w, None)]

        def issue():
            deps("G", rd, [])
            g.remote_dma_fused(tr, local_sem=T.sem.sX)
            note("X", [], lands, (sem, 2 * h, dict(seen["G"])))
        sent[sem] = collect("G", 0.6, START + (3.5 if w > 16 else 2.5 if sent else 3.2), rd, [], issue, lands=lands)

    TAB, SNDT = "TAB", "SNDT"
    OH = lambda j: W("OH", j, 1)
    PS = lambda j: W("PS", j, 1)
    LOW = lambda n: A("LOW", 0, n)

    def both(out, o, win, hi, lst, c0, c1, cv):
        if c1 > cv:
            scopy(A(out, o + 16 * (cv - c0), o + 16 * (c1 - c0)), IN(win, 0, hi, lst, cv, c1))
        if cv > c0:
            copy(A(out, o, o + 16 * (cv - c0)), IN(win, 0, hi, lst, c0, cv))

    def weights(z, col, q="V"):
        if q == "V":
            ts(A(z), A("ZA"), col, O.mult)
        else:
            slin(A(z), A("ZA"), col, 0.0)

    load("Y", "d1", "SNI", 0, 32, T.snd[:])
    load("S", "d0", "XP", BM, BM + 128, T.bs[:])
    load("Y", "d2", "XP", RM, RM + 128, T.rt[:])
    load("S", "d2", "XP", LM, LM + 128, T.lt[:])
    iota(A("IP"), [[0, 1]], 1)
    iota(A("LOW"), [[1, 256]], 0, 0, True)
    fill(A(SNDT), -2.0)
    ts(A("II"), A("IP"), 15, O.bitwise_and)
    ts(A("IG"), A("IP"), 112, O.bitwise_and)
    copy(A("qf"), A("II"))
    ts(A("g15"), A("IG"), 15.0, O.add)
    ts(A("OH"), LOW(16), A("qf"), O.is_equal)
    ts(A("ZA"), LOW(143), A("g15"), O.is_equal)
    ts(A("ca"), OH(6), 128.0, O.mult, OH(9), O.add)
    ts(A("cb"), OH(8), float(PL), O.mult)
    ts(A("s1"), OH(8), 16.0, O.mult, OH(7), O.add)
    tt(A("PS"), A("OH", 0, 16, 2), A("OH", 1, 16, 2), O.add)
    ts(A("B16"), LOW(16), A("ca"), O.mult, A("cb"), O.add)
    for r in range(16):
        if r < 10:
            slin(W(TAB, 128 * r, 128), LOW(128), A("s1"), W("B16", r, 1))
        else:
            ts(W(TAB, 128 * r, 128), LOW(128), A("s1"), O.mult, W("B16", r, 1), O.add)
    hilo(A("SH"), A("SL_"), A("SNI"))
    rows2("Y", "d5", SNDT, 16, 528, 4, "SH", "SL_", 0, 32)
    weights("ZB", PS(2))
    hilo(W("HI", 256, 128), W("LO", 256, 128), W("XP", BM, 128))
    rows2("Y", "d4", TAB, 0, V, 4, "HI", "LO", 256, 384)
    load("Y", "d6", "E", 0, V, T["err"][:])
    hilo(W("HI", 0, 256), W("LO", 0, 256), W("XP", LM, 256))

    def consts_0():
        ts(A("IO"), A("IP"), 1, O.bitwise_and)
        ts(A("s2"), A("II"), 10.0, O.is_lt)
        copy(A("odf"), A("IO"))
        ts(A("px"), A("qf"), 128.0, O.mult)
        for o in (LM, RM, BM):
            slin(W("UT", o, 128), LOW(128), 1.0, A("px"))
        slin(A("IL"), LOW(160), 16.0, A("qf"))
        ts(A("ev"), A("odf"), -1.0, O.mult, A("s2"), O.add)
        tt(A("s2"), A("s2"), A("odf"), O.mult)
        ts(A("BN"), LOW(4), 256.0, O.mult, float(V), O.add)
        ts(A("ev"), A("ev"), 0.0, O.max)
        ts(A("BC"), LOW(2), 256.0, O.mult, GH + 4.0, O.add)
        ts(A("BN"), A("BN"), A("ev"), O.mult, A("cb"), O.add)
        ts(A("BC"), A("BC"), OH(8), O.mult)
        for o, c in ((0, float(SL)), (2, BIG)):
            ts(W("wc", 6 + o // 2, 1), OH(14), c, O.mult)
            ts(W("BN", o, 2), W("BN", o, 2), W("wc", 6 + o // 2, 1), O.add)
        copy(A("pc"), A("IP"))
        for b in range(4):
            slin(W(TAB, V + 256 * b, 256), LOW(256), A("s2"), W("BN", b, 1))
        ts(W("wc", 0, 1), PS(2), float(K), O.mult, PS(4), O.add)
        ts(A("IDF"), LOW(128), A("pc"), O.is_equal)

    def slotcol(out, src):
        ts(A(out, 0, 16), A(src[0], src[1], src[1] + 16), float(272 - P), O.add, 528.0, O.min)
        ts(A(out, 16, 32), A(src[0], src[1] + 16, src[1] + 32), float(16 - 256 - P), O.add)

    wlist("ps7", 0, "ZB", SNDT, 512, 16)
    copy(A("SNL"), A("ps7", 0, 32))
    copy(A("ONS"), IN(TAB, 0, V, "SNL", 0, 32))
    rows2("Y", "d7", TAB, 0, V, 0, "HI", "LO", 128, 256)
    rows2("Y", "d7", TAB, 0, V, 2, "HI", "LO", 0, 128)
    wlist("ps6", BB, "ZB", "ONS", 512)
    slotcol("GO0", ("ps6", BB))
    send("GO0", 16, "GI0", 0, "gi0")
    scopy(A("BB00"), IN("E", 0, V, "SNL", 0, 32))
    send("BB00", 256, "D0", GH, "ga00")
    load("Y", "d9", "THI", 0, 1, T["th"][:])
    load("Y", "d9", "WTI", 0, 1, T["wt"][:])
    consts_0()
    for o in (LB, RB, BB):
        scopy(W("UT", o, 32), A("ps7", 0, 32))
    weights("ZL", PS(1), "S")
    weights("ZR", PS(0), "S")
    copy(A("OBS"), IN(TAB, 0, V, "SNL", 0, 32))
    wlist("ps4", LB, "ZL", "OBS", 512)
    wlist("ps4", RB, "ZR", "OBS", 512)
    copy(A("RAW", 0, 64), A("ps4", 0, 64))
    slin(A("NKU"), A("UT", 0, 320), float(-K), 0.0)
    weights("ZV", W("wc", 0, 1), "S")
    mm("ps5", 0, 64, "IDF", "NKU", True, False)
    for s in range(2):
        slin(W("CG", 256 * s, 256), LOW(256), OH(9), W("BC", s, 1))
    gfill("D0", PL + V, DW)
    for k in range(4):
        gfill("D%d" % k, 0, GH)
    for r in range(16):
        copy(A("D0", PL + r, PL + V, 16), W("E", 128 * r, 128))
    copy(A("RAW", LM, BM), A("XP", LM, BM))
    ts(W("RAW", BM, 128), W("XP", BM, 128), float(P - 1), O.min)
    ts(W("RAW", BB, 32), W("ps6", BB, 32), float(P - 1), O.min)
    copy(W("XP", BB, 32), W("ps6", BB, 32))
    copy(A("XP", 0, 64), A("ps4", 0, 64))
    scopy(A("OUTB", 0, V), IN(TAB, 0, P, "RAW", BM, BB))

    def consts_a():
        ts(A("px"), A("qf"), 32.0, O.mult)
        ts(W("wc", 1, 1), PS(1), float(K), O.mult, PS(4), O.add)
        ts(A("U160", 128, 160), LOW(32), A("px"), O.add, float(V), O.add)
        weights("ZW", W("wc", 1, 1), "S")
        scopy(A("U160", 0, 128), W("UT", LM, 128))
        for s in range(2):
            slin(W("ILs", 16 * s, 16), A("IL", 0, 16), 1.0, float(P + 256 * s))

    def consts_b():
        copy(A("wtc"), A("WTI"))
        copy(A("thc"), A("THI"))
        ts(A("bth"), A("THI"), -256.0, O.mult, 256.0, O.add)
        ts(A("th2"), A("THI"), -2.0, O.mult)
        ts(A("px"), A("odf"), -2.0, O.mult, A("pc"), O.add)
        ts(A("mA"), A("IDF"), A("th2"), O.mult)
        ts(A("px"), A("px"), 1.0, O.add)
        ts(A("mB"), LOW(128), A("px"), O.is_equal)
        weights("ZH", A("wtc"), "S")
        tt(A("BTH"), A("mA"), A("mB"), O.add)

    def consts_c():
        ts(A("px"), A("g15"), -15.0, O.add)
        ts(A("mA"), LOW(128), A("g15"), O.is_gt)
        ts(A("mB"), LOW(128), A("pc"), O.is_ge)
        ts(A("BLK"), LOW(128), A("px"), O.is_ge)
        tt(A("TRI"), A("mB"), A("mA"), O.subtract)
        tt(A("BLK"), A("BLK"), A("mA"), O.subtract)
        ts(W("wc", 2, 1), PS(5), float(K), O.mult, PS(4), O.add)
        ts(W("wc", 3, 1), OH(10), -4096.0, O.mult, PS(2), O.add)
        ts(W("wc", 4, 1), OH(1), 4096.0, O.mult, OH(0), O.add)
        ts(A("lowb"), OH(1), 255.0, O.mult, -1.0, O.add)
        tt(W("wc", 5, 1), OH(14), PS(6), O.add)
        for z, col in (("ZN", W("wc", 2, 1)), ("ZC", W("wc", 3, 1)), ("ZX", W("wc", 4, 1)), ("ZO", PS(3)), ("ZF", OH(11)), ("ZG", PS(6)),
                       ("ZT", W("wc", 5, 1)), ("ZQ", A("qf"))):
            weights(z, col, "S")
        for z, c in (("IDN", 1.0), ("ID2", 2.0), ("N4K", -4096.0)):
            slin(A(z), A("IDF"), c, 0.0)
        slin(A("PHU"), A("IL", 0, 128), 1.0, float(PL))
        slin(A("DUMPC"), A("IL", 0, 10), 1.0, JUMP + 255.0)
        ts(A("KH"), A("IL", 0, 32), A("odf"), O.subtract, 0.5, O.mult)
        for t in range(2):
            slin(W("OWL", 32 * t, 32), A("IL", 0, 32), 1.0, float(V + 512 * t))
        slin(A("DUM"), A("IL", 0, 32), 1.0, float(DUMP))

    def given():
        tt(A("sg"), A("UT", BM, 480), A("XP", BM, 480), O.is_lt)
        tt(A("ne", 0, 128), W("XP", RM, 128), W("XP", BM, 128), O.not_equal)
        tt(A("tA", 0, 256), A("XP", LM, BM), A("UT", LM, BM), O.is_equal)
        tt(A("nLR"), W("XP", LM, 128), W("XP", RM, 128), O.not_equal)
        tt(A("nLB"), W("XP", LM, 128), W("XP", BM, 128), O.not_equal)
        tt(A("sA"), A("tA", 0, 128), A("tA", 128, 256), O.mult)
        copy(A("GOf"), A("GO0"))
        slin(A("eRB"), A("ne", 0, 128), -1.0, 1.0)
        slin(A("sgb"), A("sg"), 2.0, -1.0 - BIG)
        slin(A("CT"), A("NKU"), 1.0, float(GH + 2 - P))

    def given_b():
        ts(A("plc"), A("XP", 0, 320), float(P), O.is_lt)
        tt(A("RSq"), W("XP", RB, 32), A("ILs"), O.is_equal)
        tt(A("e2"), W("XP", RB, 32), W("XP", LB, 32), O.subtract)
        tt(A("ne", 128, 160), W("XP", RB, 32), W("XP", BB, 32), O.not_equal)
        tt(A("e2"), A("e2"), A("RSq"), O.mult)
        tt(A("ne", 128, 160), A("ne", 128, 160), A("RSq"), O.subtract)
        tt(A("nLR"), A("nLR"), W("plc", LM, 128), O.mult)
        tt(A("alt"), W("XP", LB, 32), A("e2"), O.add)
        slotcol("SP2", ("alt", 0))
        copy(A("GOd"), A("SP2"))

    def given_s():
        slin(A("nLR"), A("nLR"), BIG, 0.0)
        slin(A("sg"), A("sg"), 2.0, -1.0)
        slin(A("isg"), A("plc"), -1.0, 1.0)
        slin(A("kg"), A("plc"), float(-K), float(K))

    def found_pe(x):
        if x == 0:
            wlist("ps7", 0, "ZB", "OUTB", V)
            mm("ps6", 0, 320, "IDF", "NKU", True, False)
            mm("ps6", BM, 128, "IDF", "NKU", False, False, LM)
            wlist("ps6", BM, "ZW", "OUTB", V, 0, False, False)
        if x == 1:
            wlist("ps4", BM, "ZR", "OUTB", V + 512)
            wlist("ps4", 0, "ZR", "OSS", 1024)
            wlist("ps4", LM, "ZR", "OUTL", V)
            wlist("ps4", RM, "ZR", "OUTR", V)
        if x == 2:
            wlist("ps6", 0, "ZW", "OSS", 1024, 0, False, False)
            wlist("ps6", LM, "ZW", "OUTL", V, 0, False, False)
            wlist("ps6", RM, "ZW", "OUTR", V, 0, False, True)

    def found_0():
        tt(A("mBB"), A("ps7", 0, 128), W("UT", BM, 128), O.is_equal)
        tt(A("cand", 0, 128), A("mBB"), A("sg", 0, 128), O.mult)
        rows("Y", "d10", TAB, 0, V, 10, "cand", 0, 128)

    def found_a():
        tt(A("tB"), A("ps4", 0, 480), A("UT"), O.is_equal)
        ts(A("tA", 0, 448), A("ps6", 0, 448), float(K), O.is_lt)
        slin(A("UR"), A("tB"), BIG, 0.0)
        tt(A("pb"), A("PHU"), A("sA"), O.mult)
        tt(A("ps6", 0, 448), A("ps6", 0, 448), A("tA", 0, 448), O.mult)
        rows("Y", "d11", TAB, 0, V, 11, "UR", RM, RM + 128)

    def found_c():
        tt(W("ps7", 0, 128), W("ps6", BM, 128), A("eRB"), O.mult)
        tt(W("ps7", 0, 128), W("ps7", 0, 128), A("pb"), O.add)
        copy(A("GH_"), W("ps7", 0, 128))
        tt(A("GL_"), W("ps7", 0, 128), A("GH_"), O.subtract)
        rows2("Y", "d11", TAB, 0, V, 12, "GH_", "GL_", 0, 128)

    later = [
        lambda: ts(A("ps7", 128, 448), A("ps5", 0, 320), float(K), O.is_lt),
        lambda: tt(A("tA", 0, 320), A("ps7", 128, 448), A("plc"), O.mult),
        lambda: tt(A("lo"), A("ps5", 0, 320), A("tA", 0, 320), O.mult),
        lambda: ts(A("mLR"), W("ps6", RM, 128), 0.0, O.is_gt, BIG, O.mult),
        lambda: tt(A("ps6", 0, 448), A("ps6", 0, 448), A("UR", 0, 448), O.max),
        lambda: tt(A("UB", 0, 320), A("ps6", 0, 320), A("kg"), O.max),
        lambda: copy(W("UB", BM, 128), W("ps6", BM, 128)),
        lambda: tt(A("pre"), A("UR", BM, 480), A("ne"), O.mult),
        lambda: tt(A("ps6", 0, 320), A("XP", 0, 320), A("CT"), O.add),
        lambda: tt(A("lo2"), W("lo", LM, 128), A("nLB"), O.mult),
        lambda: tt(A("CT"), A("ps6", 0, 320), A("isg"), O.mult),
        lambda: tt(A("pre"), A("pre"), A("sgb"), O.add),
    ]

    def meanwhile(k):
        for f in later[:k]:
            f()
        del later[:k]

    tt(A(TAB, P, G), IN(SNDT, 0, 544, "GI0", 0, 32), A("CG"), O.add)
    both("OSS", 0, TAB, G, "RAW", 0, 64, 32)
    wlist("ps5", 0, "ZV", "OSS", 1024, 0, False, True)
    scopy(A("OUTR", 0, V), IN(TAB, 0, G, "RAW", RM, BM))
    ts(A("GL", 0, 64), A("ps5", 0, 64), float(K), O.min)

    DB = ["D0", "D1", "D2", "D3", "D4"]

    def border(t, k, first="S"):
        out = "BB%d%d" % (t, k + 1)
        for s in range(2):
            (scopy if first == "S" else copy)(W("AQ", 256 * s, 256), IN(DB[k], 0, DW, "GL", RB + 16 * s, RB + 16 * s + 16))
        for s in range(2):
            tt(W(out, 256 * s, 256), IN(DB[k], 0, DW, "GL", LB + 16 * s, LB + 16 * s + 16), W("AQ", 256 * s, 256), O.max)
        send(out, 256, DB[k + 1], GH, "ga%d%d" % (t, k + 1))

    def inner(t, k, at=None):
        cuts = (0, 32, 64, 96, 128) if k in (1, 2) else (0, 8, 32, 64, 96, 128)
        o = PL if k < 3 else 0
        m = (16, 0, 0, 32)[k]
        for c0, c1 in zip(cuts, cuts[1:]):
            scopy(A("AB", 16 * c0, 16 * c1), IN(DB[k], 0, DW, "GL", RM + c0, RM + c1))
        if t and m < 32:
            scopy(A(DB[k + 1], o + V + 16 * m, o + V + 512), IN(DB[k], 0, DW, "GL", LN + m, LN + 32))
        if t and m:
            copy(W(DB[k + 1], o + V, 16 * m), IN(DB[k], 0, DW, "GL", LN, LN + m))
        for c0, c1 in zip(cuts, cuts[1:]):
            tt(A(DB[k + 1], o + 16 * c0, o + 16 * c1), IN(DB[k], 0, DW, "GL", LM + c0, LM + c1), A("AB", 16 * c0, 16 * c1), O.max)
            if at and c1 == 64:
                at()

    def flags(t, k, q):
        b = "FL" if k % 2 else "FS"
        for lo, hi in ((0, 1024), (1024, V), (V, V + 512))[:2 + t]:
            if q == "V":
                ts(A(b, lo, hi), A(DB[k], PL + lo, PL + hi), A("thc"), O.is_ge, 256.0, O.mult)
            else:
                slin(A(b, lo, hi), A(DB[k], PL + lo, PL + hi), 256.0, A("bth"), F.Relu)
            if lo < V:
                unmix(b, lo // 16, hi // 16, range(4))
            else:
                mm("ps4", 0, 512, "ID2", b, False, False, V)

    def opensums(t):
        for c in range(4 + t):
            mm("ps%d" % c, 0, 512, "BTH", "ONE", True, False)

    CNT = ("ps4", "ps5")

    def partners(t, part=7):
        n = V + 512 * t
        nc = n // 16
        if part & 1:
            wlist("ps7", 0, "ZC", TAB, n)
        if part & 4:
            ts(A("BL", 0, nc), A("ps7", 0, nc), 4096.0, O.add, float(n - 1), O.min)
            ts(A("nm", 0, nc), A("ps7", 0, nc), 0.0, O.is_ge)
        if part & 2:
            mm(CNT[t], 0, nc, "N4K", "nm", True, False)

    def select(t, rest=None):
        n = V + 512 * t
        nc = n // 16
        hh = VPART[t]
        inner(t, 3, lambda: unmix("D4", 0, 64, range(4)))
        if t:
            mm("ps4", 0, 512, "ID2", "D4", False, True, V)
            scopy(W("H", V, 512), A("ps4"), F.Sign)
        for b in range(4):
            unmix("D4", 64, 128, [b], True)
        for b in range(4):
            if b % 2:
                ts(W("H", 512 * b, 512), A("ps%d" % b), 1.0, O.min, -1.0, O.max)
            else:
                scopy(W("H", 512 * b, 512), A("ps%d" % b), F.Sign)
        parts = [(lo, min(lo + 512, n)) for lo in range(hh, n, 512)]
        for lo, hi in parts:
            scopy(A("AB", lo, hi), IN("H", 0, n, "BL", lo // 16, hi // 16))
        for lo, hi in ((0, 1024), (1024, hh)):
            copy(A("M", lo, hi), A("H", lo, hi))
        for lo, hi in ((0, 1024), (1024, hh)):
            tt(A("M", lo, hi), IN("H", 0, n, "BL", lo // 16, hi // 16), A("M", lo, hi), O.max)
        for i, (lo, hi) in enumerate(parts):
            mm("ps%d" % i, 0, hi - lo, "ID2", "H", True, False, lo)
            mm("ps%d" % i, 0, hi - lo, "ID2", "AB", False, True, lo)
            slin(A("M", lo, hi), A("ps%d" % i, 0, hi - lo), 1.0, A("one"), F.Sign)
        wlist(CNT[t], 0, "ZA", "M", 1024, 0, False, False)
        wlist(CNT[t], 64, "ZA", "M", n - 1024, 1024, False, True)
        if rest:
            rest()
        ts(A("go", 0, nc), A(CNT[t], 0, nc), 2.0, O.is_ge)
        mm("ps2", 0, nc, "BLK", "go")
        mm("ps3", 0, nc, "TRI", "go")
        ts(A("z0", 0, nc), A("ps2", 0, nc), 0.0, O.is_equal, 256.0, O.mult)
        scan(A("sc", 1, nc + 1), A("ones", 0, nc), A("ps2", 0, nc), -1.0, O.mult, O.add)
        wlist("ps0", 0, "ZA", "z0", nc, 0, True, False)
        tt(A("ps3", 0, nc), A("ps3", 0, nc), A("go", 0, nc), O.mult)
        ts(A("a0", 0, nc), A("sc", 0, nc), 255.0, O.min, A("lowb"), O.max)
        wlist("ps0", 0, "ZX", "a0", nc, 0, False, True)
        tt(A("val", 0, nc), A("ps3", 0, nc), A("sc", 0, nc), O.add)
        ts(A("ye_", 0, 16), A("IL", 0, 16), W("sc", nc, 1), O.is_gt, -1.0, O.mult)
        ts(A("yo"), A("KH"), W("sc", nc, 1), O.is_gt)
        mm("ps2", 256, 16, "N4K", "ye_", True, False)
        tt(A("yo"), A("yo"), W("OWL", 32 * t, 32), O.mult)
        mm("ps1", 0, 32, "IDF", "yo", True, False)
        k = nc // 16
        tt(A("of", 0, k), A("ps0", 0, k), A("DUMPC", 0, k), O.min)
        ts(A("OFF", 0, k), A("of", 0, k), 1.0 - JUMP, O.add)
        cw, vw = "CW%d" % t, "VW%d" % t
        copy(IN(cw, 0, 416, "OFF", 0, k), LOW(nc))
        copy(IN(vw, 0, 416, "OFF", 0, k), A("val", 0, nc))
        scan(A("CF"), A(cw, 0, 256), A(cw, 0, 256), 0.0, O.max, O.max)
        scan(A("ps3", 0, 256), A(vw, 0, 256), A(vw, 0, 256), -1.0, O.max, O.max)
        wlist("ps2", 256, "ZA", "CF", 256, 0, False, False)
        tt(A("MM"), A("ps3", 0, 256), LOW(256), O.is_equal)
        wlist("ps2", 256, "ZQ", "MM", 256, 0, False, True)
        ts(A("T0"), A("ps2", 256, 272), float(G), O.min)
        copy(A("G0"), IN(TAB, 0, G + 16, "T0", 0, 16))
        wrap("ps1", 0, 32, "ZO", "G0", lambda r: (r >> 1, 256, 8), "ZB", False, True)
        copy(A("TD"), A("ps1", 0, 32))
        copy(A("TF"), A("ps1", 0, 32))
        for x, win in (("ET", "E"), ("GT", TAB)):
            scopy(A(x), IN(win, 0, P, "TD", 0, 32))
        copy(IN("OS%d" % t, 0, P, "TD", 0, 32), W(TAB, n, 512))

    def err0(t):
        tt(A("hx", 0, 32), A("ps4", 0, 32), A("TF"), O.add)
        tt(A("hx", 32, 64), A("ps4", 0, 32), W("OWL", 32 * t, 32), O.add)
        ts(A("hy"), A("hx"), 2047, O.bitwise_and)
        copy(A("HX"), A("hy"))

    def halves():
        ts(A("E1"), A("ET"), 0.5, O.mult, 127.8, O.add)
        ts(A("E2"), A("E1"), -256.0, O.add)

    def details(x):
        slin(W("DG", 512 * x, 512), IN("DR", 0, V, "HX", 32 * x, 32 * x + 32), 0.5, 127.8)

    def err1(bk, out):
        mm(bk, 0, 512, "IDN", "E2", True, False)
        mm(bk, 0, 512, "IDN", "DG", False, True, 512)
        scopy(out, A(bk), F.Relu)

    def levels(t, extra):
        for k in range(3):
            if k:
                border(t, k)
            extra(k)
            inner(t, k)
            for j, q in ((), ((0, "S"), (1, "S")), ((2, "S"), (3, "V")))[k]:
                flags(t, j, q)
        extra(3)

    border(0, 0, "V")
    for k in (1, 2, 3):
        gfill("D%d" % k, PL + V, DW)
    mm("ps5", LM, 256, "IDF", "NKU", True, False, LM)
    def sides(win, z):
        for c in range(0, 96, 16):
            copy(W("OUTL", 16 * c, 256), IN(win, 0, G, "RAW", LM + c, LM + c + 16))
        scopy(A("OUTL", 1536, V), IN(win, 0, G, "RAW", LM + 96, RM))
        wlist("ps5", RM, z, "OUTR", V, 0, False, False)
        wlist("ps5", LM, z, "OUTL", 1024, 0, False, False)
        wlist("ps5", LM + 64, z, "OUTL", 1024, 1024, False, True)
    sides(TAB, "ZV")
    ts(A("GL", LM, BM), A("ps5", LM, BM), float(K), O.min)

    def fills(t):
        for b, c in (("CW%d" % t, 0), ("VW%d" % t, -1)):
            iota(A(b), [[0, WIDTH[b]]], 0, c, True)
        for c in range(0, P, 1024):
            gfill("OS%d" % t, c, c + 1024)

    def extra0(k):
        if k == 1:
            scopy(A("OUTB", V, V + 512), IN(TAB, 0, P, "RAW", BB, BB + 32))
            weights("ZP", PS(4), "S")
            wlist("ps7", 0, "ZP", "ONS", 512)
            copy(A("PHS"), A("ps7", 0, 32))
            consts_a()
            iota(A("ONE"), [[0, 512]], 0, 1, True)
            consts_c()
            consts_b()
            given()
            found_pe(0)
            found_0()
            found_pe(1)
            opensums(0)
            found_pe(2)
            partners(0, 1)
        if k == 2:
            found_a()
            partners(0, 6)
            found_c()
        if k == 3:
            iota(A("SND2"), [[0, 544]], 0, -1, True)
            rows2("Y", "d24", "SND2", 16, 528, 10, "SH", "SL_", 0, 32)
            for b in ("ones", "one"):
                iota(A(b), [[0, WIDTH[b]]], 0, 1, True)
            iota(A("sc", 0, 1), [[0, 1]], 0, -1, True)
            gfill(TAB, G, G + 16)
            iota(A("E", V, P), [[0, P - V]], 0, -256, True)
            fills(0)
    levels(0, extra0)
    load("Y", "d15", "DR", 0, 2048, T["det"][:], (sent["ga03"], "ga03"))
    select(0)
    aside(given_b, given_s, lambda: meanwhile(99))

    OS = "OS0"
    wlist("ps4", 0, "ZH", "ET", 512)
    scopy(A("ONS"), IN(OS, 0, P, "SNL", 0, 32))
    wlist("ps2", 0, "ZP", "ONS", 512)
    wlist("ps1", 0, "ZP", "GT", 512)
    err0(0)
    details(0)
    details(1)
    halves()
    ts(A("TP"), A("ps1", 0, 32), float(-PL), O.add)
    tt(A("sp"), A("ps2", 0, 32), A("GOd"), O.min)
    tt(A("s3"), A("GOf"), A("ps2", 0, 32), O.subtract)
    tt(A("sq"), A("ps2", 0, 32), A("RSq"), O.mult)
    tt(A("sp"), A("sp"), A("s3"), O.max)
    tt(A("sq"), A("sq"), A("PHS"), O.max)
    copy(A("GO1"), A("sp"))
    send("GO1", 16, "GI1", 0, "gi1")
    tt(IN("D0", PL, PL + V + 512, "TP", 0, 32), A("DG", 0, 512), A("E2"), O.add)
    ts(A("SP2"), A("sq"), float(-PL), O.add)
    err1("ps4", W("D0", PL + V, 512))
    scopy(A("BB10"), IN("D0", PL, PL + V + 512, "SP2", 0, 32))
    send("BB10", 256, "D0", GH, "ga10")
    wlist("ps1", 32, "ZR", "GT", 512)
    wnat("ps0", 0, "ZP", OS, 128)
    for i, j in ((0, 6), (1, 7), (12, 6), (13, 7)):
        dma("Y", "d21", T[TAB][i::16, V:V + 512], T["GT"][j::16, 0:512], [("GT", 0, 512, j)], [(TAB, V, V + 512, i)])
    mm("ps7", 0, 64, "IDF", "CT", True, False)
    wlist("ps3", 0, "ZG", "GT", 512)
    mm("ps5", LM, 256, "IDF", "CT", True, False, LM)
    CAP, CPS = W("ps6", 384, 128), W("ps6", 256, 128)
    def newtiles():
        ts(A("TR"), A("ps1", 32, 64), float(P - 1), O.min)
        scopy(A("ONT"), IN(OS, 0, P, "TR", 0, 32))
        for a, z in enumerate(("ZB", "ZO", "ZR", "ZF")):
            wnat("ps1", 32 * a, z, "GT", 32)
        wnat("ps1", 160, "ZO", "ONT", 32)
        for r in range(16):
            copy(W("E", 128 * r, 128), A("D0", PL + r, PL + V, 16))
        copy(W("E", V, 512), W("D0", PL + V, 512))
    for o in (LB, RB):
        ts(W("tA", o, 32), A("ps2", 0, 32), 0.0, O.is_equal, BIG, O.mult)
    tt(A("e2"), A("ps2", 0, 32), A("pre", 128, 160), O.add)
    tt(A("UB2", 0, 64), A("UB", 0, 64), A("tA", 0, 64), O.min)
    tt(A("LO2", 0, 64), A("lo", 0, 64), A("tA", 0, 64), O.min)
    ts(CAP, A("ps0", 0, 128), 0.0, O.is_equal, BIG, O.mult)
    tt(W("LO2", RB, 32), W("LO2", RB, 32), A("e2"), O.max)
    tt(A("pa"), A("ps0", 0, 128), A("pre", 0, 128), O.add)
    ts(A("vn", 0, 128), A("ps0", 0, 128), float(-PL), O.add)
    for o in (LM, RM):
        tt(W("UB2", o, 128), CAP, W("UB", o, 128), O.min)
        tt(W("LO2", o, 128), CAP, W("lo", o, 128), O.min)
    copy(W("GL", LN, 32), A("ps3", 0, 32))
    tt(W("LO2", RM, 128), W("LO2", RM, 128), A("pa"), O.max)
    both(OS, P, "SND2", 544, "GI1", 0, 32, 16)
    both("OSS", 0, OS, G, "RAW", 0, 64, 32)
    wlist("ps7", 0, "ZN", "OSS", 1024, 0, False, True)
    scopy(A("OUTR", 0, V), IN(OS, 0, G, "RAW", RM, BM))

    def newlists(bk, lo, hi):
        tt(A(bk, lo, hi), A(bk, lo, hi), A("UB2", lo, hi), O.min)
        tt(A(bk, lo, hi), A(bk, lo, hi), A("LO2", lo, hi), O.max)
        copy(A("GL", lo, hi), A(bk, lo, hi))

    X2 = lambda a, o=0, n=128: W("X2", 160 * a + o, n)
    N3 = lambda a: W("N3", 128 * a, 128)
    T1, T2 = W("ps6", 0, 128), W("ps6", 128, 128)

    def renamed():
        ts(A("tA", 0, 128), A("ps6", 128, 256), 0.0, O.is_le, BIG, O.mult)
        tt(A("pa"), A("ps6", 256, 384), W("UB", BM, 128), O.min)
        tt(A("pb"), A("ps6", 0, 128), W("UB", LM, 128), O.min)
        tt(A("ps6", 0, 384), A("ps6", 0, 384), A("UR", LM, BB), O.min)
        tt(A("pa"), A("pa"), A("mBB"), O.max)
        tt(A("N3"), A("ps6", 0, 384), A("XP", LM, BB), O.max)
        tt(A("pa"), CAP, A("pa"), O.min)
        ts(CPS, A("vn", 0, 128), 0.0, O.is_gt, BIG, O.mult)
        tt(T1, CAP, N3(2), O.min)
        tt(T2, A("pb"), A("lo2"), O.max)
        tt(A("tB", 0, 128), CPS, N3(0), O.min)
        tt(A("pb"), T2, A("nLR"), O.min)
        tt(X2(2), T1, A("tB", 0, 128), O.max)
        tt(T2, CPS, A("pb"), O.min)
        copy(W("HI", 256, 128), X2(2))
        tt(A("SG2", 0, 128), A("U160", 0, 128), X2(2), O.is_lt)
        tt(T2, T2, A("pa"), O.max)
        tt(W("LO", 256, 128), X2(2), W("HI", 256, 128), O.subtract)
        tt(A("cand", 0, 128), T2, A("SG2", 0, 128), O.min)
        rows2("Y", "d20", TAB, 0, V, 4, "HI", "LO", 256, 384)
        rows("Y", "d20", TAB, 0, V, 10, "cand", 0, 128)

    def renamed2():
        tt(A("vs", 0, 128), A("vn", 0, 128), A("sg", 0, 128), O.add)
        tt(T2, CAP, N3(1), O.min)
        tt(A("tA", 0, 128), CAP, A("tA", 0, 128), O.min)
        tt(T2, T2, A("vs", 0, 128), O.max)
        copy(W("HI", 128, 128), T2)
        copy(X2(1), T2)
        tt(W("LO", 128, 128), T2, W("HI", 128, 128), O.subtract)
        rows2("Y", "d22", TAB, 0, V, 0, "HI", "LO", 128, 256)

    def target():
        tt(T1, A("tA", 0, 128), A("mLR"), O.min)
        tt(A("pa"), A("tA", 0, 128), W("UR", RM, 128), O.min)
        ts(A("pd"), W("GL", RM, 128), float(PL), O.is_lt, BIG, O.mult)
        copy(A("pb"), CPS)
        slin(A("pa"), A("pa"), -1.0, BIG)
        slin(A("pd"), A("pd"), 1.0, float(SB))
        tt(A("pb"), T1, A("pb"), O.max)
        tt(T1, A("pa"), A("pd"), O.min)
        slin(A("pb"), A("pb"), -1.0, BIG + SL)
        tt(A("pb"), T1, A("pb"), O.min)
        tt(T2, T2, A("pb"), O.add)
        copy(A("GH_"), T2)
        tt(A("GL_"), T2, A("GH_"), O.subtract)
        rows2("Y", "d25", TAB, 0, V, 12, "GH_", "GL_", 0, 128)

    def fresh():
        n1 = lambda a: W("ps1", 32 * a, 32)
        copy(A("e2"), n1(3))
        scopy(X2(0, 128, 32), n1(0))
        scopy(X2(1, 128, 32), n1(1))
        tt(A("sq"), n1(5), A("e2"), O.min)
        tt(X2(2, 128, 32), n1(2), A("sq"), O.max)
        tt(A("SG2", 128, 160), A("U160", 128, 160), X2(2, 128, 32), O.is_lt)
        ts(A("sq"), A("sq"), 0.0, O.max)
        hilo(A("SH"), A("SL_"), X2(2, 128, 32))
        tt(A("cand", 128, 160), A("sq"), A("SG2", 128, 160), O.min)
        rows2("Y", "d23", TAB, V, V + 512, 4, "SH", "SL_", 0, 32)
        rows("Y", "d23", TAB, V, V + 512, 10, "cand", 128, 160)

    newlists("ps7", 0, 64)
    border(1, 0, "V")
    sides(OS, "ZN")
    newlists("ps5", LM, BM)

    def others():
        for c in range(0, 128, 32):
            scopy(W("OUTB", 16 * c, 512), IN(OS, 0, P, "RAW", BM + c, BM + c + 32))
        newtiles()
        for a, x in enumerate(("OUTL", "OUTR", "OUTB")):
            wlist("ps6", 128 * a, "ZO", x, V)
        fresh()
        opensums(1)

    XA = lambda a: X2(a, 0, 160)
    EQ = lambda a: W("EQ", 160 * a, 160)

    def alike():
        tt(T1, CAP, N3(0), O.min)
        tt(X2(0), T1, A("vn", 0, 128), O.max)
        for a, (x, y) in enumerate(((1, 0), (1, 2), (0, 2))):
            tt(EQ(a), XA(x), XA(y), O.is_equal)
        slin(A("SG2"), A("SG2"), 2.0, -1.0)

    def extra1(k):
        if k == 1:
            others()
        if k == 2:
            renamed()
            partners(1, 1)
        if k == 3:
            renamed2()
            aside(lambda: partners(1, 6), target, alike)
            fills(1)
            for c in range(0, DUMP + 512, 1088):
                gfill("RN", c, c + 1088)
    levels(1, extra1)
    select(1)

    n = V + 512

    def tile(bk, x, o):
        wnat(bk, 0, "ZO", x, 128, o)
        wnat(bk, 128, "ZO", x, 32, o + V)

    def out(a, q):
        y = ("yl", "yr", "yb")[a]
        store(q, "d31", T[y][:, 0:V], "PO", 160 * a, 160 * a + 128)
        store("S", "d31", T[y][:, V:n], "PO", 160 * a + 128, 160 * a + 160)

    def row(bk, r, z, src, start, stop):
        zb, zo = loc(z)
        call("P", lambda e: e.matmul(T[bk][:, 0:512], T[zb][:, zo + 15 - r:zo + 143 - r], T[src][:, 0:512], start, stop), [A(bk)], [A(z), A(src)], cost=256)
    wlist("ps4", 0, "ZH", "ET", 512)
    wlist("ps1", 0, "ZT", "GT", 512)
    err0(1)
    tt(A("e3"), A("ps1", 0, 32), A("DUM"), O.min)
    copy(A("TR"), A("e3"))
    details(0)
    details(1)
    halves()
    copy(IN("RN", 0, DUMP + 512, "TR", 0, 32), W(TAB, n, 512))
    tt(IN("E", 0, P, "TD", 0, 32), A("DG", 0, 512), A("E2"), O.add)
    store("Y", "d30", T["ye"][:, 0:n], "E", 0, n)
    tile("ps0", "OS1", 0)
    for a, z in enumerate(("ZB", "ZO", "ZR")):
        row("ps2", a, z, "GT", a == 0, a == 2)
    scopy(A("ONT"), IN("RN", 0, P, "TD", 0, 32))
    tile("ps6", "RN", 0)
    err1("ps4", A("CR"))
    store("Y", "d30", T["ye"][:, n:P], "CR", 0, 512)
    scopy(A("NW"), A("ps2"))
    tile("ps5", "RN", SL)
    row("ps1", 2, "ZO", "ONT", True, True)
    tile("ps7", "RN", SB)
    CAP, CPS, T1 = W("ps3", 0, 160), W("ps3", 160, 160), W("ps3", 320, 160)
    z0, z5, z6, z7 = [A("ps%d" % b, 0, 160) for b in (0, 5, 6, 7)]
    ts(A("v2"), z0, 0.0, O.is_equal, BIG, O.mult)
    ts(CPS, z0, 0.0, O.is_gt, BIG, O.mult)
    tt(A("vs"), z0, A("SG2"), O.add)
    ts(CAP, z0, 0.0, O.is_equal, BIG, O.mult)
    tt(A("vs"), CPS, A("vs"), O.min)
    tt(T1, CAP, XA(1), O.min)
    tt(XA(2), CAP, XA(2), O.min)
    tt(XA(1), T1, A("vs"), O.max)
    tt(EQ(0), z6, EQ(0), O.mult)
    tt(EQ(1), z6, EQ(1), O.mult)
    tt(z6, z6, A("v2"), O.min)
    tt(T1, EQ(0), XA(0), O.max)
    tt(W("PO", 160, 160), z6, XA(1), O.max)
    out(1, "Y")
    copy(A("vn"), T1)
    tt(A("NW"), A("ps1"), A("NW"), O.max)
    for a, y in enumerate(("yl", "yr", "yb")):
        dma("S", "d32", T[y][:, n:P], T["NW"][a::16, 0:512], [("NW", 0, 512, None)], [])
    tt(EQ(2), z5, EQ(2), O.mult)
    tt(A("vn"), z5, A("vn"), O.max)
    tt(T1, EQ(1), EQ(2), O.max)
    tt(A("vs"), CAP, A("vn"), O.min)
    tt(A("v3"), CPS, A("vn"), O.min)
    tt(T1, T1, A("v2"), O.min)
    tt(W("PO", 0, 160), z0, A("vs"), O.max)
    out(0, "Y")
    tt(T1, T1, XA(2), O.max)
    tt(z7, z7, A("v2"), O.min)
    tt(A("v3"), T1, A("v3"), O.max)
    tt(W("PO", 320, 160), z7, A("v3"), O.max)
    out(2, "Y")
    issue_all()
    for d in sorted(dcount):
        wait("Y", (d, dcount[d], {}))
    for q in ("V", "S", "P", "G"):
        wait("Y", ("s" + q, count[q], {}))
    g.wait_ge(T.sem.sX, lsum[0])
